import numpy as np, ml_dtypes
CORES = [51,54,179,182]
N = 4
BF = ml_dtypes.bfloat16
W, B, RO, NEED = 4096, 192, 5, 9
def spot(o, u, t):
    return (((o * (2 * u + 1)) >> 5) + o + 77 * t) & (W - 1)
def base(rng):
    amp = rng.integers(32, 256, (N, 8, 1, W))
    return {"hue": (rng.random((N, 8, 16, W)) * (amp + 1)).astype(np.int64), "own": rng.integers(0, W, (N, 8, 16, B)), "nb": rng.integers(0, B, (N, 8, 16, B)),
            "tau": rng.integers(0, B, (N, 8, B)), "prev": rng.integers(0, B, (N, 8, B)), "foe": rng.integers(0, B, (N, 8, B)),
            "tas": rng.integers(0, 1024, (N, 8, B)), "wt": rng.integers(0, 256, (N, 8, 16, 1))}
def pack(d):
    out = {"hue": np.ascontiguousarray(d["hue"].reshape(N, 128, W)).astype(np.float32).astype(BF)}
    for k in ("own", "nb"): out[k] = np.ascontiguousarray(d[k].reshape(N, 128, B)).astype(np.int32)
    for k in ("tau", "prev", "foe", "tas"): out[k] = np.ascontiguousarray(d[k]).astype(np.int32)
    out["wt"] = np.ascontiguousarray(d["wt"].reshape(N, 128, 1)).astype(np.int32)
    return out
def setup_inputs(rng):
    return pack(base(rng))
def setup_inputs_ties(rng):
    d = base(rng)
    e = rng.choice(np.array([3.0, 6.0, 12.0]), (N, 8, 1, W)); m = rng.choice(np.array([1, 17, 85]), (N, 8, 1, 1)); m[0, 0] = 85; m[0, 1] = 1
    d["hue"] = np.minimum((4 * rng.random((N, 8, 16, W)) ** e).astype(np.int64), 3) * m
    pool = rng.integers(0, W, (N, 8, 24)); some = np.take_along_axis(pool, rng.integers(0, 24, (N, 8, 16 * B)), 2).reshape(N, 8, 16, B)
    d["own"][:, 1::2] = some[:, 1::2]; d["tas"][:, 1::2] = rng.choice(np.array([5, 512, 1000]), (N, 4, B))
    for a in (2, 5):
        d["own"][:, a, :, 1::2] = d["own"][:, a, :, 0::2]; d["tas"][:, a, 1::2] = d["tas"][:, a, 0::2]
    pool = rng.integers(0, B, (N, 8, 20)); few = np.take_along_axis(pool, rng.integers(0, 20, (N, 8, B)), 2)
    d["tau"][:, 3:] = few[:, 3:]
    return pack(d)
def setup_inputs_corners(rng):
    d = base(rng); b = np.arange(B)
    pats = np.stack([0 * b, 0 * b + B - 1, b, B - 1 - b, (b + 1) % B, (B - 1) * (b & 1), b >> 1, np.minimum(b + 1, B - 1)])
    ia = np.arange(8)[None, :] + np.arange(N)[:, None] + rng.integers(0, 8)
    d["tau"] = pats[ia & 7]; d["prev"] = pats[(ia + 3) & 7]; d["foe"] = pats[(ia + 5) & 7]; d["nb"] = pats[(ia[:, :, None] + np.arange(16)) & 7]
    d["tau"][0] = np.argsort(rng.random((8, B)), axis=1)
    d["tau"][0, :4] = np.stack([b, B - 1 - b, (b + 1) % B, (b + B - 1) % B])
    d["tau"][0, 6, 0] = d["tau"][0, 6, 1]
    d["hue"][0] = 128 + (d["hue"][0] >> 1); d["hue"][1] = d["hue"][1] & 1
    d["hue"][2] = 255; d["hue"][3, 7] = 255; d["tau"][2] = np.argsort(rng.random((8, B)), axis=1)
    kind = rng.integers(0, 5, (N, 8, 1, B)); one = d["own"][:, :, :1, :]; two = (W - 1) * rng.integers(0, 2, (N, 8, 16, B))
    o = d["own"]; o = np.where(kind == 0, 0, np.where(kind == 1, W - 1, np.where(kind == 2, one, np.where(kind == 3, two, o)))); d["own"] = o
    d["tas"] = np.where(rng.random((N, 8, B)) < 0.5, rng.choice(np.array([0, 1, 511, 512, 1023]), (N, 8, B)), d["tas"])
    d["wt"][:, 0] = 0; d["wt"][:, 7] = 255
    return pack(d)
def setup_inputs_close(rng):
    d = base(rng); b = np.arange(B); p = rng.permutation(N); s, m = int(p[0]), int(p[1]); o, u = d["own"], d["tas"]
    hn = (NEED - 1) // 2; nn = max(NEED, 17 - NEED); ca = int(spot(W - 1, 0, 0)); last = int(spot(W - 1, 1023, RO - 1))
    x = np.minimum(d["hue"], 253)
    x[:, 2:4, :, ca] = 254
    for a, lo in ((2, B - 1), (3, B // 2)):
        c = spot(o[:, a], u[:, a, None, :], 0); o[:, a] = np.where(c == ca, 0, o[:, a])
        o[:, a, 3, lo:] = W - 1; u[:, a, lo:] = 0
        d["tau"][:, a] = rng.integers(lo, B, (N, 1))
    x[:, 4, NEED - 1:] = 7; d["tau"][:, 4] = b; d["prev"][:, 4] = B - 1 - b
    for a, lo in ((5, 129), (6, 250)):
        x[:, a] = 0
        x[:, a, :hn] = lo + rng.integers(0, 4, (N, hn, W)); x[:, a, 8:8 + hn] = lo + rng.integers(0, 4, (N, hn, W))
        x[m, a] = rng.integers(0, 2, (16, W))
    x[:, 7, nn:, last] = 255; x[:, 7, nn:, W - 1] = 0
    o[:, 7] = np.where(np.argsort(rng.random((N, 16, B)), axis=1) < 10, W - 1, o[:, 7])
    x[s] = rng.integers(0, 16, (8, 16, W)); x[s, :, :nn] = 255
    u[s, 7] = 1023; d["wt"][s, 7] = 0; d["wt"][s, 7, 0, 0] = 255; d["wt"][s, 7, 1, 0] = 2
    d["hue"] = x
    return pack(d)
def setup_inputs_spread(rng):
    d = base(rng); lw = int(W).bit_length() - 1
    d["hue"] = np.minimum((np.exp2(8 * rng.random((N, 8, 1, W))) * rng.random((N, 8, 16, W))).astype(np.int64), 255)
    n = np.minimum(np.exp2(lw * rng.random((N, 8, 16, B))).astype(np.int64) - 1, W - 1)
    d["own"] = np.where(rng.random((N, 8, 16, B)) < 0.5, W - 1 - n, n)
    for k in ("tau", "prev", "foe"): d[k] = np.minimum((B * rng.random((N, 8, B)) ** rng.choice(np.array([1.0, 2.0, 4.0]), (N, 8, 1))).astype(np.int64), B - 1)
    d["nb"] = np.minimum((B * rng.random((N, 8, 16, B)) ** 2).astype(np.int64), B - 1)
    d["tas"] = np.minimum((1024 * rng.random((N, 8, B)) ** 3).astype(np.int64), 1023)
    d["wt"] = np.minimum(np.exp2(8 * rng.random((N, 8, 16, 1))).astype(np.int64), 255)
    return pack(d)
def setup_inputs_ends(rng):
    d = base(rng)
    def pick(hi, *s): return hi * rng.integers(0, 2, s)
    d["hue"] = pick(255, N, 8, 16, W); o = pick(W - 1, N, 8, 16, B); kind = rng.integers(0, 4, (N, 8, 1, B))
    o = np.where(kind == 0, 0, np.where(kind == 1, W - 1, o)); u = pick(1023, N, 8, B); ta = pick(B - 1, N, 8, B)
    for k in ("prev", "foe"): d[k] = pick(B - 1, N, 8, B)
    d["foe"] = np.where(rng.random((N, 8, B)) < 0.3, rng.integers(0, B, (N, 8, B)), d["foe"])
    d["nb"] = pick(B - 1, N, 8, 16, B); w = pick(255, N, 8, 16, 1); w[:, 7] = 255; w[:, 3] = 0
    ca, cb, cc, cd = spot(W - 1, 0, 0), spot(W - 1, 1023, 0), spot(W - 2, 1023, 0), spot(W - 2, 0, 0)
    cnt = np.array([NEED - 1, NEED, NEED - 1, NEED - 1, NEED, NEED - 1, NEED - 1, NEED - 1])
    d["hue"][..., 0] = 0; d["hue"][..., cd] = 0; d["hue"][..., cb] = 255; d["hue"][..., cc] = 255; d["hue"][:, :, 5, cc] = 254
    d["hue"][..., ca] = np.where(np.argsort(rng.random((N, 8, 16)), axis=2) < cnt[None, :, None], 255, 0)
    for v, p in ((0, (2, 14)), (B - 1, (3, 15))):
        o[..., v] = 0; o[:, :, 1, v] = W - 2; o[:, :, p[0], v] = W - 1; o[:, :, p[1], v] = W - 1; u[..., v] = 0
    ta[..., 0] = 0; ta[..., 1] = B - 1; o[..., 1] = 0; u[..., 1] = 1023
    o[..., B - 2] = W - 1; u[..., B - 2] = 1023
    ta[N - 1, 7] = 0; ta[N - 1, 7, B - 1] = B - 1; o[N - 1, 7, :, B - 1] = 0; u[N - 1, 7, B - 1] = 1023
    d["own"], d["tas"], d["tau"], d["wt"] = o, u, ta, w
    return pack(d)
def check_inputs(d):
    bad = []
    for k, hi in (("hue", 255), ("own", W - 1), ("nb", B - 1), ("tau", B - 1), ("prev", B - 1), ("foe", B - 1), ("tas", 1023), ("wt", 255)):
        v = np.asarray(d[k]).astype(np.float64)
        if not (np.min(v) >= 0 and np.max(v) <= hi): bad.append("range of " + k)
        elif np.any(v != np.floor(v)): bad.append("whole numbers of " + k)
    return bad
def look(x, names, u, t):
    c = spot(names, u[:, None, :], t).reshape(8, 1, 16 * B)
    return np.take_along_axis(x, c, 2).reshape(8, 16, 16, B)
def reference(hue, own, nb, tau, prev, foe, tas, wt):
    x = hue.astype(np.float32).astype(np.int64).reshape(N, 8, 16, W); o = own.astype(np.int64).reshape(N, 8, 16, B); nx = nb.astype(np.int64).reshape(N, 8, 16, B)
    ta, pr, fo, u = tau.astype(np.int64), prev.astype(np.int64), foe.astype(np.int64), tas.astype(np.int64)
    w = wt.astype(np.int64).reshape(N, 8, 16, 1); bird = np.arange(B)[None, :]; grp = np.arange(8)[:, None]
    for t in range(RO):
        dist = 1 + t % (N - 1); top, low, raids = [], [], []
        for r in range(N):
            v = look(x[r], o[r], u[r], t); m = np.max(v, axis=2); top.append(m)
            low.append(np.argmin(np.add.reduce((v == m[:, :, None, :]).astype(np.int64), axis=1), axis=1))
        for r in range(N):
            q = (r + dist) % N; ix = ta[r][:, None, :]
            y = look(x[q], np.take_along_axis(o[q], ix, 2), u[r], t)
            g = np.argmax(np.add.reduce(np.maximum(y - top[r][:, :, None, :], 0), axis=1), axis=1)
            ok = np.add.reduce((np.take_along_axis(top[q], ix, 2) > top[r]).astype(np.int64), axis=1) < NEED
            first = np.full((8, B), B, np.int64); np.minimum.at(first, (np.broadcast_to(grp, (8, B)), ta[r]), np.where(ok, bird, B))
            a, b = np.nonzero(ok & (np.take_along_axis(first, ta[r], 1) == bird))
            raids.append((r, q, a, b, ta[r][a, b], g[a, b], low[r][a, b]))
        no, nt, npr, nf = np.array(o), np.array(fo), np.array(pr), np.array(fo); stolen = np.zeros((N, 1, 1), np.int64)
        for r, q, a, b, v, g, j in raids:
            no[r, a, j, b] = o[q, a, g, v]; npr[r, a, b] = v; nt[r, a, b] = nx[q, a, g, v]
        for r, q, a, b, v, g, j in raids:
            no[q, a, g, v] = o[r, a, j, b]; nf[q, a, v] = b; nt[q, a, v] = pr[r, a, b]; stolen[q] = len(a)
        u = (np.add.reduce(w * np.stack(top), axis=2) + stolen) & 1023
        o, ta, pr, fo = no, nt, npr, nf
    return {"yo": o.reshape(N, 128, B).astype(np.float32), "yt": ta.astype(np.float32), "yp": pr.astype(np.float32), "yf": fo.astype(np.float32), "yu": u.astype(np.float32)}

@@ -1,0 +1,606 @@
+from concourse.mybir import AluOpType as A, AxisListType, ActivationFunctionType as F
+
+NB, W, RO, N = 192, 4096, 5, 4
+WX = 4416
+S3 = 16 * NB
+H = NB // 2
+
+SCRATCH = {
+    "hx": ("sbuf", [128, WX], "bfloat16"), "ownI": ("sbuf", [128, NB], "int32"), "nbI": ("sbuf", [128, NB], "int32"),
+    "in4": ("sbuf", [8, 4 * NB], "int32"), "wtI": ("sbuf", [128, 1], "int32"),
+    "in4h": ("sbuf", [8, 3 * NB], "bfloat16"), "tash": ("sbuf", [8, NB], "float16"), "sel8": ("sbuf", [8, 128], "float16"),
+    "nbb": ("sbuf", [128, NB], "bfloat16"),
+    "pI": ("sbuf", [128, 4], "int32"), "pF": ("sbuf", [128, 8], "float32"), "cg": ("sbuf", [128, 128], "float32"),
+    "dif": ("sbuf", [128, 128], "float32"), "xb": ("sbuf", [12, 128], "bfloat16"), "xf": ("sbuf", [12, 128], "float32"),
+    "iB": ("sbuf", [128, 2048], "bfloat16"), "g8": ("sbuf", [128, 8], "bfloat16"), "idF": ("sbuf", [12, 12], "float32"),
+    "CLT": ("sbuf", [128, 2048], "bfloat16"), "CLP": ("sbuf", [128, 2048], "bfloat16"),
+    "blk": ("sbuf", [128, 128], "bfloat16"), "blkH": ("sbuf", [128, 128], "float16"), "blkG": ("sbuf", [128, 128], "bfloat16"),
+    "c128": ("sbuf", [128, NB], "bfloat16"),
+    "one": ("sbuf", [128, 128], "float32"), "wtb": ("sbuf", [128, 128], "bfloat16"), "idb": ("sbuf", [128, 128], "bfloat16"),
+    "nid": ("sbuf", [128, 128], "bfloat16"), "cbE": ("sbuf", [128, NB], "bfloat16"),
+    "m8": ("sbuf", [128, 16], "bfloat16"), "onM": ("sbuf", [128, 96], "bfloat16"),
+    "brow": ("sbuf", [128, 512], "bfloat16"), "mk32": ("sbuf", [128, 512], "float32"), "m16": ("sbuf", [128, S3 // 4], "bfloat16"),
+    "hf": ("sbuf", [128, NB], "float32"), "zr": ("sbuf", [128, NB], "float32"),
+    "w2": ("sbuf", [128, NB], "float32"), "w25": ("sbuf", [128, NB], "float32"), "w2b": ("sbuf", [128, NB], "bfloat16"),
+    "wL": ("sbuf", [128, 12], "float32"), "cL": ("sbuf", [128, 12], "float32"),
+    "o1": ("sbuf", [128, 6 * NB], "float32"), "w": ("sbuf", [128, 6 * NB], "float32"), "wr": ("sbuf", [128, 5 * NB], "float32"),
+    "stL": ("sbuf", [128, 6 * 24], "float32"), "stR": ("sbuf", [128, 5 * 24], "float32"), "foL": ("sbuf", [128, 6 * 12], "float32"),
+    "Ub": ("sbuf", [128, 5 * NB], "bfloat16"), "Ur": ("sbuf", [128, 5 * NB], "bfloat16"),
+    "JO": ("sbuf", [128, 5 * NB], "float16"), "JOr": ("sbuf", [128, 5 * NB], "float16"),
+    "wl": ("sbuf", [128, 5 * 12], "float32"), "wlO": ("sbuf", [128, 5 * 12], "float32"),
+    "wn": ("sbuf", [128, 5 * NB], "bfloat16"), "wnO": ("sbuf", [128, 5 * NB], "bfloat16"),
+    "got": ("sbuf", [128, 5 * NB], "float16"), "gotr": ("sbuf", [128, 5 * NB], "float16"),
+    "nbt": ("sbuf", [128, 5 * NB], "bfloat16"), "nbtr": ("sbuf", [128, 5 * NB], "bfloat16"),
+    "q": ("sbuf", [128, NB], "int32"), "sh": ("sbuf", [128, NB], "int32"), "offH": ("sbuf", [128, NB], "uint16"),
+    "q2": ("sbuf", [128, NB], "int32"), "sh2": ("sbuf", [128, NB], "int32"), "offA": ("sbuf", [128, NB], "uint16"),
+    "x": ("sbuf", [128, S3], "bfloat16"), "s": ("sbuf", [128, S3], "bfloat16"),
+    "e": ("sbuf", [128, S3], "bfloat16"), "y": ("sbuf", [128, S3], "bfloat16"), "z": ("sbuf", [128, S3], "bfloat16"),
+    "sc": ("sbuf", [128, 512], "float32"), "sc2": ("sbuf", [128, 512], "float32"),
+    "OT": ("sbuf", [128, 512], "bfloat16"), "OT2": ("sbuf", [128, 512], "bfloat16"),
+    "tl": ("sbuf", [128, 12], "uint16"), "oVm": ("sbuf", [128, NB], "float32"), "oV": ("sbuf", [128, NB], "float32"),
+    "o0": ("sbuf", [128, NB], "float32"), "om": ("sbuf", [128, NB], "float32"),
+    "nbV": ("sbuf", [128, NB], "bfloat16"), "UV": ("sbuf", [128, NB], "bfloat16"), "stb": ("sbuf", [128, 24], "bfloat16"),
+    "tR": ("sbuf", [128, NB], "bfloat16"), "FB": ("sbuf", [128, NB], "bfloat16"),
+    "G": ("sbuf", [128, 12 * NB], "bfloat16"), "LT": ("sbuf", [128, 12 * 128], "bfloat16"),
+    "cmp": ("sbuf", [128, NB], "bfloat16"), "okw": ("sbuf", [128, 12], "float32"), "thr": ("sbuf", [128, NB], "float32"),
+    "cnt": ("sbuf", [128, 1], "float32"), "offV": ("sbuf", [128, 12], "uint16"), "Vo": ("sbuf", [128, NB], "float32"),
+    "nbw": ("sbuf", [128, NB], "float32"), "V3": ("sbuf", [128, NB], "bfloat16"),
+    "Cw": ("sbuf", [128, 2 * NB], "bfloat16"), "Xw": ("sbuf", [128, 2 * NB], "float32"),
+    "nj": ("sbuf", [128, NB], "float32"), "XS": ("sbuf", [128, NB], "float32"),
+    "uA": ("sbuf", [128, NB], "int32"), "uI": ("sbuf", [128, NB], "int32"),
+    "jw": ("sbuf", [128, NB], "float32"), "nw": ("sbuf", [128, NB], "float32"), "oj": ("sbuf", [128, NB], "float32"),
+    "c2": ("sbuf", [128, NB], "float32"), "jk": ("sbuf", [128, NB], "float32"), "Jw": ("sbuf", [128, NB], "float32"),
+    "bw": ("sbuf", [128, NB], "float32"), "cw": ("sbuf", [128, NB], "float32"),
+    "cI": ("sbuf", [128, 12], "int32"), "lo": ("sbuf", [128, 12], "int32"), "hi": ("sbuf", [128, 12], "int32"),
+    "Lt": ("sbuf", [128, 12 * 16], "float32"), "stO": ("sbuf", [128, 36], "bfloat16"), "o8": ("sbuf", [8, 3 * NB], "float32"),
+    "pD0": ("psum", [128, 512], "float32"), "pD1": ("psum", [128, 512], "float32"),
+    "pK": ("psum", [128, 512], "float32"), "pK2": ("psum", [128, 512], "float32"), "pK3": ("psum", [128, 512], "float32"),
+    "pU": ("psum", [128, 512], "float32"), "pS": ("psum", [128, 512], "float32"), "pR": ("psum", [128, 512], "float32"),
+}
+PS = ("pD0", "pD1", "pK", "pK2", "pK3", "pU", "pS", "pR")
+TWO = ("bfloat16", "uint16", "float16")
+MSG = ("A", "W", "B", "C", "F", "D", "E", "L")
+SEMAPHORES = ["v", "a", "p", "k", "left"] + ["ld%d" % i for i in range(9)] + ["st%d" % i for i in range(5)] \
+    + ["m%s%d" % (m, t) for m in MSG for t in range(RO)]
+CHAIN = ("G", "s")
+EV = (0, 1, 2, 3, 4, 5)
+PRI = {"G@0": 4, "s@0": 1, "Lt@0": 2, "xb@0": -2, "pD0@0": 2, "pK@16": -8, "pK2@160": -8, "pK@48": 2, "pK3@16": 8, "Vo@0": -2,
+       "pK2@16": -8, "pK3@128": 4, "pK3@48": -2, "pK3@224": -2, "pK@64": -4, "uA@0": -4, "pK3@96": 8, "pK2@80": -8, "pK@160": 8,
+       "one@0": 8, "pK2@224": -1, "blkH@0": 4, "g8@0": 1, "V3@0": -1, "pS@432": 8, "pS@256": -8, "hf@0": -4, "pR@384": 0.3,
+       "wtb@0": -4, "pK3@32": 8, "pK@0": -1, "pK3@64": -4, "pK2@176": -2, "m8@0": -2, "nj@0": 0.3, "pS@272": -4, "OT@0": -1,
+       "Lt@84": -2, "okw@0": 0.3}
+ENG = {"LT@0": 3, "oV@0": -1, "stb@0": -1, "pU@192": -0.3, "wn@0": 1, "x@0": 0.3, "o0@0": -0.3}
+CYC, LATE, FLY, SPARE, SPARE2, AHEAD, VF = 0.001, 0.08, 2.2, 1.5, 3.0, 0.07, 0.01
+
+
+def order(ops):
+    n = len(ops)
+    succ = [[] for _ in ops]
+    miss = [0] * n
+    for i, o in enumerate(ops):
+        for d in o["deps"]:
+            succ[d].append(i)
+            miss[i] += 1
+    tail, name = [0.0] * n, []
+    for i in range(n - 1, -1, -1):
+        tail[i] = min(c[1] for c in ops[i]["alt"]) + ops[i]["late"] + max([tail[j] for j in succ[i]] + [0.0])
+    for i, o in enumerate(ops):
+        r = (o["writes"] or o["reads"])[0]
+        name.append("%s@%d" % (r[1], r[2] if r[1] in PS or r[1] == "Lt" else 0))
+        tail[i] += PRI.get(name[i], 0.0)
+    ready = {i: 0.0 for i in range(n) if not miss[i]}
+    free, bank, out, done = {}, {}, [], {}
+    while ready:
+        can = {}
+        top = max(max(r, min(free.get(q, 0.0) for q, _ in ops[i]["alt"])) + tail[i] for i, r in ready.items())
+        for i, r in ready.items():
+            o, mine = ops[i], None
+            for q, c in o["alt"]:
+                t0 = max(r, free.get(q, 0.0))
+                for b in o["banks"]:
+                    for q2, e in bank.get(b, {}).items():
+                        if q2 != q:
+                            t0 = max(t0, e + LATE)
+                z = t0 + c
+                if q == "v" and len(o["alt"]) > 1:
+                    z += ENG.get(name[i], 0.0) + min(SPARE, SPARE2 * max(0.0, top - t0 - tail[i]))
+                if mine is None or z < mine[0]:
+                    mine = (z, t0, t0 + c, i, q)
+            can.setdefault(mine[4], []).append(mine)
+        best = None
+        for q, lst in can.items():
+            m = min(z[1] for z in lst) + AHEAD
+            z = max((z for z in lst if z[1] <= m), key=lambda z: tail[z[3]])
+            if best is None or z[1] < best[1]:
+                best = z
+        _, t0, fin, i, q = best
+        del ready[i]
+        o = ops[i]
+        free[q] = fin
+        for b in o["banks"]:
+            bank.setdefault(b, {})[q] = fin
+        done[i] = fin + o["late"]
+        out.append((t0, i, q))
+        for j in succ[i]:
+            miss[j] -= 1
+            if not miss[j]:
+                ready[j] = max(done[d] for d in ops[j]["deps"])
+    out.sort(key=lambda z: (z[0], z[1]))
+    return out
+
+
+def rank_program(g, core, T, topo):
+    rank = T.rank_of(core)
+    if rank is None:
+        return
+    queues = {"v": g.vector, "a": g.scalar, "p": g.tensor, "k": g, "y": g.sync}
+    ops, last, chain, sent = [], {}, {}, {}
+
+    def P(name, c0=0, c1=None, step=1, p=128):
+        b = T[name]
+        c1 = b.shape[1] if c1 is None else c1
+        p = min(p, b.shape[0])
+        return (b[0:p, c0:c1:step] if step > 1 else b[0:p, c0:c1], name, c0, c1, (c1 - c0 + step - 1) // step)
+
+    def IND(win, off):
+        return (win[0].indirect(off[0]), win, off)
+
+    def flat(xs):
+        out = []
+        for x in xs:
+            out += [x[1], x[2]] if len(x) == 3 else [x]
+        return out
+
+    def put(kind, alt, reads, writes, late=None, **more):
+        reads, writes = flat(reads), flat(writes)
+        i, deps = len(ops), set()
+        for lst, wr in ((reads, False), (writes, True)):
+            for r in lst:
+                for (a0, a1, w, j) in last.get(r[1], ()):
+                    if (wr or w) and a0 < r[3] and r[2] < a1:
+                        deps.add(j)
+        for lst, wr in ((reads, False), (writes, True)):
+            for r in lst:
+                h = last.setdefault(r[1], [])
+                if wr:
+                    h[:] = [z for z in h if not (r[2] <= z[0] and z[1] <= r[3])]
+                h.append((r[2], r[3], wr, i))
+        if writes and writes[0][1] in CHAIN:
+            if writes[0][1] in chain:
+                deps.add(chain[writes[0][1]])
+            chain[writes[0][1]] = i
+        deps.discard(i)
+        banks = sorted(set(r[1] for r in reads + writes if r[1] in PS))
+        o = {"kind": kind, "alt": [(q, c) for q, c, _ in alt], "fns": {q: f for q, _, f in alt}, "reads": reads, "writes": writes,
+             "deps": deps, "banks": banks, "late": LATE if late is None else late}
+        o.update(more)
+        ops.append(o)
+        return i
+
+    V, Sc, Te = g.vector, g.scalar, g.tensor
+    dts = lambda x: SCRATCH[(x[1] if len(x) == 3 else x)[1]][2]
+    two = lambda xs: all(dts(x) in TWO and (len(x) == 3 or x[1] not in PS) for x in xs)
+    vc = lambda n, cyc=1.0: (0.05 if cyc in (1.5, 3.5) else VF) + max(64, n * cyc) * CYC
+    ac = lambda n, cyc=1.0: (0.065 if cyc == 1.5 else VF) + max(64, n * cyc) * CYC
+    size = lambda x: 16 * (x[2][3] - x[2][2]) if len(x) == 3 else x[4]
+
+    def cp(out, in_, qs="v"):
+        alt = []
+        gat, sca = len(in_) == 3, len(out) == 3
+        n = size(in_)
+        if "v" in qs:
+            alt.append(("v", vc(n, 1.5 if gat else 3.5 if sca else 0.5 if two([out, in_]) else 1.0), [lambda: V.tensor_copy(out[0], in_[0])]))
+        if "a" in qs:
+            alt.append(("a", ac(n, 1.5 if gat else 1.0), [lambda: Sc.activation(out[0], in_[0], F.Copy)]))
+        put("op", alt, [in_], [out])
+
+    def act(out, in_, func, bias=0.0):
+        put("op", [("a", ac(size(out)), [lambda: Sc.activation(out[0], in_[0], func, bias=bias)])], [in_], [out])
+
+    def lin(out, in_, m, b):
+        put("op", [("v", vc(size(out), 0.5 if two([out, in_]) else 1.0), [lambda: V.tensor_scalar(out[0], in_[0], m, b, A.mult, A.add)]),
+                   ("a", ac(size(out)), [lambda: Sc.activation(out[0], in_[0], F.Identity, bias=b, scale=m)])], [in_], [out])
+
+    def lin1(out, in_):
+        put("op", [("v", vc(size(out)), [lambda: V.tensor_scalar(out[0], in_[0], 0.5, None, A.is_lt)]),
+                   ("a", ac(size(out)), [lambda: Sc.activation(out[0], in_[0], F.Relu, bias=1.0, scale=-1.0)])], [in_], [out])
+
+    def tt(out, a, b, o):
+        ps = a[1] in PS or b[1] in PS
+        put("op", [("v", vc(size(out), 1.0 if ps else 2.0), [lambda: V.tensor_tensor(out[0], a[0], b[0], o)])], [a, b], [out])
+
+    def ts(out, a, s1, o1, s2=None, o2=None):
+        rs = [a]
+        x1, x2 = s1, s2
+        if isinstance(s1, tuple):
+            rs.append(s1)
+            x1 = s1[0]
+        if o2 is None:
+            f = lambda: V.tensor_scalar(out[0], a[0], x1, None, o1)
+        else:
+            f = lambda: V.tensor_scalar(out[0], a[0], x1, x2, o1, o2)
+        put("op", [("v", vc(size(out), 0.5 if two([out, a]) else 1.0), [f])], rs, [out])
+
+    def ms(out, c):
+        put("op", [("v", vc(size(out)), [lambda: V.memset(out[0], c)])], [], [out])
+
+    def scan(out, d0, d1, init, o0, o1):
+        put("op", [("v", vc(size(out), 0.5 if two([out, d0, d1]) else 1.0),
+                    [lambda: V.tensor_tensor_scan(out[0], d0[0], d1[0], init, o0, o1)])], [d0, d1], [out])
+
+    def closes(n):
+        n[0] -= 1
+        return n[0] == 0
+
+    def mms(lst, reads=()):
+        c = sum((0.01 + max(min(64, l[4]), n) / 1300.0) * (4 if dts(r) == "float32" else 1) for _, l, r, _, _, n in lst)
+        fns = [lambda z=z: Te.matmul(z[0][0], z[1][0], z[2][0], z[3], z[4] if isinstance(z[4], bool) else closes(z[4])) for z in lst]
+        rd, wr = {}, {}
+        for o, l, r, _, _, _ in lst:
+            for x, d in ((l, rd), (r, rd), (o, wr)):
+                z = d.get(x[1])
+                d[x[1]] = (None, x[1], min(x[2], z[2]) if z else x[2], max(x[3], z[3]) if z else x[3], 0)
+        put("op", [("p", c, fns)], list(rd.values()) + list(reads), list(wr.values()))
+
+    def mm(out, l, r, start=True, stop=True, reads=()):
+        mms([(out, l, r, start, stop, r[4])], reads)
+
+    def iota(out, pattern, base, cmul, flag=True):
+        if flag:
+            f = lambda: g.iota(out[0], pattern, base, cmul, allow_small_or_imprecise_dtypes=True)
+        else:
+            f = lambda: g.iota(out[0], pattern, base, cmul)
+        put("op", [("k", 0.15 + 2 * size(out) * CYC, [f])], [], [out])
+
+    def dma(q, out, in_, sem, reads=(), writes=(), late=2.2):
+        put("dma", [(q, 0.1, [lambda: queues[q].dma_start(out, in_)])], list(reads), list(writes), late, sem=sem)
+
+    def send(msg, t, dst, out, in_):
+        sent[(msg, t)] = put("send", [("k", 0.6, None)], [in_], [], FLY + 0.0015 * in_[4] * (2 if dts(in_) in TWO else 4),
+                             args=(msg, t, dst, out, in_))
+
+    def recv(msg, t, src, buf):
+        i = put("recv", [("r%s%d" % (msg, t), 0.0, None)], [], [buf], 0.0, args=(msg, t, src, buf))
+        ops[i]["deps"].add(sent[(msg, t)])
+
+    def rl(out, src, c0=0, p=128, wide=False):
+        k, sel = (8, P("idb", 0, 8, 1, 8)) if p == 8 else (128, P("g8"))
+        mms([(P("pR", 384 + i, 512, 16, 12), P(src, c0 + i, c0 + NB, 16, k), sel, True, True, 8) for i in range(16)])
+        xt, turn = (P("xf"), P("idF")) if wide else (P("xb"), P("idb", 0, 12, 1, 12))
+        cp(xt, P("pR", 384, 512, 1, 12), "va")
+        mms([(out, xt, turn, True, True, 12)])
+
+    dma("y", T.in4[0:8, 3 * NB:4 * NB], T.tas[:, :], "ld1", [], [P("in4", 3 * NB, 4 * NB, 1, 8)])
+    dma("y", T.ownI[:, :], T.own[:, :], "ld2", [], [P("ownI")])
+    dma("y", T.hx[:, 0:W], T.hue[:, :], "ld3", [], [P("hx", 0, W)], 8.0)
+    dma("a", T.in4[0:8, 0:NB], T.tau[:, :], "ld0", [], [P("in4", 0, NB, 1, 8)])
+    dma("a", T.in4[0:8, NB:2 * NB], T.prev[:, :], "ld4", [], [P("in4", NB, 2 * NB, 1, 8)])
+    dma("a", T.in4[0:8, 2 * NB:3 * NB], T.foe[:, :], "ld5", [], [P("in4", 2 * NB, 3 * NB, 1, 8)])
+    dma("a", T.wtI[:, :], T.wt[:, :], "ld6", [], [P("wtI")])
+    dma("a", T.nbI[:, :], T.nb[:, :], "ld7", [], [P("nbI")])
+    dma("y", T.hx[:, W:WX], T.hue[:, 0:WX - W], "ld8", [], [P("hx", W, WX)])
+
+    PI = lambda j: P("pI", j, j + 1)
+    PF = lambda j, p=128: P("pF", j, j + 1, 1, p)
+    iota(PI(0), [[0, 1]], 0, 1, False)
+    iota(P("cg"), [[1, 8], [0, 16]], 0, 0)
+    iota(P("iB"), [[1, 16], [16, 8], [0, 16]], 0, 0)
+    iota(P("dif"), [[1, 128]], 0, -1)
+    iota(P("thr", 0, 8), [[1, 2], [2, 4]], 0, 0)
+    iota(P("brow"), [[0, 16], [-1000, 2], [-1, 16]], 15, 0)
+    iota(P("w25"), [[1, NB]], 1, 0)
+    iota(P("cL"), [[16, 12]], NB, 0)
+    iota(P("okw", 0, 8), [[1, 8]], 0, 0)
+    ts(PI(1), PI(0), 4, A.logical_shift_right)
+    ts(PI(2), PI(0), 15, A.bitwise_and)
+    for j in range(3):
+        cp(PF(j), PI(j))
+    ts(PF(5), PF(2), 0.0, A.is_equal)
+    ts(P("idb"), P("dif"), 0.0, A.is_equal)
+    ts(P("g8"), P("okw", 0, 8), PF(1), A.is_equal)
+    ts(P("sel8"), P("cg", 0, 128, 1, 8), PF(0, 8), A.is_equal)
+    cp(P("tash"), P("in4", 3 * NB, 4 * NB, 1, 8))
+    mm(P("pS", 0, NB), P("sel8"), P("tash"))
+    lin(P("w", 0, NB), P("pS", 0, NB), 2.0, 33.0)
+    host = T.cores[(rank + 1) % N]
+    send("W", 0, host, P("wr", 0, NB), P("w", 0, NB))
+    tt(P("q"), P("ownI"), P("w", 0, NB), A.mult)
+    ts(P("sh"), P("q"), 5, A.logical_shift_right, W - 1, A.bitwise_and)
+    cp(P("offH"), P("sh"))
+    cp(P("in4h"), P("in4", 0, 3 * NB, 1, 8))
+    for f in range(3):
+        rl(P("pS", 448 + 12 * f, 460 + 12 * f), "in4h", NB * f, 8)
+    cp(P("stL", 0, 24), P("pS", 448, 472), "va")
+    send("A", 0, host, P("stR", 0, 24), P("stL", 0, 24))
+    lin(P("foL", 0, 12), P("pS", 472, 484), 1.0, 1.0)
+    ts(P("blk"), P("cg"), PF(1), A.is_equal)
+    ms(P("m16"), 1.0)
+    ms(P("m16", 0, S3 // 4, 16), 0.0)
+    ts(P("CLT"), P("iB"), PF(0), A.is_equal)
+    ts(P("o1", 0, NB), P("ownI"), 1.0, A.add)
+    ts(P("idF"), P("dif", 0, 12, 1, 12), 0.0, A.is_equal)
+    ts(P("nid"), P("dif"), 0.0, A.is_equal, -1.0, A.mult)
+    cp(PF(6), P("wtI"))
+    ts(P("wtb"), P("blk"), PF(6), A.mult)
+    ts(P("m8", 0, 8), P("thr", 0, 8), PF(1), A.is_equal, -16.0, A.mult)
+    ts(P("m8", 8, 16), P("thr", 0, 8), PF(1), A.is_equal, 16.0, A.mult)
+    cp(P("nbb"), P("nbI"))
+    ms(P("onM"), 1.0 / 128)
+    ms(P("mk32"), 0.0)
+    ms(P("mk32", 0, 512, 32), -1000000.0)
+    ts(P("cbE"), P("w25"), PF(5), A.mult)
+    ms(P("hf"), 0.5)
+    ms(P("zr"), 0.0)
+    scan(P("w2"), P("hf"), P("zr"), 2.0 ** 97, A.mult, A.add)
+    cp(P("w2b"), P("w2"))
+    ts(P("w25"), P("w2"), 2.5, A.mult)
+    rl(P("pS", 484, 496), "w2b")
+    lin(P("wL"), P("pS", 484, 496), 1.0 / 16, 0.0)
+    ts(P("cL"), P("cL"), PF(2), A.add)
+    ms(P("CLP"), 0.0)
+    ts(P("CLP", 1, 2048, 16), P("CLT", 1, 2048, 16), 256.0, A.mult)
+    cp(P("blkH"), P("blk"))
+    ts(P("blkG"), P("blk"), 128.0, A.mult)
+    ms(P("c128"), 128.0)
+    ms(P("one"), 1.0)
+
+    def key(pk, h, k, lhs, sgn, n):
+        return ((T[pk][0:96, 256 * h + k:256 * h + 256:32], pk, 16 * k, 16 * k + 16, 8), lhs, P("m8", 8 * sgn, 8 * sgn + 8), False, n, 8)
+
+    def onehot(pk, sc, ot, out, half=None):
+        n, d, hs = (512, 0, (0, 1)) if half is None else (256, 256 * half, (half,))
+        scan(P(sc, d, d + n, 1, 96), P("mk32", 0, n, 1, 96), P(pk, 0, n, 1, 96), 0.0, A.add, A.max)
+        tt(P(ot, d, d + n - 16, 1, 96), P(pk, 0, n - 16, 1, 96), P(sc, d + 16, d + n, 1, 96), A.is_equal)
+        mms([(P("pR", out + H * h, out + H * h + H), P(ot, c, c + 128, 1, 96), P("idb", 0, 96, 1, 96), c == 256 * h, c != 256 * h, 96)
+             for h in hs for c in (256 * h, 256 * h + 112)])
+
+    Lx = lambda j: P("Lt", 12 * j, 12 * j + 12)
+    Q4 = S3 // 4
+    HALVES = ((0, H), (H, NB))
+    wR, wP, GP = P("pU", NB, 2 * NB), P("pU", 0, NB), P("pR", NB, 2 * NB)
+    x0, x1, x2 = P("pD0", 0, NB), P("pD0", NB, 2 * NB), P("pD1", 0, NB)
+    for t in range(RO):
+        dist = 1 + t % (N - 1)
+        host, guest = T.cores[(rank + dist) % N], T.cores[(rank - dist) % N]
+        nhost = T.cores[(rank + 1 + (t + 1) % (N - 1)) % N]
+        b0, b1 = NB * t, NB * t + NB
+        R = lambda n: P(n, b0, b1)
+        fin = t == RO - 1
+        nK, nK2, nK3 = [32], [16], [16]
+        for pk, n in (("pK", 512), ("pK2", 256), ("pK3", 256)):
+            mms([(P(pk, 0, n, 1, 96), P("onM"), P("brow", 0, n), True, False, n)])
+        for h in range(4):
+            cp(P("x", Q4 * h, Q4 * h + Q4), IND(P("hx"), P("offH", 48 * h, 48 * h + 48)), "va")
+        for h in range(4):
+            scan(P("s", Q4 * h, Q4 * h + Q4), P("m16"), P("x", Q4 * h, Q4 * h + Q4), 0.0, A.mult, A.max)
+        cp(R("Ub"), P("s", 15, S3, 16), "va")
+        send("B", t, host, R("Ur"), R("Ub"))
+        mm(P("pS", 0, NB), P("wtb"), R("Ub"))
+        recv("A", t, guest, P("stR", 24 * t, 24 * t + 24))
+        recv("W", t, guest, R("wr"))
+        sr = P("stR", 24 * t, 24 * t + 12)
+        cp(P("tl"), sr)
+        lin(P("o0"), R("o1"), 1.0, -1.0)
+        lin(P("om"), R("o1"), 1.0, -2048.0)
+        cp(P("oV"), IND(P("o0"), P("tl")), "va")
+        lin(P("oVm"), P("oV"), 1.0, -2047.0)
+        cp(wR, R("wr"), "va")
+        for a, b in HALVES:
+            tt(P("q2", a, b), P("oV", a, b), P("pU", NB + a, NB + b), A.mult)
+            ts(P("sh2", a, b), P("q2", a, b), 5, A.logical_shift_right, W - 1, A.bitwise_and)
+            if t:
+                ts(P("offA", a, b), P("sh2", a, b), 77.0 * t, A.add)
+            else:
+                cp(P("offA", a, b), P("sh2", a, b))
+        for h in range(4):
+            cp(P("y", Q4 * h, Q4 * h + Q4), IND(P("hx"), P("offA", 48 * h, 48 * h + 48)), "va")
+        cp(P("stb"), P("stR", 24 * t, 24 * t + 24), "va")
+        mms([(P("pR", i, NB, 16), P("CLT", 128 * i, 128 * i + 128), P("stb", 0, 12), True, True, 12) for i in range(16)])
+        cp(P("tR"), P("pR", 0, NB), "va")
+        mms([(GP, P("idb"), P("cbE"), True, False, NB)] +
+            [(P("pR", NB + i, 2 * NB, 16), P("CLP", 128 * i, 128 * i + 128), P("stb", 12, 24), False, i == 15, 12) for i in range(16)])
+        cp(P("FB"), GP, "va")
+        Uo = P("pS", 256, 448)
+        if EV:
+            cp(Uo, R("Ub"))
+        for c in range(8):
+            if c in EV:
+                for k in (2 * c, 2 * c + 1):
+                    tt(P("e", NB * k, NB * k + NB), P("x", k, S3, 16), Uo, A.is_equal)
+                    mms([key("pK", h, k, P("e", NB * k + H * h, NB * k + H * h + H), 0, nK) for h in (0, 1)])
+                continue
+            pd = "pD%d" % (c % 2)
+            mms([z for d in (0, 1) for z in ((P(pd, NB * d, NB * d + NB), P("idb"), P("x", 2 * c + d, S3, 16), True, False, NB),
+                                             (P(pd, NB * d, NB * d + NB), P("nid"), R("Ub"), False, True, NB))])
+            act(P("e", 384 * c, 384 * c + 384), P(pd, 0, 384), F.Relu, 1.0)
+            mms([key("pK", h, 2 * c + d, P("e", 384 * c + NB * d + H * h, 384 * c + NB * d + H * h + H), 0, nK)
+                 for d in (0, 1) for h in (0, 1)])
+        for c in range(12):
+            ts(P("G", NB * c + 16 * c, NB * c + NB), P("tR", 16 * c, NB), P("stR", 24 * t + c, 24 * t + c + 1), A.is_equal)
+        cp(P("nbV"), IND(P("nbb"), P("tl")), "va")
+        recv("B", t, guest, R("Ur"))
+        cp(P("UV"), IND(R("Ub"), P("tl")), "va")
+        cp(P("pU", 0, NB), R("Ur"))
+        tt(P("cmp"), P("UV"), P("pU", 0, NB), A.is_gt)
+        rl(P("pS", 448, 460), "cmp")
+        mm(P("pS", 256, 448), P("blk"), P("cmp"))
+        ts(Lx(8), P("pS", 448, 460), 8.5, A.is_lt)
+        tt(P("okw"), Lx(8), P("wL"), A.mult)
+        ts(wR, P("pS", 256, 448), 8.5, A.is_lt)
+        tt(P("thr"), wR, P("w25"), A.mult)
+        for c in range(12):
+            o, s = P("LT", 128 * c, 128 * c + 128), P("okw", c, c + 1)
+            put("op", [("v", vc(128, 0.5), [lambda o=o, s=s: V.tensor_scalar(o[0], T.blk[:, :], s[0], None, A.mult)]),
+                       ("a", ac(128), [lambda o=o, s=s: Sc.activation(o[0], T.blk[:, :], F.Copy, scale=s[0])])], [P("blk"), s], [o])
+        for c in range(12):
+            mm(P("pS", 256 + 16 * c, 448), P("LT", 128 * c, 128 * c + 128), P("G", NB * c + 16 * c, NB * c + NB), c == 0, c == 11, [P("pS", 0, 1)])
+        tt(wR, P("pS", 256, 448), P("thr"), A.is_lt)
+        cp(R("wn"), wR, "va")
+        send("F", t, guest, R("wnO"), R("wn"))
+        for h in (0, 1):
+            for k in range(16):
+                zz = P("z", 1536 * h + H * k, 1536 * h + H * k + H)
+                tt(zz, P("y", 1536 * h + k, 1536 * h + 1536, 16), P("pU", H * h, H * h + H), A.max)
+                mms([key(("pK2", "pK3")[h], 0, k, zz, 1, (nK2, nK3)[h])])
+        onehot("pK", "sc", "OT", 0)
+        tt(R("JO"), P("om"), P("pR", 0, NB), A.mult)
+        send("C", t, host, R("JOr"), R("JO"))
+        onehot("pK2", "sc2", "OT2", NB, 0)
+        onehot("pK3", "sc2", "OT2", NB, 1)
+        tt(P("Vo"), P("oVm"), wR, A.mult)
+        tt(R("got"), P("Vo"), GP, A.mult)
+        send("D", t, guest, R("gotr"), R("got"))
+        tt(P("nbw"), P("nbV"), wR, A.mult)
+        tt(R("nbt"), P("nbw"), GP, A.mult)
+        send("E", t, guest, R("nbtr"), R("nbt"))
+        rl(P("pS", 460, 472), "wn", b0)
+        wl, wo = P("wl", 12 * t, 12 * t + 12), P("wlO", 12 * t, 12 * t + 12)
+        lin(wl, P("pS", 460, 472), 1.0 / 16, 0.0)
+        send("L", t, guest, wo, wl)
+        put("op", [("v", vc(12), [lambda wl=wl: V.tensor_reduce(T.cnt[:, :], wl[0], AxisListType.X, A.add)])], [wl], [P("cnt")])
+        mm(P("pS", NB, NB + 1), P("one"), P("cnt"))
+        w_ = P("w", b0 + NB, b1 + NB)
+        ts(P("uA"), P("pS", 0, NB), P("pS", NB, NB + 1), A.add)
+        ts(P("uI"), P("uA"), 1023, A.bitwise_and)
+        if not fin:
+            ts(wP, P("uI"), 2.0, A.mult, 33.0, A.add)
+            cp(w_, wP, "va")
+            send("W", t + 1, nhost, P("wr", b0 + NB, b1 + NB), w_)
+        tt(Lx(6), sr, P("cL"), A.subtract)
+        tt(Lx(7), wl, Lx(6), A.mult)
+        tt(Lx(7), Lx(7), P("cL"), A.add)
+        cp(P("offV"), Lx(7))
+        tt(P("V3"), P("FB"), wR, A.mult)
+        cp(P("Cw", 0, NB), P("zr"), "va")
+        cp(IND(P("Cw"), P("offV")), P("V3"))
+        rl(P("pS", 472, 484), "Cw", 0, 128, True)
+        recv("C", t, guest, R("JOr"))
+        mms([(P("pS", 256, 448), P("blk"), P("c128"), True, False, NB), (P("pS", 256, 448), P("blkH"), R("JOr"), False, True, NB)])
+        tt(P("nj"), R("wn"), P("pS", 256, 448), A.mult)
+        tt(P("XS"), P("nj"), GP, A.mult)
+        cp(P("Xw", 0, NB), P("zr"), "va")
+        cp(IND(P("Xw"), P("offV")), P("XS"))
+        recv("F", t, host, R("wnO"))
+        mm(P("pK2", 0, NB), P("blkG"), R("wnO"), True, False)
+        tt(P("jw"), P("pR", 0, NB), R("wnO"), A.mult)
+        lin(x0, P("jw"), -1.0, 1.0)
+        tt(P("oj"), x0, R("o1"), A.mult)
+        lin1(x1, P("Xw", 0, NB))
+        tt(x2, P("oj"), x1, A.mult)
+        tt(P("c2"), x2, P("Xw", 0, NB), A.add)
+        tt(P("jk"), P("jw"), x1, A.mult)
+        if not fin:
+            tt(P("Jw"), P("jk"), wP, A.mult)
+            lin(P("cw"), P("c2"), 1.0, -1.0)
+            tt(P("bw"), P("cw"), wP, A.mult)
+        tau, prev = P("stL", 24 * t, 24 * t + 12), P("stL", 24 * t + 12, 24 * t + 24)
+        tau_, prev_ = P("stL", 24 * t + 24, 24 * t + 36), P("stL", 24 * t + 36, 24 * t + 48)
+        fo, fo_ = P("foL", 12 * t, 12 * t + 12), P("foL", 12 * t + 12, 12 * t + 24)
+        recv("L", t, host, wo)
+        lin(Lx(2), wo, -1.0, 1.0)
+        cp(P("cI"), P("pS", 472, 484))
+        ts(P("lo"), P("cI"), 255, A.bitwise_and)
+        ts(P("hi"), P("cI"), 8, A.logical_shift_right)
+        ts(Lx(0), P("lo"), 0.5, A.is_lt)
+        tt(Lx(1), Lx(0), fo, A.mult)
+        tt(fo_, Lx(1), P("lo"), A.add)
+        lin(Lx(3), fo, 1.0, -1.0)
+        tt(Lx(11), Lx(3), Lx(2), A.mult)
+        tt(Lx(12), Lx(11), Lx(0), A.mult)
+        tt(Lx(13), Lx(12), P("hi"), A.add)
+        tt(Lx(4), tau, prev, A.subtract)
+        tt(Lx(14), Lx(4), wo, A.mult)
+        tt(prev_, Lx(14), prev, A.add)
+        recv("D", t, host, R("gotr"))
+        mm(P("pK2", 0, NB), P("blkH"), R("gotr"), False, True)
+        o1_ = P("o1", b0 + NB, b1 + NB)
+        if not fin:
+            for a, b in HALVES:
+                tt(P("pD1", NB + a, NB + b), P("Jw", a, b), P("pK2", a, b), A.mult)
+                tt(P("q", a, b), P("pD1", NB + a, NB + b), P("bw", a, b), A.add)
+                ts(P("sh", a, b), P("q", a, b), 5, A.logical_shift_right, W - 1, A.bitwise_and)
+                ts(P("offH", a, b), P("sh", a, b), 77.0 * (t + 1), A.add)
+        recv("E", t, host, R("nbtr"))
+        rl(P("pS", 484, 496), "nbtr", b0)
+        tt(Lx(5), Lx(0), P("pS", 484, 496), A.mult)
+        tt(tau_, Lx(5), Lx(13), A.add)
+        if not fin:
+            send("A", t + 1, nhost, P("stR", 24 * t + 24, 24 * t + 48), P("stL", 24 * t + 24, 24 * t + 48))
+        tt(x0, P("jk"), P("pK2", 0, NB), A.mult)
+        tt(o1_, x0, P("c2"), A.add)
+    tN = 24 * RO
+    cp(P("stO", 0, 24), P("stL", tN, tN + 24), "va")
+    lin(P("stO", 24, 36), P("foL", 12 * RO, 12 * RO + 12), 1.0, -1.0)
+    for f, (pn, c0) in enumerate((("pD0", 0), ("pD0", NB), ("pD1", 0))):
+        mms([(P(pn, c0 + i, c0 + NB, 16, 8), P("CLT", 128 * i, 128 * i + 128, 16), P("stO", 12 * f, 12 * f + 12), True, True, 12) for i in range(16)])
+    lin(P("oj"), P("o1", NB * RO, NB * RO + NB), 1.0, -1.0)
+    dma("y", T.yo[:, :], T.oj[:, :], "st0", [P("oj")])
+    cp(P("nw"), P("uI"))
+    dma("y", T.yu[:, :], T.nw[0:128:16, :], "st1", [P("nw")])
+    cp(P("o8", 0, 2 * NB, 1, 8), P("pD0", 0, 2 * NB, 1, 8), "va")
+    cp(P("o8", 2 * NB, 3 * NB, 1, 8), P("pD1", 0, NB, 1, 8), "va")
+    dma("y", T.yt[:, :], T.o8[0:8, 0:NB], "st2", [P("o8", 0, NB)])
+    dma("y", T.yp[:, :], T.o8[0:8, NB:2 * NB], "st3", [P("o8", NB, 2 * NB)])
+    dma("y", T.yf[:, :], T.o8[0:8, 2 * NB:3 * NB], "st4", [P("o8", 2 * NB, 3 * NB)])
+
+    count, known, clocks, hist = {}, {q: {} for q in queues}, {}, {}
+    left = 0
+
+    def need(q, reads, writes):
+        want = {}
+        for lst, wr in ((reads, False), (writes, True)):
+            for r in lst:
+                ps = r[1] in PS
+                for (a0, a1, w, oq, point) in hist.get(r[1], ()):
+                    over = a0 < r[3] and r[2] < a1
+                    if (over and (wr or w) and not (ps and q == "p" and oq == "p")) or (ps and oq != q):
+                        want[point[0]] = max(want.get(point[0], 0), point[1])
+        kn = known[q]
+        for s in sorted(want, key=lambda z: -want[z]):
+            if kn.get(s, 0) < want[s]:
+                queues[q].wait_ge(T.sem[s], want[s])
+                for s2, n2 in clocks.get((s, want[s]), {}).items():
+                    kn[s2] = max(kn.get(s2, 0), n2)
+                kn[s] = want[s]
+
+    def note(q, reads, writes, point, clock):
+        clocks[point] = clock
+        for lst, wr in ((reads, False), (writes, True)):
+            for r in lst:
+                h = hist.setdefault(r[1], [])
+                if r[1] in PS:
+                    h[:] = [z for z in h if not (z[3] == q and z[2] == wr and r[2] <= z[0] and z[1] <= r[3])]
+                elif wr:
+                    h[:] = [z for z in h if not (r[2] <= z[0] and z[1] <= r[3])]
+                h.append((r[2], r[3], wr, q, point))
+
+    for _, i, q in order(ops):
+        o = ops[i]
+        rd, wr = o["reads"], o["writes"]
+        if o["kind"] == "recv":
+            msg, t, src, buf = o["args"]
+            note("r", rd, wr, ("m%s%d" % (msg, t), len(topo.engines(src, core)[:8])), {})
+            continue
+        need(q, rd, wr)
+        if o["kind"] == "send":
+            msg, t, dst, out, in_ = o["args"]
+            rid, pid = topo.addr(dst, core)
+            eng = topo.engines(core, dst)[:8]
+            g.remote_dma(out[0], in_[0], T.sem["m%s%d" % (msg, t)], T.sem.left, pid, rid, sum(1 << e for e in eng))
+            left += len(eng)
+        elif o["kind"] == "dma":
+            o["fns"][q][0]().then_inc(T.sem[o["sem"]], 16)
+            note(q, rd, wr, (o["sem"], 16), dict(known[q]))
+        else:
+            for f in o["fns"][q]:
+                f().then_inc(T.sem[q], 1)
+            count[q] = count.get(q, 0) + len(o["fns"][q])
+            note(q, rd, wr, (q, count[q]), dict(known[q]))
+    for i in range(5):
+        g.sync.wait_ge(T.sem["st%d" % i], 16)
+    for i in range(9):
+        if known["v"].get("ld%d" % i, 0) < 16:
+            g.vector.wait_ge(T.sem["ld%d" % i], 16)
+    for s in ("v", "a", "p", "k"):
+        g.wait_ge(T.sem[s], count[s])
+    g.wait_ge(T.sem.left, left)

@@ -1,132 +1,113 @@
-from concourse.mybir import AluOpType as A, AxisListType, ActivationFunctionType as F
+from concourse.mybir import AluOpType as A, ActivationFunctionType as F
 
 NB, W, RO, N = 192, 4096, 5, 4
 WX = 4416
 S3 = 16 * NB
 H = NB // 2
+DM = 592
+ST = 88
+AM = 72
+NONE = -4096.0
 
 SCRATCH = {
     "hx": ("sbuf", [128, WX], "bfloat16"), "ownI": ("sbuf", [128, NB], "int32"), "nbI": ("sbuf", [128, NB], "int32"),
-    "in4": ("sbuf", [8, 4 * NB], "int32"), "wtI": ("sbuf", [128, 1], "int32"),
-    "in4h": ("sbuf", [8, 3 * NB], "bfloat16"), "tash": ("sbuf", [8, NB], "float16"), "sel8": ("sbuf", [8, 128], "float16"),
-    "nbb": ("sbuf", [128, NB], "bfloat16"),
+    "in4": ("sbuf", [8, 4 * NB], "int32"), "wtI": ("sbuf", [128, 1], "int32"), "in4h": ("sbuf", [8, 4 * NB], "float16"),
+    "x48": ("sbuf", [48, 128], "float16"), "nbb": ("sbuf", [128, NB], "bfloat16"),
     "pI": ("sbuf", [128, 4], "int32"), "pF": ("sbuf", [128, 8], "float32"), "cg": ("sbuf", [128, 128], "float32"),
-    "dif": ("sbuf", [128, 128], "float32"), "xb": ("sbuf", [12, 128], "bfloat16"), "xf": ("sbuf", [12, 128], "float32"),
-    "iB": ("sbuf", [128, 2048], "bfloat16"), "g8": ("sbuf", [128, 8], "bfloat16"), "idF": ("sbuf", [12, 12], "float32"),
-    "CLT": ("sbuf", [128, 2048], "bfloat16"), "CLP": ("sbuf", [128, 2048], "bfloat16"),
-    "blk": ("sbuf", [128, 128], "bfloat16"), "blkH": ("sbuf", [128, 128], "float16"), "blkG": ("sbuf", [128, 128], "bfloat16"),
-    "c128": ("sbuf", [128, NB], "bfloat16"),
-    "one": ("sbuf", [128, 128], "float32"), "wtb": ("sbuf", [128, 128], "bfloat16"), "idb": ("sbuf", [128, 128], "bfloat16"),
-    "nid": ("sbuf", [128, 128], "bfloat16"), "cbE": ("sbuf", [128, NB], "bfloat16"),
-    "m8": ("sbuf", [128, 16], "bfloat16"), "onM": ("sbuf", [128, 96], "bfloat16"),
-    "brow": ("sbuf", [128, 512], "bfloat16"), "mk32": ("sbuf", [128, 512], "float32"), "m16": ("sbuf", [128, S3 // 4], "bfloat16"),
-    "hf": ("sbuf", [128, NB], "float32"), "zr": ("sbuf", [128, NB], "float32"),
-    "w2": ("sbuf", [128, NB], "float32"), "w25": ("sbuf", [128, NB], "float32"), "w2b": ("sbuf", [128, NB], "bfloat16"),
-    "wL": ("sbuf", [128, 12], "float32"), "cL": ("sbuf", [128, 12], "float32"),
-    "o1": ("sbuf", [128, 6 * NB], "float32"), "w": ("sbuf", [128, 6 * NB], "float32"), "wr": ("sbuf", [128, 5 * NB], "float32"),
-    "stL": ("sbuf", [128, 6 * 24], "float32"), "stR": ("sbuf", [128, 5 * 24], "float32"), "foL": ("sbuf", [128, 6 * 12], "float32"),
+    "dif": ("sbuf", [128, 128], "float32"), "ia": ("sbuf", [128, 128], "float32"), "ib": ("sbuf", [128, 128], "float32"),
+    "i32": ("sbuf", [128, 32], "float32"), "g16": ("sbuf", [128, 16], "float32"), "lane": ("sbuf", [128, NB], "float32"),
+    "idb": ("sbuf", [128, 128], "bfloat16"), "idh": ("sbuf", [128, 128], "float16"), "blk": ("sbuf", [128, 128], "bfloat16"),
+    "blkH": ("sbuf", [128, 128], "float16"), "g8h": ("sbuf", [128, 8], "float16"), "g8s": ("sbuf", [128, 8], "float16"),
+    "g32": ("sbuf", [128, 8], "bfloat16"), "g01": ("sbuf", [128, 16], "bfloat16"), "TRI": ("sbuf", [128, 128], "bfloat16"),
+    "CLT": ("sbuf", [128, 2048], "float16"), "CLP": ("sbuf", [128, 2048], "float16"), "RL": ("sbuf", [128, 2048], "float16"),
+    "KL": ("sbuf", [128, 2048], "bfloat16"), "WL": ("sbuf", [128, 2048], "bfloat16"), "SEL": ("sbuf", [8, 2048], "bfloat16"),
+    "SE0": ("sbuf", [8, 2048], "float16"),
+    "cbE": ("sbuf", [128, NB], "bfloat16"), "cst": ("sbuf", [128, 5 * NB], "bfloat16"), "kH": ("sbuf", [128, NB], "bfloat16"),
+    "kA": ("sbuf", [128, NB], "bfloat16"), "mH": ("sbuf", [128, NB], "float32"), "mA": ("sbuf", [128, NB], "float32"),
+    "m16": ("sbuf", [128, S3 // 4], "bfloat16"), "Ej": ("sbuf", [128, 16], "bfloat16"), "Eg": ("sbuf", [128, 32], "bfloat16"),
+    "cL": ("sbuf", [128, 12], "float32"), "half": ("sbuf", [8, 128], "float32"),
+    "dm": ("sbuf", [128, 6 * DM], "float16"), "st": ("sbuf", [128, 6 * ST], "float16"),
+    "am": ("sbuf", [128, 6 * AM], "float16"), "ar": ("sbuf", [128, 5 * AM], "float16"),
     "Ub": ("sbuf", [128, 5 * NB], "bfloat16"), "Ur": ("sbuf", [128, 5 * NB], "bfloat16"),
     "JO": ("sbuf", [128, 5 * NB], "float16"), "JOr": ("sbuf", [128, 5 * NB], "float16"),
-    "wl": ("sbuf", [128, 5 * 12], "float32"), "wlO": ("sbuf", [128, 5 * 12], "float32"),
-    "wn": ("sbuf", [128, 5 * NB], "bfloat16"), "wnO": ("sbuf", [128, 5 * NB], "bfloat16"),
     "got": ("sbuf", [128, 5 * NB], "float16"), "gotr": ("sbuf", [128, 5 * NB], "float16"),
-    "nbt": ("sbuf", [128, 5 * NB], "bfloat16"), "nbtr": ("sbuf", [128, 5 * NB], "bfloat16"),
+    "nbt": ("sbuf", [128, 5 * NB], "float16"), "nbtr": ("sbuf", [128, 5 * NB], "float16"), "nbtn": ("sbuf", [128, 5 * NB], "float16"),
+    "Cw": ("sbuf", [128, 6 * NB], "bfloat16"),
+    "o": ("sbuf", [128, NB], "float32"), "d0": ("sbuf", [128, 3 * NB], "bfloat16"),
     "q": ("sbuf", [128, NB], "int32"), "sh": ("sbuf", [128, NB], "int32"), "offH": ("sbuf", [128, NB], "uint16"),
     "q2": ("sbuf", [128, NB], "int32"), "sh2": ("sbuf", [128, NB], "int32"), "offA": ("sbuf", [128, NB], "uint16"),
-    "x": ("sbuf", [128, S3], "bfloat16"), "s": ("sbuf", [128, S3], "bfloat16"),
-    "e": ("sbuf", [128, S3], "bfloat16"), "y": ("sbuf", [128, S3], "bfloat16"), "z": ("sbuf", [128, S3], "bfloat16"),
-    "sc": ("sbuf", [128, 512], "float32"), "sc2": ("sbuf", [128, 512], "float32"),
-    "OT": ("sbuf", [128, 512], "bfloat16"), "OT2": ("sbuf", [128, 512], "bfloat16"),
-    "tl": ("sbuf", [128, 12], "uint16"), "oVm": ("sbuf", [128, NB], "float32"), "oV": ("sbuf", [128, NB], "float32"),
-    "o0": ("sbuf", [128, NB], "float32"), "om": ("sbuf", [128, NB], "float32"),
-    "nbV": ("sbuf", [128, NB], "bfloat16"), "UV": ("sbuf", [128, NB], "bfloat16"), "stb": ("sbuf", [128, 24], "bfloat16"),
-    "tR": ("sbuf", [128, NB], "bfloat16"), "FB": ("sbuf", [128, NB], "bfloat16"),
-    "G": ("sbuf", [128, 12 * NB], "bfloat16"), "LT": ("sbuf", [128, 12 * 128], "bfloat16"),
-    "cmp": ("sbuf", [128, NB], "bfloat16"), "okw": ("sbuf", [128, 12], "float32"), "thr": ("sbuf", [128, NB], "float32"),
-    "cnt": ("sbuf", [128, 1], "float32"), "offV": ("sbuf", [128, 12], "uint16"), "Vo": ("sbuf", [128, NB], "float32"),
-    "nbw": ("sbuf", [128, NB], "float32"), "V3": ("sbuf", [128, NB], "bfloat16"),
-    "Cw": ("sbuf", [128, 2 * NB], "bfloat16"), "Xw": ("sbuf", [128, 2 * NB], "float32"),
-    "nj": ("sbuf", [128, NB], "float32"), "XS": ("sbuf", [128, NB], "float32"),
-    "uA": ("sbuf", [128, NB], "int32"), "uI": ("sbuf", [128, NB], "int32"),
-    "jw": ("sbuf", [128, NB], "float32"), "nw": ("sbuf", [128, NB], "float32"), "oj": ("sbuf", [128, NB], "float32"),
-    "c2": ("sbuf", [128, NB], "float32"), "jk": ("sbuf", [128, NB], "float32"), "Jw": ("sbuf", [128, NB], "float32"),
-    "bw": ("sbuf", [128, NB], "float32"), "cw": ("sbuf", [128, NB], "float32"),
-    "cI": ("sbuf", [128, 12], "int32"), "lo": ("sbuf", [128, 12], "int32"), "hi": ("sbuf", [128, 12], "int32"),
-    "Lt": ("sbuf", [128, 12 * 16], "float32"), "stO": ("sbuf", [128, 36], "bfloat16"), "o8": ("sbuf", [8, 3 * NB], "float32"),
-    "pD0": ("psum", [128, 512], "float32"), "pD1": ("psum", [128, 512], "float32"),
-    "pK": ("psum", [128, 512], "float32"), "pK2": ("psum", [128, 512], "float32"), "pK3": ("psum", [128, 512], "float32"),
-    "pU": ("psum", [128, 512], "float32"), "pS": ("psum", [128, 512], "float32"), "pR": ("psum", [128, 512], "float32"),
+    "x": ("sbuf", [128, S3], "bfloat16"), "s": ("sbuf", [128, S3], "bfloat16"), "y": ("sbuf", [128, S3], "bfloat16"),
+    "e": ("sbuf", [128, 12, 256], "bfloat16"), "z": ("sbuf", [128, 12, 256], "bfloat16"),
+    "sc": ("sbuf", [128, NB], "float32"), "sc2": ("sbuf", [128, NB], "float32"),
+    "jI": ("sbuf", [128, 24], "int32"), "gI": ("sbuf", [128, 24], "int32"), "uI": ("sbuf", [128, 24], "int32"),
+    "jl": ("sbuf", [128, 12], "uint16"), "gl": ("sbuf", [128, 12], "uint16"), "tl": ("sbuf", [128, 12], "uint16"),
+    "offV": ("sbuf", [128, 12], "uint16"), "thl": ("sbuf", [128, 12], "uint16"), "ovf": ("sbuf", [128, 12], "float32"),
+    "OJ": ("sbuf", [128, NB], "bfloat16"), "OG": ("sbuf", [128, NB], "bfloat16"),
+    "oV": ("sbuf", [128, NB], "float32"), "nbV": ("sbuf", [128, NB], "bfloat16"),
+    "tR": ("sbuf", [128, NB], "bfloat16"), "FB": ("sbuf", [128, NB], "bfloat16"), "G": ("sbuf", [128, 12 * NB], "bfloat16"),
+    "cmp": ("sbuf", [128, NB], "float16"), "sg": ("sbuf", [8, NB], "bfloat16"), "acc": ("sbuf", [8, 1], "float32"),
+    "xb": ("sbuf", [12, 256], "bfloat16"), "XS": ("sbuf", [128, 200], "float32"), "nm": ("sbuf", [128, 12], "float32"),
+    "l0": ("sbuf", [128, 84], "float32"), "g0": ("sbuf", [128, 36], "float32"), "gt": ("sbuf", [128, 36], "float32"),
+    "gth": ("sbuf", [128, 12], "float16"), "o8": ("sbuf", [8, 4 * NB], "float32"),
+    "p0": ("psum", [128, 512], "float32"), "p1": ("psum", [128, 512], "float32"), "p2": ("psum", [128, 512], "float32"),
+    "p3": ("psum", [128, 512], "float32"), "p4": ("psum", [128, 512], "float32"), "p5": ("psum", [128, 512], "float32"),
+    "p6": ("psum", [128, 512], "float32"), "p7": ("psum", [128, 512], "float32"),
 }
-PS = ("pD0", "pD1", "pK", "pK2", "pK3", "pU", "pS", "pR")
+PS = ("p0", "p1", "p2", "p3", "p4", "p5", "p6", "p7")
 TWO = ("bfloat16", "uint16", "float16")
-MSG = ("A", "W", "B", "C", "F", "D", "E", "L")
-SEMAPHORES = ["v", "a", "p", "k", "left"] + ["ld%d" % i for i in range(9)] + ["st%d" % i for i in range(5)] \
+MSG = ("A", "P", "B", "b", "C", "D", "d", "E", "F")
+SEMAPHORES = ["v", "a", "p", "k", "left"] + ["ld%d" % i for i in range(10)] + ["st%d" % i for i in range(5)] \
     + ["m%s%d" % (m, t) for m in MSG for t in range(RO)]
-CHAIN = ("G", "s")
-EV = (0, 1, 2, 3, 4, 5)
-PRI = {"G@0": 4, "s@0": 1, "Lt@0": 2, "xb@0": -2, "pD0@0": 2, "pK@16": -8, "pK2@160": -8, "pK@48": 2, "pK3@16": 8, "Vo@0": -2,
-       "pK2@16": -8, "pK3@128": 4, "pK3@48": -2, "pK3@224": -2, "pK@64": -4, "uA@0": -4, "pK3@96": 8, "pK2@80": -8, "pK@160": 8,
-       "one@0": 8, "pK2@224": -1, "blkH@0": 4, "g8@0": 1, "V3@0": -1, "pS@432": 8, "pS@256": -8, "hf@0": -4, "pR@384": 0.3,
-       "wtb@0": -4, "pK3@32": 8, "pK@0": -1, "pK3@64": -4, "pK2@176": -2, "m8@0": -2, "nj@0": 0.3, "pS@272": -4, "OT@0": -1,
-       "Lt@84": -2, "okw@0": 0.3}
-ENG = {"LT@0": 3, "oV@0": -1, "stb@0": -1, "pU@192": -0.3, "wn@0": 1, "x@0": 0.3, "o0@0": -0.3}
-CYC, LATE, FLY, SPARE, SPARE2, AHEAD, VF = 0.001, 0.08, 2.2, 1.5, 3.0, 0.07, 0.01
+PAR = {"CYC": 0.001, "PE": 0.0006, "LATE": 0.08, "FLY": 2.2, "VF": 0.01, "HUE": 7.0, "BIAS": 1.0, "PASSES": 6, "NG": 4, "BH": 2,
+       "DH": 2, "K2": "p2"}
+PLAN = []
+
+
+def place(ops, before, rank, back):
+    n = len(ops)
+    start, end, queue, busy, late = [0.0] * n, [0.0] * n, [None] * n, {}, PAR["LATE"]
+    for i in sorted(range(n), key=lambda i: rank[i]):
+        o, best = ops[i], None
+        r = max([end[j] + ops[i if back else j]["late"] for j in before[i]] + [ops[i]["late"] if back else 0.0])
+        for q, c in o["alt"]:
+            held = [z[:2] for z in busy.get(q, ()) if z[1] > r]
+            for b in o["banks"]:
+                held += [(a - late, e + late) for a, e, q2 in busy.get(b, ()) if q2 != q and e + late > r]
+            t0 = r
+            for a, e in sorted(held):
+                if a >= t0 + c:
+                    break
+                t0 = max(t0, e)
+            z = t0 + c + (PAR["BIAS"] * c if q == "v" else 0.0)
+            if best is None or z < best[0]:
+                best = (z, t0, c, q)
+        _, start[i], c, queue[i] = best
+        end[i] = start[i] + c
+        for b in [queue[i]] + o["banks"]:
+            busy.setdefault(b, []).append((start[i], end[i], queue[i]))
+    return start, end, queue
 
 
 def order(ops):
     n = len(ops)
+    pred = [sorted(o["deps"]) for o in ops]
     succ = [[] for _ in ops]
-    miss = [0] * n
-    for i, o in enumerate(ops):
-        for d in o["deps"]:
+    for i in range(n):
+        for d in pred[i]:
             succ[d].append(i)
-            miss[i] += 1
-    tail, name = [0.0] * n, []
+    tail = [0.0] * n
     for i in range(n - 1, -1, -1):
-        tail[i] = min(c[1] for c in ops[i]["alt"]) + ops[i]["late"] + max([tail[j] for j in succ[i]] + [0.0])
-    for i, o in enumerate(ops):
-        r = (o["writes"] or o["reads"])[0]
-        name.append("%s@%d" % (r[1], r[2] if r[1] in PS or r[1] == "Lt" else 0))
-        tail[i] += PRI.get(name[i], 0.0)
-    ready = {i: 0.0 for i in range(n) if not miss[i]}
-    free, bank, out, done = {}, {}, [], {}
-    while ready:
-        can = {}
-        top = max(max(r, min(free.get(q, 0.0) for q, _ in ops[i]["alt"])) + tail[i] for i, r in ready.items())
-        for i, r in ready.items():
-            o, mine = ops[i], None
-            for q, c in o["alt"]:
-                t0 = max(r, free.get(q, 0.0))
-                for b in o["banks"]:
-                    for q2, e in bank.get(b, {}).items():
-                        if q2 != q:
-                            t0 = max(t0, e + LATE)
-                z = t0 + c
-                if q == "v" and len(o["alt"]) > 1:
-                    z += ENG.get(name[i], 0.0) + min(SPARE, SPARE2 * max(0.0, top - t0 - tail[i]))
-                if mine is None or z < mine[0]:
-                    mine = (z, t0, t0 + c, i, q)
-            can.setdefault(mine[4], []).append(mine)
-        best = None
-        for q, lst in can.items():
-            m = min(z[1] for z in lst) + AHEAD
-            z = max((z for z in lst if z[1] <= m), key=lambda z: tail[z[3]])
-            if best is None or z[1] < best[1]:
-                best = z
-        _, t0, fin, i, q = best
-        del ready[i]
-        o = ops[i]
-        free[q] = fin
-        for b in o["banks"]:
-            bank.setdefault(b, {})[q] = fin
-        done[i] = fin + o["late"]
-        out.append((t0, i, q))
-        for j in succ[i]:
-            miss[j] -= 1
-            if not miss[j]:
-                ready[j] = max(done[d] for d in ops[j]["deps"])
-    out.sort(key=lambda z: (z[0], z[1]))
-    return out
+        tail[i] = min(c for _, c in ops[i]["alt"]) + ops[i]["late"] + max([tail[j] for j in succ[i]] + [0.0])
+    rank, best = [(-tail[i], i) for i in range(n)], None
+    for _ in range(PAR["PASSES"]):
+        start, end, queue = place(ops, pred, rank, False)
+        span = max(end[i] + ops[i]["late"] for i in range(n))
+        if best is None or span < best[0]:
+            best = (span, start, queue)
+        _, end, _ = place(ops, succ, [(-end[i], -i) for i in range(n)], True)
+        rank = [(-end[i], i) for i in range(n)]
+    PAR["SPAN"] = best[0]
+    return sorted((best[1][i], i, best[2][i]) for i in range(n))
 
 
 def rank_program(g, core, T, topo):
@@ -134,13 +115,17 @@ def rank_program(g, core, T, topo):
     if rank is None:
         return
     queues = {"v": g.vector, "a": g.scalar, "p": g.tensor, "k": g, "y": g.sync}
-    ops, last, chain, sent = [], {}, {}, {}
+    ops, last, sent, group = [], {}, {}, {}
+    CYC, VF = PAR["CYC"], PAR["VF"]
 
     def P(name, c0=0, c1=None, step=1, p=128):
         b = T[name]
         c1 = b.shape[1] if c1 is None else c1
         p = min(p, b.shape[0])
-        return (b[0:p, c0:c1:step] if step > 1 else b[0:p, c0:c1], name, c0, c1, (c1 - c0 + step - 1) // step)
+        return (b[0:p, c0:c1:step] if step > 1 else b[0:p, c0:c1], name, c0, c1, (c1 - c0 + step - 1) // step, step)
+
+    def P3(name, c0, c1, a, b, step=1):
+        return (T[name][:, c0:c1, a:b:step], name, 256 * c0 + a, 256 * c1, (c1 - c0) * ((b - a + step - 1) // step), step)
 
     def IND(win, off):
         return (win[0].indirect(off[0]), win, off)
@@ -151,38 +136,38 @@ def rank_program(g, core, T, topo):
             out += [x[1], x[2]] if len(x) == 3 else [x]
         return out
 
-    def put(kind, alt, reads, writes, late=None, **more):
+    meet = lambda a, b: a[2] < b[3] and b[2] < a[3] and (a[5] != b[5] or (a[2] - b[2]) % a[5] == 0)
+    cover = lambda a, b: a[2] <= b[2] and b[3] <= a[3] and (a[5] == 1 or (a[5] == b[5] and (a[2] - b[2]) % a[5] == 0))
+
+    def put(kind, alt, reads, writes, late=None, loose=(), **more):
         reads, writes = flat(reads), flat(writes)
         i, deps = len(ops), set()
         for lst, wr in ((reads, False), (writes, True)):
             for r in lst:
-                for (a0, a1, w, j) in last.get(r[1], ()):
-                    if (wr or w) and a0 < r[3] and r[2] < a1:
+                for (z, w, j) in last.get(r[1], ()):
+                    if (wr or w) and meet(r, z) and j not in loose:
                         deps.add(j)
         for lst, wr in ((reads, False), (writes, True)):
             for r in lst:
                 h = last.setdefault(r[1], [])
-                if wr:
-                    h[:] = [z for z in h if not (r[2] <= z[0] and z[1] <= r[3])]
-                h.append((r[2], r[3], wr, i))
-        if writes and writes[0][1] in CHAIN:
-            if writes[0][1] in chain:
-                deps.add(chain[writes[0][1]])
-            chain[writes[0][1]] = i
+                if wr and not loose:
+                    h[:] = [z for z in h if not cover(r, z[0])]
+                h.append((r, wr, i))
         deps.discard(i)
         banks = sorted(set(r[1] for r in reads + writes if r[1] in PS))
         o = {"kind": kind, "alt": [(q, c) for q, c, _ in alt], "fns": {q: f for q, _, f in alt}, "reads": reads, "writes": writes,
-             "deps": deps, "banks": banks, "late": LATE if late is None else late}
+             "deps": deps, "banks": banks, "late": PAR["LATE"] if late is None else late}
         o.update(more)
         ops.append(o)
         return i
 
     V, Sc, Te = g.vector, g.scalar, g.tensor
     dts = lambda x: SCRATCH[(x[1] if len(x) == 3 else x)[1]][2]
-    two = lambda xs: all(dts(x) in TWO and (len(x) == 3 or x[1] not in PS) for x in xs)
+    two = lambda xs: all(dts(x) in TWO for x in xs)
     vc = lambda n, cyc=1.0: (0.05 if cyc in (1.5, 3.5) else VF) + max(64, n * cyc) * CYC
     ac = lambda n, cyc=1.0: (0.065 if cyc == 1.5 else VF) + max(64, n * cyc) * CYC
     size = lambda x: 16 * (x[2][3] - x[2][2]) if len(x) == 3 else x[4]
+    col = lambda s: s[0] if isinstance(s, tuple) else s
 
     def cp(out, in_, qs="v"):
         alt = []
@@ -194,35 +179,25 @@ def rank_program(g, core, T, topo):
             alt.append(("a", ac(n, 1.5 if gat else 1.0), [lambda: Sc.activation(out[0], in_[0], F.Copy)]))
         put("op", alt, [in_], [out])
 
-    def act(out, in_, func, bias=0.0):
-        put("op", [("a", ac(size(out)), [lambda: Sc.activation(out[0], in_[0], func, bias=bias)])], [in_], [out])
-
-    def lin(out, in_, m, b):
-        put("op", [("v", vc(size(out), 0.5 if two([out, in_]) else 1.0), [lambda: V.tensor_scalar(out[0], in_[0], m, b, A.mult, A.add)]),
-                   ("a", ac(size(out)), [lambda: Sc.activation(out[0], in_[0], F.Identity, bias=b, scale=m)])], [in_], [out])
-
-    def lin1(out, in_):
-        put("op", [("v", vc(size(out)), [lambda: V.tensor_scalar(out[0], in_[0], 0.5, None, A.is_lt)]),
-                   ("a", ac(size(out)), [lambda: Sc.activation(out[0], in_[0], F.Relu, bias=1.0, scale=-1.0)])], [in_], [out])
+    def lin(out, in_, m, b, qs="va"):
+        alt = [("v", vc(size(out), 0.5 if two([out, in_]) else 1.0), [lambda: V.tensor_scalar(out[0], in_[0], col(m), b, A.mult, A.add)]),
+               ("a", ac(size(out)), [lambda: Sc.activation(out[0], in_[0], F.Identity, bias=b, scale=col(m))])]
+        put("op", [z for z in alt if z[0] in qs], [in_] + ([m] if isinstance(m, tuple) else []), [out])
 
     def tt(out, a, b, o):
-        ps = a[1] in PS or b[1] in PS
-        put("op", [("v", vc(size(out), 1.0 if ps else 2.0), [lambda: V.tensor_tensor(out[0], a[0], b[0], o)])], [a, b], [out])
+        c = 1.5 if len(a) == 3 else 1.0 if a[1] in PS or b[1] in PS else 2.0
+        put("op", [("v", vc(size(out), c), [lambda: V.tensor_tensor(out[0], a[0], b[0], o)])], [a, b], [out])
 
     def ts(out, a, s1, o1, s2=None, o2=None):
-        rs = [a]
-        x1, x2 = s1, s2
-        if isinstance(s1, tuple):
-            rs.append(s1)
-            x1 = s1[0]
+        rs = [a] + [s for s in (s1, s2) if isinstance(s, tuple)]
         if o2 is None:
-            f = lambda: V.tensor_scalar(out[0], a[0], x1, None, o1)
+            f = lambda: V.tensor_scalar(out[0], a[0], col(s1), None, o1)
         else:
-            f = lambda: V.tensor_scalar(out[0], a[0], x1, x2, o1, o2)
+            f = lambda: V.tensor_scalar(out[0], a[0], col(s1), col(s2), o1, o2)
         put("op", [("v", vc(size(out), 0.5 if two([out, a]) else 1.0), [f])], rs, [out])
 
     def ms(out, c):
-        put("op", [("v", vc(size(out)), [lambda: V.memset(out[0], c)])], [], [out])
+        put("op", [("v", vc(size(out), 0.5 if two([out]) else 1.0), [lambda: V.memset(out[0], c)])], [], [out])
 
     def scan(out, d0, d1, init, o0, o1):
         put("op", [("v", vc(size(out), 0.5 if two([out, d0, d1]) else 1.0),
@@ -232,18 +207,30 @@ def rank_program(g, core, T, topo):
         n[0] -= 1
         return n[0] == 0
 
-    def mms(lst, reads=()):
-        c = sum((0.01 + max(min(64, l[4]), n) / 1300.0) * (4 if dts(r) == "float32" else 1) for _, l, r, _, _, n in lst)
-        fns = [lambda z=z: Te.matmul(z[0][0], z[1][0], z[2][0], z[3], z[4] if isinstance(z[4], bool) else closes(z[4])) for z in lst]
+    def mms(lst, first=True, left=None):
+        c = sum((0.005 + max(min(64, z[1][4]), z[2][4]) * PAR["PE"]) * (4 if dts(z[2]) == "float32" else 1) for z in lst)
+        fns = []
+        for j, z in enumerate(lst):
+            if left is None:
+                fns.append(lambda z=z: Te.matmul(z[0][0], z[1][0], z[2][0], *(z[3:] or (True, True))))
+            else:
+                fns.append(lambda z=z, j=j: Te.matmul(z[0][0], z[1][0], z[2][0], first and j == 0, closes(left)))
         rd, wr = {}, {}
-        for o, l, r, _, _, _ in lst:
-            for x, d in ((l, rd), (r, rd), (o, wr)):
-                z = d.get(x[1])
-                d[x[1]] = (None, x[1], min(x[2], z[2]) if z else x[2], max(x[3], z[3]) if z else x[3], 0)
-        put("op", [("p", c, fns)], list(rd.values()) + list(reads), list(wr.values()))
+        for z in lst:
+            for x, d in ((z[1], rd), (z[2], rd), (z[0], wr)):
+                y = d.get(x[1], x)
+                d[x[1]] = x if cover(x, y) else (None, x[1], min(x[2], y[2]), max(x[3], y[3]), 0, 1)
+        bank = lst[0][0][1]
+        mark = [(None, "group", 0, 1, 0, 1)] if bank == "p5" else []
+        if first:
+            i = put("op", [("p", c, fns)], list(rd.values()), list(wr.values()) + mark)
+            group[bank] = []
+        else:
+            i = put("op", [("p", c, fns)], list(rd.values()) + mark, list(wr.values()), loose=group[bank])
+            group[bank].append(i)
 
-    def mm(out, l, r, start=True, stop=True, reads=()):
-        mms([(out, l, r, start, stop, r[4])], reads)
+    def acc(lst):
+        mms([z + (j == 0, j == len(lst) - 1) for j, z in enumerate(lst)])
 
     def iota(out, pattern, base, cmul, flag=True):
         if flag:
@@ -256,292 +243,271 @@ def rank_program(g, core, T, topo):
         put("dma", [(q, 0.1, [lambda: queues[q].dma_start(out, in_)])], list(reads), list(writes), late, sem=sem)
 
     def send(msg, t, dst, out, in_):
-        sent[(msg, t)] = put("send", [("k", 0.6, None)], [in_], [], FLY + 0.0015 * in_[4] * (2 if dts(in_) in TWO else 4),
+        sent[(msg, t)] = put("send", [("k", 0.6, None)], [in_], [], PAR["FLY"] + 0.0015 * in_[4] * (2 if dts(in_) in TWO else 4),
                              args=(msg, t, dst, out, in_))
 
     def recv(msg, t, src, buf):
-        i = put("recv", [("r%s%d" % (msg, t), 0.0, None)], [], [buf], 0.0, args=(msg, t, src, buf))
+        i = put("recv", [("r%s%d" % (msg, t), 0.001, None)], [], [buf], 0.0, args=(msg, t, src, buf))
         ops[i]["deps"].add(sent[(msg, t)])
 
-    def rl(out, src, c0=0, p=128, wide=False):
-        k, sel = (8, P("idb", 0, 8, 1, 8)) if p == 8 else (128, P("g8"))
-        mms([(P("pR", 384 + i, 512, 16, 12), P(src, c0 + i, c0 + NB, 16, k), sel, True, True, 8) for i in range(16)])
-        xt, turn = (P("xf"), P("idF")) if wide else (P("xb"), P("idb", 0, 12, 1, 12))
-        cp(xt, P("pR", 384, 512, 1, 12), "va")
-        mms([(out, xt, turn, True, True, 12)])
+    blk_ = lambda m, i, p=128: P(m, 128 * i, 128 * i + 128, 1, p)
+    to_list = lambda out, m, src, c0, p=128: [(out, blk_(m, i, p), P(src, c0 + i, c0 + NB, 16, p)) for i in range(16)]
+    to_rows = lambda pn, c0, c1, m, lst: [(P(pn, c0 + i, c1, 16), blk_(m, i), lst) for i in range(16)]
+    const = lambda out, j: (out, P("blk"), P("cst", NB * j, NB * j + out[4]))
+    CONST = (3840.0, 64.0, 240.0, -4.0, 15.0 / 512)
+    away = lambda t: 1 + t % (N - 1)
+    at = lambda r: T.cores[r % N]
 
-    dma("y", T.in4[0:8, 3 * NB:4 * NB], T.tas[:, :], "ld1", [], [P("in4", 3 * NB, 4 * NB, 1, 8)])
-    dma("y", T.ownI[:, :], T.own[:, :], "ld2", [], [P("ownI")])
-    dma("y", T.hx[:, 0:W], T.hue[:, :], "ld3", [], [P("hx", 0, W)], 8.0)
-    dma("a", T.in4[0:8, 0:NB], T.tau[:, :], "ld0", [], [P("in4", 0, NB, 1, 8)])
-    dma("a", T.in4[0:8, NB:2 * NB], T.prev[:, :], "ld4", [], [P("in4", NB, 2 * NB, 1, 8)])
-    dma("a", T.in4[0:8, 2 * NB:3 * NB], T.foe[:, :], "ld5", [], [P("in4", 2 * NB, 3 * NB, 1, 8)])
+    for j, (q, src) in enumerate((("a", T.tau), ("a", T.prev), ("a", T.foe), ("y", T.tas))):
+        dma(q, T.in4[0:8, NB * j:NB * j + NB], src[:, :], "ld%d" % j, [], [P("in4", NB * j, NB * j + NB)])
+    dma("y", T.ownI[:, :], T.own[:, :], "ld4", [], [P("ownI")])
+    dma("y", T.hx[:, 0:W], T.hue[:, :], "ld5", [], [P("hx", 0, W)], PAR["HUE"])
     dma("a", T.wtI[:, :], T.wt[:, :], "ld6", [], [P("wtI")])
     dma("a", T.nbI[:, :], T.nb[:, :], "ld7", [], [P("nbI")])
     dma("y", T.hx[:, W:WX], T.hue[:, 0:WX - W], "ld8", [], [P("hx", W, WX)])
 
     PI = lambda j: P("pI", j, j + 1)
-    PF = lambda j, p=128: P("pF", j, j + 1, 1, p)
+    PF = lambda j: P("pF", j, j + 1)
     iota(PI(0), [[0, 1]], 0, 1, False)
-    iota(P("cg"), [[1, 8], [0, 16]], 0, 0)
-    iota(P("iB"), [[1, 16], [16, 8], [0, 16]], 0, 0)
     iota(P("dif"), [[1, 128]], 0, -1)
-    iota(P("thr", 0, 8), [[1, 2], [2, 4]], 0, 0)
-    iota(P("brow"), [[0, 16], [-1000, 2], [-1, 16]], 15, 0)
-    iota(P("w25"), [[1, NB]], 1, 0)
-    iota(P("cL"), [[16, 12]], NB, 0)
-    iota(P("okw", 0, 8), [[1, 8]], 0, 0)
+    iota(P("cg"), [[1, 8], [0, 16]], 0, 0)
+    iota(P("i32"), [[1, 32]], 0, 0)
+    iota(P("ia"), [[0, 16], [1, 8]], 0, 0)
+    iota(P("ib"), [[1, 16], [0, 8]], 0, 0)
+    iota(P("cL"), [[16, 12]], 0, 0)
+    iota(P("lane"), [[1, NB]], 0, 0)
+    iota(P("kH"), [[0, 12], [64, 16]], 0, 0)
+    iota(P("kA"), [[0, 12], [-64, 16]], 980, 0)
     ts(PI(1), PI(0), 4, A.logical_shift_right)
     ts(PI(2), PI(0), 15, A.bitwise_and)
-    for j in range(3):
-        cp(PF(j), PI(j))
-    ts(PF(5), PF(2), 0.0, A.is_equal)
-    ts(P("idb"), P("dif"), 0.0, A.is_equal)
-    ts(P("g8"), P("okw", 0, 8), PF(1), A.is_equal)
-    ts(P("sel8"), P("cg", 0, 128, 1, 8), PF(0, 8), A.is_equal)
-    cp(P("tash"), P("in4", 3 * NB, 4 * NB, 1, 8))
-    mm(P("pS", 0, NB), P("sel8"), P("tash"))
-    lin(P("w", 0, NB), P("pS", 0, NB), 2.0, 33.0)
-    host = T.cores[(rank + 1) % N]
-    send("W", 0, host, P("wr", 0, NB), P("w", 0, NB))
-    tt(P("q"), P("ownI"), P("w", 0, NB), A.mult)
-    ts(P("sh"), P("q"), 5, A.logical_shift_right, W - 1, A.bitwise_and)
-    cp(P("offH"), P("sh"))
-    cp(P("in4h"), P("in4", 0, 3 * NB, 1, 8))
-    for f in range(3):
-        rl(P("pS", 448 + 12 * f, 460 + 12 * f), "in4h", NB * f, 8)
-    cp(P("stL", 0, 24), P("pS", 448, 472), "va")
-    send("A", 0, host, P("stR", 0, 24), P("stL", 0, 24))
-    lin(P("foL", 0, 12), P("pS", 472, 484), 1.0, 1.0)
-    ts(P("blk"), P("cg"), PF(1), A.is_equal)
+    cp(P("pF", 0, 3), P("pI", 0, 3))
+    ts(P("idh"), P("dif"), 0.0, A.is_equal)
+    ts(P("blkH"), P("cg"), PF(1), A.is_equal)
+    ts(P("g16"), P("i32", 0, 16), PF(2), A.is_equal)
+    ms(P("am", 0, AM), 0.0)
+    cp(P("in4h"), P("in4"))
+    mms([(P("p6", i, 128, 16, 48), P("in4h", i, 4 * NB, 16), P("idh", 0, 8, 1, 8)) for i in range(16)])
+    cp(P("x48"), P("p6", 0, 128, 1, 48))
+    mms([(P("p6", 128, 176), P("x48"), P("idh", 0, 48, 1, 48))])
+    FO, PR, TA = [lambda t, a=a, b=b, s=s: P("st", ST * t + a, ST * t + b, s) for a, b, s in ((1, 24, 2), (25, 48, 2), (50, 84, 3))]
+    WW = lambda t: P("am", AM * t + 36, AM * t + 48)
+    lin(WW(0), P("p6", 164, 176), 2.0, -991.0, "v")
+    cp(P("am", 2, 36, 3), P("p6", 128, 140))
+    cp(P("am", 49, 72, 2), P("p6", 140, 152))
+    send("A", 0, at(rank + 1), P("ar", 0, AM), P("am", 0, AM))
+    cp(TA(0), P("p6", 128, 140), "va")
+    cp(PR(0), P("p6", 140, 152), "va")
+    cp(FO(0), P("p6", 152, 164), "va")
+    for i in range(16):
+        ts(blk_("CLT", i), P("blkH"), P("g16", i, i + 1), A.mult)
+    cp(P("blk"), P("blkH"))
+    cp(P("idb"), P("idh"))
+    for j, c in enumerate(CONST):
+        ms(P("cst", NB * j, NB * j + NB), c)
+    cp(P("o"), P("ownI"))
+    lin(P("dm", 2, 3 * NB, 3), P("ownI"), 1.0, -2048.0, "v")
     ms(P("m16"), 1.0)
     ms(P("m16", 0, S3 // 4, 16), 0.0)
-    ts(P("CLT"), P("iB"), PF(0), A.is_equal)
-    ts(P("o1", 0, NB), P("ownI"), 1.0, A.add)
-    ts(P("idF"), P("dif", 0, 12, 1, 12), 0.0, A.is_equal)
-    ts(P("nid"), P("dif"), 0.0, A.is_equal, -1.0, A.mult)
-    cp(PF(6), P("wtI"))
-    ts(P("wtb"), P("blk"), PF(6), A.mult)
-    ts(P("m8", 0, 8), P("thr", 0, 8), PF(1), A.is_equal, -16.0, A.mult)
-    ts(P("m8", 8, 16), P("thr", 0, 8), PF(1), A.is_equal, 16.0, A.mult)
-    cp(P("nbb"), P("nbI"))
-    ms(P("onM"), 1.0 / 128)
-    ms(P("mk32"), 0.0)
-    ms(P("mk32", 0, 512, 32), -1000000.0)
-    ts(P("cbE"), P("w25"), PF(5), A.mult)
-    ms(P("hf"), 0.5)
-    ms(P("zr"), 0.0)
-    scan(P("w2"), P("hf"), P("zr"), 2.0 ** 97, A.mult, A.add)
-    cp(P("w2b"), P("w2"))
-    ts(P("w25"), P("w2"), 2.5, A.mult)
-    rl(P("pS", 484, 496), "w2b")
-    lin(P("wL"), P("pS", 484, 496), 1.0 / 16, 0.0)
-    ts(P("cL"), P("cL"), PF(2), A.add)
+    ts(P("g8h"), P("i32", 0, 8), PF(1), A.is_equal)
+    ts(P("g8s"), P("i32", 0, 8), PF(1), A.is_equal, 1.0 / 16, A.mult)
+    ts(P("g32"), P("i32", 0, 8), PF(1), A.is_equal, 32.0, A.mult)
+    for f in range(2):
+        ts(P("g01", 8 * f, 8 * f + 8), P("i32", 0, 8), PF(1), A.is_equal, P("g16", f, f + 1), A.mult)
+    ms(P("RL"), 0.0)
+    for i in range(16):
+        cp(P("RL", 129 * i, 128 * i + 128, 16), P("g8s"))
+    lin(P("KL"), P("RL"), 16.0 * 16384, 0.0)
+    lin(PF(3), P("wtI"), 16.0, 0.0, "v")
+    lin(P("WL"), P("RL"), PF(3), 0.0)
+    dma("y", T.SE0[0:8, :], T.RL[0:128:16, :], "ld9", [P("RL")], [P("SE0")])
+    lin(P("SEL"), P("SE0"), 4096.0, 0.0)
     ms(P("CLP"), 0.0)
-    ts(P("CLP", 1, 2048, 16), P("CLT", 1, 2048, 16), 256.0, A.mult)
-    cp(P("blkH"), P("blk"))
-    ts(P("blkG"), P("blk"), 128.0, A.mult)
-    ms(P("c128"), 128.0)
-    ms(P("one"), 1.0)
+    cp(P("CLP", 1, 2048, 16), P("CLT", 1, 2048, 16))
+    ts(P("ia"), P("ia"), PF(1), A.is_equal, 32.0, A.mult)
+    ts(P("ib"), P("ib"), PF(2), A.is_gt)
+    tt(P("TRI"), P("ia"), P("ib"), A.mult)
+    ts(P("cbE"), P("lane"), P("g16", 0, 1), A.mult)
+    ts(P("cL"), P("cL"), PF(2), A.add)
+    lin(P("nbb"), P("nbI"), 16.0, 0.0, "v")
+    ms(P("mA"), 1.0)
+    ms(P("mA", 0, NB, 16), 0.0)
+    ms(P("mH"), 0.0)
+    ms(P("mH", 0, NB, 16), 1e9)
+    lin(P("Ej"), P("g16"), 8192.0, NONE, "v")
+    lin(PF(4), PF(2), -2.0, 31.0, "v")
+    ts(P("Eg"), P("i32"), PF(4), A.is_equal, 8192.0, A.mult)
+    ts(P("Eg"), P("Eg"), NONE, A.add)
+    ms(P("half"), 0.5)
+    ms(P("Cw", NB, 6 * NB), NONE)
+    ms(P("XS"), NONE)
+    ms(P("d0", 0, 3 * NB, 3), NONE)
 
-    def key(pk, h, k, lhs, sgn, n):
-        return ((T[pk][0:96, 256 * h + k:256 * h + 256:32], pk, 16 * k, 16 * k + 16, 8), lhs, P("m8", 8 * sgn, 8 * sgn + 8), False, n, 8)
-
-    def onehot(pk, sc, ot, out, half=None):
-        n, d, hs = (512, 0, (0, 1)) if half is None else (256, 256 * half, (half,))
-        scan(P(sc, d, d + n, 1, 96), P("mk32", 0, n, 1, 96), P(pk, 0, n, 1, 96), 0.0, A.add, A.max)
-        tt(P(ot, d, d + n - 16, 1, 96), P(pk, 0, n - 16, 1, 96), P(sc, d + 16, d + n, 1, 96), A.is_equal)
-        mms([(P("pR", out + H * h, out + H * h + H), P(ot, c, c + 128, 1, 96), P("idb", 0, 96, 1, 96), c == 256 * h, c != 256 * h, 96)
-             for h in hs for c in (256 * h, 256 * h + 112)])
-
-    Lx = lambda j: P("Lt", 12 * j, 12 * j + 12)
-    Q4 = S3 // 4
     HALVES = ((0, H), (H, NB))
-    wR, wP, GP = P("pU", NB, 2 * NB), P("pU", 0, NB), P("pR", NB, 2 * NB)
-    x0, x1, x2 = P("pD0", 0, NB), P("pD0", NB, 2 * NB), P("pD1", 0, NB)
-    for t in range(RO):
-        dist = 1 + t % (N - 1)
-        host, guest = T.cores[(rank + dist) % N], T.cores[(rank - dist) % N]
-        nhost = T.cores[(rank + 1 + (t + 1) % (N - 1)) % N]
-        b0, b1 = NB * t, NB * t + NB
-        R = lambda n: P(n, b0, b1)
-        fin = t == RO - 1
-        nK, nK2, nK3 = [32], [16], [16]
-        for pk, n in (("pK", 512), ("pK2", 256), ("pK3", 256)):
-            mms([(P(pk, 0, n, 1, 96), P("onM"), P("brow", 0, n), True, False, n)])
-        for h in range(4):
-            cp(P("x", Q4 * h, Q4 * h + Q4), IND(P("hx"), P("offH", 48 * h, 48 * h + 48)), "va")
-        for h in range(4):
-            scan(P("s", Q4 * h, Q4 * h + Q4), P("m16"), P("x", Q4 * h, Q4 * h + Q4), 0.0, A.mult, A.max)
-        cp(R("Ub"), P("s", 15, S3, 16), "va")
-        send("B", t, host, R("Ur"), R("Ub"))
-        mm(P("pS", 0, NB), P("wtb"), R("Ub"))
-        recv("A", t, guest, P("stR", 24 * t, 24 * t + 24))
-        recv("W", t, guest, R("wr"))
-        sr = P("stR", 24 * t, 24 * t + 12)
-        cp(P("tl"), sr)
-        lin(P("o0"), R("o1"), 1.0, -1.0)
-        lin(P("om"), R("o1"), 1.0, -2048.0)
-        cp(P("oV"), IND(P("o0"), P("tl")), "va")
-        lin(P("oVm"), P("oV"), 1.0, -2047.0)
-        cp(wR, R("wr"), "va")
+    NG = PAR["NG"]
+    Uo, Nc, Ur, FBp = P("p0", 0, NB), P("p0", NB, 2 * NB), P("p1", 0, NB), P("p1", NB, 2 * NB)
+    kH, kA, So = P("p2", 0, NB), P("p3", 0, NB), P("p3", NB, 2 * NB)
+    res, Tp, nj = P("p4", 384, 396), P("p5", 0, NB, 1, 8), P("p5", NB, 2 * NB)
+    Pl, taste, cnt = P("p6", 0, 12), P("p6", 12, 24), P("p6", 24, 25)
+    dl = lambda a, b, s=1: P("p6", 32 + a, 32 + b, s)
+    dg = lambda a, b, s=1: P("p4", 400 + a, 400 + b, s)
+    oVc, nbp = P("p7", 0, NB), P("p7", NB, 2 * NB)
+    id12 = P("idb", 0, 12, 1, 12)
+
+    def offsets(t, names, pw, c0, q, sh, off):
         for a, b in HALVES:
-            tt(P("q2", a, b), P("oV", a, b), P("pU", NB + a, NB + b), A.mult)
-            ts(P("sh2", a, b), P("q2", a, b), 5, A.logical_shift_right, W - 1, A.bitwise_and)
-            if t:
-                ts(P("offA", a, b), P("sh2", a, b), 77.0 * t, A.add)
-            else:
-                cp(P("offA", a, b), P("sh2", a, b))
-        for h in range(4):
-            cp(P("y", Q4 * h, Q4 * h + Q4), IND(P("hx"), P("offA", 48 * h, 48 * h + 48)), "va")
-        cp(P("stb"), P("stR", 24 * t, 24 * t + 24), "va")
-        mms([(P("pR", i, NB, 16), P("CLT", 128 * i, 128 * i + 128), P("stb", 0, 12), True, True, 12) for i in range(16)])
-        cp(P("tR"), P("pR", 0, NB), "va")
-        mms([(GP, P("idb"), P("cbE"), True, False, NB)] +
-            [(P("pR", NB + i, 2 * NB, 16), P("CLP", 128 * i, 128 * i + 128), P("stb", 12, 24), False, i == 15, 12) for i in range(16)])
-        cp(P("FB"), GP, "va")
-        Uo = P("pS", 256, 448)
-        if EV:
-            cp(Uo, R("Ub"))
-        for c in range(8):
-            if c in EV:
-                for k in (2 * c, 2 * c + 1):
-                    tt(P("e", NB * k, NB * k + NB), P("x", k, S3, 16), Uo, A.is_equal)
-                    mms([key("pK", h, k, P("e", NB * k + H * h, NB * k + H * h + H), 0, nK) for h in (0, 1)])
-                continue
-            pd = "pD%d" % (c % 2)
-            mms([z for d in (0, 1) for z in ((P(pd, NB * d, NB * d + NB), P("idb"), P("x", 2 * c + d, S3, 16), True, False, NB),
-                                             (P(pd, NB * d, NB * d + NB), P("nid"), R("Ub"), False, True, NB))])
-            act(P("e", 384 * c, 384 * c + 384), P(pd, 0, 384), F.Relu, 1.0)
-            mms([key("pK", h, 2 * c + d, P("e", 384 * c + NB * d + H * h, 384 * c + NB * d + H * h + H), 0, nK)
-                 for d in (0, 1) for h in (0, 1)])
-        for c in range(12):
-            ts(P("G", NB * c + 16 * c, NB * c + NB), P("tR", 16 * c, NB), P("stR", 24 * t + c, 24 * t + c + 1), A.is_equal)
-        cp(P("nbV"), IND(P("nbb"), P("tl")), "va")
-        recv("B", t, guest, R("Ur"))
-        cp(P("UV"), IND(R("Ub"), P("tl")), "va")
-        cp(P("pU", 0, NB), R("Ur"))
-        tt(P("cmp"), P("UV"), P("pU", 0, NB), A.is_gt)
-        rl(P("pS", 448, 460), "cmp")
-        mm(P("pS", 256, 448), P("blk"), P("cmp"))
-        ts(Lx(8), P("pS", 448, 460), 8.5, A.is_lt)
-        tt(P("okw"), Lx(8), P("wL"), A.mult)
-        ts(wR, P("pS", 256, 448), 8.5, A.is_lt)
-        tt(P("thr"), wR, P("w25"), A.mult)
-        for c in range(12):
-            o, s = P("LT", 128 * c, 128 * c + 128), P("okw", c, c + 1)
-            put("op", [("v", vc(128, 0.5), [lambda o=o, s=s: V.tensor_scalar(o[0], T.blk[:, :], s[0], None, A.mult)]),
-                       ("a", ac(128), [lambda o=o, s=s: Sc.activation(o[0], T.blk[:, :], F.Copy, scale=s[0])])], [P("blk"), s], [o])
-        for c in range(12):
-            mm(P("pS", 256 + 16 * c, 448), P("LT", 128 * c, 128 * c + 128), P("G", NB * c + 16 * c, NB * c + NB), c == 0, c == 11, [P("pS", 0, 1)])
-        tt(wR, P("pS", 256, 448), P("thr"), A.is_lt)
-        cp(R("wn"), wR, "va")
-        send("F", t, guest, R("wnO"), R("wn"))
+            tt(P(q, a, b), P(names, a, b), P(pw, c0 + a, c0 + b), A.mult)
+            ts(P(sh, a, b), P(q, a, b), 5, A.logical_shift_right, W - 1, A.bitwise_and)
+            ts(P(off, a, b), P(sh, a, b), 77.0 * t, A.add)
+
+    def looks(t, out, off):
+        n = NB // NG
+        for h in range(NG):
+            cp(P(out, 16 * n * h, 16 * n * h + 16 * n), IND(P("hx", 0, WX if t else W), P(off, n * h, n * h + n)), "va")
+
+    def own_taste(t):
+        acc([const(P("p2", NB, 2 * NB), 1)] + to_rows("p2", NB, 2 * NB, "CLT", WW(t)))
+
+    def keys(pk, row, src, dat, U, op):
         for h in (0, 1):
             for k in range(16):
-                zz = P("z", 1536 * h + H * k, 1536 * h + H * k + H)
-                tt(zz, P("y", 1536 * h + k, 1536 * h + 1536, 16), P("pU", H * h, H * h + H), A.max)
-                mms([key(("pK2", "pK3")[h], 0, k, zz, 1, (nK2, nK3)[h])])
-        onehot("pK", "sc", "OT", 0)
-        tt(R("JO"), P("om"), P("pR", 0, NB), A.mult)
+                tt(P3(dat, 6 * h, 6 * h + 6, k, 256, 16), P(src, 1536 * h + k, 1536 * h + 1536, 16), P(U[1], H * h, H * h + H), op)
+            out = P(pk[h], H * h, H * h + H)
+            acc([(out, P("blk"), P(row, 0, H))] + [(out, blk_("KL", i), P3(dat, 6 * h, 6 * h + 6, 16 * i, 16 * i + 16)) for i in range(16)])
+
+    own_taste(0)
+    offsets(0, "o", "p2", NB, "q", "sh", "offH")
+    for t in range(RO):
+        host, guest = at(rank + away(t)), at(rank - away(t))
+        b0, b1, a0 = NB * t, NB * t + NB, AM * t
+        R = lambda n, a=0, b=NB: P(n, b0 + a, b0 + b)
+        fin = t == RO - 1
+        slot = lambda j, a=0, b=NB: P("dm", DM * t + 2 + j + 3 * a, DM * t + 2 + 3 * b, 3)
+        looks(t, "x", "offH")
+        for h in range(4):
+            scan(P("s", 768 * h, 768 * h + 768), P("m16"), P("x", 768 * h, 768 * h + 768), 0.0, A.mult, A.max)
+        BH = HALVES if PAR["BH"] == 2 else ((0, NB),)
+        for m, (a, b) in zip("Bb", BH):
+            cp(R("Ub", a, b), P("s", 16 * a + 15, 16 * b, 16), "va")
+            send(m, t, host, R("Ur", a, b), R("Ub", a, b))
+        gt = P("gt", 2, 36, 3)
+        if t:
+            recv("A", t, guest, P("ar", a0, a0 + 48))
+            recv("F", t - 1, at(rank - away(t) + away(t - 1)), P("nbtn", b0 - NB, b0))
+            mms([(dg(0, 36), P("idh"), P("ar", a0, a0 + 36))])
+            acc([const(dg(1, 36, 3), 2)] + to_list(dg(1, 36, 3), "RL", "nbtn", b0 - NB))
+            lin(P("g0"), dg(0, 36), -2.0, 0.0)
+            scan(P("gt"), P("g0"), dg(0, 36), 0.0, A.min, A.max)
+            recv("P", t, guest, P("ar", a0 + 48, a0 + AM))
+        else:
+            recv("A", t, guest, P("ar", 0, AM))
+            cp(gt, P("ar", 2, 36, 3))
+        cp(P("tl"), gt)
+        cp(P("gth"), gt, "va")
+        cp(P("oV"), IND(P("o"), P("tl")), "va")
+        acc([const(P("p4", NB, 2 * NB), 1)] + to_rows("p4", NB, 2 * NB, "CLT", P("ar", a0 + 36, a0 + 48)))
+        offsets(t, "oV", "p4", NB, "q2", "sh2", "offA")
+        looks(t, "y", "offA")
+        mms(to_rows("p4", 0, NB, "CLT", P("gth")))
+        cp(P("tR"), P("p4", 0, NB), "va")
+        acc([(FBp, P("idb"), P("cbE"))] + to_rows("p1", NB, 2 * NB, "CLP", P("ar", a0 + 49, a0 + AM, 2)))
+        cp(P("FB"), FBp, "va")
+        lin(oVc, P("oV"), 1.0, -2048.0)
+        cp(P("nbV"), IND(P("nbb"), P("tl")), "va")
+        mms([(nbp, P("idb"), P("nbV"))])
+        for a, b in BH:
+            mms([(P("p0", a, b), P("idb"), R("Ub", a, b))])
+        keys(("p2", "p2"), "kH", "x", "e", Uo, A.is_equal)
+        scan(P("sc"), P("mH"), kH, 0.0, A.add, A.min)
+        cp(P("jI", 0, 12), P("sc", 15, NB, 16))
+        ts(P("jI", 12, 24), P("jI", 0, 12), 10, A.logical_shift_right, 15, A.bitwise_and)
+        cp(P("jl"), P("jI", 12, 24))
+        cp(P("OJ"), IND(P("Ej"), P("jl")), "va")
+        mms([(Nc, P("idh"), slot(0))])
+        tt(R("JO"), P("OJ"), Nc, A.min)
         send("C", t, host, R("JOr"), R("JO"))
-        onehot("pK2", "sc2", "OT2", NB, 0)
-        onehot("pK3", "sc2", "OT2", NB, 1)
-        tt(P("Vo"), P("oVm"), wR, A.mult)
-        tt(R("got"), P("Vo"), GP, A.mult)
-        send("D", t, guest, R("gotr"), R("got"))
-        tt(P("nbw"), P("nbV"), wR, A.mult)
-        tt(R("nbt"), P("nbw"), GP, A.mult)
+        for m, (a, b) in zip("Bb", BH):
+            recv(m, t, guest, R("Ur", a, b))
+        tt(P("cmp"), IND(R("Ub"), P("tl")), R("Ur"), A.is_gt)
+        acc([const(res, 4)] + to_list(res, "RL", "cmp", 0))
+        left = [28]
+        mms([(Tp, P("g8h"), P("cmp"))], True, left)
+        for c in range(12):
+            ts(P("G", 208 * c, NB * c + NB), P("tR", 16 * c, NB), P("gt", 2 + 3 * c, 3 + 3 * c), A.is_equal, P("p4", 384 + c, 385 + c), A.is_gt)
+            if c < 11:
+                mms([(P("p5", 16 * c + 16, NB, 1, 8), P("g32"), P("G", 208 * c + 16, NB * c + NB))], False, left)
+        mms([(P("p5", i, NB, 16, 8), P("TRI", 8 * i, 8 * i + 8), P("G", i, 12 * NB, 208)) for i in range(16)], False, left)
+        put("op", [("a", ac(NB) + 0.02, [lambda: Sc.activation(T.sg[:, :], Tp[0], F.Sign, bias=8.5, scale=-1.0, accum_out=T.acc[:, :])])],
+            [Tp], [P("sg"), P("acc")])
+        acc([const(Pl, 3), (Pl, P("idh"), P("gth"))] + to_list(Pl, "SEL", "sg", 0, 8))
+        acc(to_list(taste, "WL", "Ub", b0))
+        mms([(cnt, P("half"), P("acc"))])
+        ts(P("uI", 0, 12), taste, cnt, A.add, 768.0, A.add)
+        ts(P("uI", 12, 24), P("uI", 0, 12), 1023, A.bitwise_and)
+        if fin:
+            cp(WW(t + 1), P("uI", 12, 24))
+        else:
+            lin(WW(t + 1), P("uI", 12, 24), 2.0, -991.0, "v")
+            own_taste(t + 1)
+        tt(P("ovf"), Pl, P("cL"), A.max)
+        cp(P("offV"), P("ovf"))
+        cp(IND(P("Cw", b0, b1 + NB), P("offV")), P("FB"))
+        mms([(P("p6", 128 + i, 384, 16, 12), P("Cw", b1 + i, b1 + NB, 16), P("g01")) for i in range(16)])
+        cp(P("xb"), P("p6", 128, 384, 1, 12), "va")
+        mms([(dl(1, 24, 2), P("xb", 0, 128), id12), (dl(50, 84, 3), P("xb", 128, 256), id12), (dl(0, 24, 2), P("idh"), FO(t)),
+             (dl(24, 48, 2), P("idh"), PR(t)), (dl(48, 84, 3), P("idh"), FO(t)), (dl(49, 84, 3), P("idh"), FO(t))])
+        ts(P("thl"), dl(1, 24, 2), 1.0, A.add)
+        if not fin:
+            cp(P("am", a0 + AM, a0 + AM + 36), dl(48, 84), "va")
+            send("A", t + 1, at(rank + away(t + 1)), P("ar", a0 + AM, a0 + AM + 48), P("am", a0 + AM, a0 + AM + 48))
+        for a, b in BH:
+            mms([(P("p1", a, b), P("idb"), R("Ur", a, b))])
+        keys(("p3", PAR["K2"]), "kA", "y", "z", Ur, A.max)
+        DH = HALVES if PAR["DH"] == 2 else ((0, NB),)
+        for m, (a, b) in zip("Dd", DH):
+            c, d = a // 16, b // 16
+            scan(P("sc2", a, b), P("mA", a, b), P("p3" if a == 0 else PAR["K2"], a, b), 0.0, A.mult, A.max)
+            tt(P("gI", c, d), P("sc2", a + 15, b, 16), P("p6", c, d), A.add)
+            ts(P("gI", 12 + c, 12 + d), P("gI", c, d), 9, A.logical_shift_right, 31, A.bitwise_and)
+            cp(P("gl", c, d), P("gI", 12 + c, 12 + d))
+            cp(P("OG", a, b), IND(P("Eg"), P("gl", c, d)), "va")
+            tt(R("got", a, b), P("OG", a, b), P("p7", a, b), A.min)
+            send(m, t, guest, R("gotr", a, b), R("got", a, b))
+        tt(R("nbt"), P("OG"), nbp, A.min)
+        if not fin:
+            send("F", t, at(rank - away(t) + away(t + 1)), R("nbtn"), R("nbt"))
         send("E", t, guest, R("nbtr"), R("nbt"))
-        rl(P("pS", 460, 472), "wn", b0)
-        wl, wo = P("wl", 12 * t, 12 * t + 12), P("wlO", 12 * t, 12 * t + 12)
-        lin(wl, P("pS", 460, 472), 1.0 / 16, 0.0)
-        send("L", t, guest, wo, wl)
-        put("op", [("v", vc(12), [lambda wl=wl: V.tensor_reduce(T.cnt[:, :], wl[0], AxisListType.X, A.add)])], [wl], [P("cnt")])
-        mm(P("pS", NB, NB + 1), P("one"), P("cnt"))
-        w_ = P("w", b0 + NB, b1 + NB)
-        ts(P("uA"), P("pS", 0, NB), P("pS", NB, NB + 1), A.add)
-        ts(P("uI"), P("uA"), 1023, A.bitwise_and)
-        if not fin:
-            ts(wP, P("uI"), 2.0, A.mult, 33.0, A.add)
-            cp(w_, wP, "va")
-            send("W", t + 1, nhost, P("wr", b0 + NB, b1 + NB), w_)
-        tt(Lx(6), sr, P("cL"), A.subtract)
-        tt(Lx(7), wl, Lx(6), A.mult)
-        tt(Lx(7), Lx(7), P("cL"), A.add)
-        cp(P("offV"), Lx(7))
-        tt(P("V3"), P("FB"), wR, A.mult)
-        cp(P("Cw", 0, NB), P("zr"), "va")
-        cp(IND(P("Cw"), P("offV")), P("V3"))
-        rl(P("pS", 472, 484), "Cw", 0, 128, True)
         recv("C", t, guest, R("JOr"))
-        mms([(P("pS", 256, 448), P("blk"), P("c128"), True, False, NB), (P("pS", 256, 448), P("blkH"), R("JOr"), False, True, NB)])
-        tt(P("nj"), R("wn"), P("pS", 256, 448), A.mult)
-        tt(P("XS"), P("nj"), GP, A.mult)
-        cp(P("Xw", 0, NB), P("zr"), "va")
-        cp(IND(P("Xw"), P("offV")), P("XS"))
-        recv("F", t, host, R("wnO"))
-        mm(P("pK2", 0, NB), P("blkG"), R("wnO"), True, False)
-        tt(P("jw"), P("pR", 0, NB), R("wnO"), A.mult)
-        lin(x0, P("jw"), -1.0, 1.0)
-        tt(P("oj"), x0, R("o1"), A.mult)
-        lin1(x1, P("Xw", 0, NB))
-        tt(x2, P("oj"), x1, A.mult)
-        tt(P("c2"), x2, P("Xw", 0, NB), A.add)
-        tt(P("jk"), P("jw"), x1, A.mult)
+        acc([const(nj, 0), (nj, P("blkH"), R("JOr"))])
+        tt(P("XS", 1, NB + 1), P("OG"), nj, A.min)
+        cp(slot(2), IND(P("XS"), P("thl")), "va")
+        lin(P("d0", 2, 3 * NB, 3), slot(2), -2.0, -6144.0)
+        for m, (a, b) in zip("Dd", DH):
+            recv(m, t, host, R("gotr", a, b))
+            acc([const(P("p3", NB + a, NB + b), 0), (P("p3", NB + a, NB + b), P("blkH"), R("gotr", a, b))])
+        for a, b in HALVES:
+            tt(slot(1, a, b), P("OJ", a, b), P("p3", NB + a, NB + b), A.min)
+            lin(P("d0", 1 + 3 * a, 3 * b, 3), slot(1, a, b), -2.0, -6144.0, "v")
+            scan(P("dm", DM * (t + 1) + 3 * a, DM * (t + 1) + 3 * b), P("d0", 3 * a, 3 * b), P("dm", DM * t + 2 + 3 * a, DM * t + 2 + 3 * b),
+                 0.0, A.min, A.max)
+            lin(P("o", a, b), P("dm", DM * (t + 1) + 2 + 3 * a, DM * (t + 1) + 3 * b, 3), 1.0, 2048.0)
         if not fin:
-            tt(P("Jw"), P("jk"), wP, A.mult)
-            lin(P("cw"), P("c2"), 1.0, -1.0)
-            tt(P("bw"), P("cw"), wP, A.mult)
-        tau, prev = P("stL", 24 * t, 24 * t + 12), P("stL", 24 * t + 12, 24 * t + 24)
-        tau_, prev_ = P("stL", 24 * t + 24, 24 * t + 36), P("stL", 24 * t + 36, 24 * t + 48)
-        fo, fo_ = P("foL", 12 * t, 12 * t + 12), P("foL", 12 * t + 12, 12 * t + 24)
-        recv("L", t, host, wo)
-        lin(Lx(2), wo, -1.0, 1.0)
-        cp(P("cI"), P("pS", 472, 484))
-        ts(P("lo"), P("cI"), 255, A.bitwise_and)
-        ts(P("hi"), P("cI"), 8, A.logical_shift_right)
-        ts(Lx(0), P("lo"), 0.5, A.is_lt)
-        tt(Lx(1), Lx(0), fo, A.mult)
-        tt(fo_, Lx(1), P("lo"), A.add)
-        lin(Lx(3), fo, 1.0, -1.0)
-        tt(Lx(11), Lx(3), Lx(2), A.mult)
-        tt(Lx(12), Lx(11), Lx(0), A.mult)
-        tt(Lx(13), Lx(12), P("hi"), A.add)
-        tt(Lx(4), tau, prev, A.subtract)
-        tt(Lx(14), Lx(4), wo, A.mult)
-        tt(prev_, Lx(14), prev, A.add)
-        recv("D", t, host, R("gotr"))
-        mm(P("pK2", 0, NB), P("blkH"), R("gotr"), False, True)
-        o1_ = P("o1", b0 + NB, b1 + NB)
-        if not fin:
-            for a, b in HALVES:
-                tt(P("pD1", NB + a, NB + b), P("Jw", a, b), P("pK2", a, b), A.mult)
-                tt(P("q", a, b), P("pD1", NB + a, NB + b), P("bw", a, b), A.add)
-                ts(P("sh", a, b), P("q", a, b), 5, A.logical_shift_right, W - 1, A.bitwise_and)
-                ts(P("offH", a, b), P("sh", a, b), 77.0 * (t + 1), A.add)
+            offsets(t + 1, "o", "p2", NB, "q", "sh", "offH")
         recv("E", t, host, R("nbtr"))
-        rl(P("pS", 484, 496), "nbtr", b0)
-        tt(Lx(5), Lx(0), P("pS", 484, 496), A.mult)
-        tt(tau_, Lx(5), Lx(13), A.add)
+        acc([const(dl(49, 84, 3), 2)] + to_list(dl(49, 84, 3), "RL", "nbtr", b0))
+        lin(P("nm"), dl(49, 84, 3), 4.0, 192.0)
+        tt(dl(25, 48, 2), P("nm"), TA(t), A.min)
+        lin(P("l0"), dl(0, 84), -2.0, 0.0)
+        scan(P("st", ST * t + ST, ST * t + ST + 84), P("l0"), dl(0, 84), 0.0, A.min, A.max)
         if not fin:
-            send("A", t + 1, nhost, P("stR", 24 * t + 24, 24 * t + 48), P("stL", 24 * t + 24, 24 * t + 48))
-        tt(x0, P("jk"), P("pK2", 0, NB), A.mult)
-        tt(o1_, x0, P("c2"), A.add)
-    tN = 24 * RO
-    cp(P("stO", 0, 24), P("stL", tN, tN + 24), "va")
-    lin(P("stO", 24, 36), P("foL", 12 * RO, 12 * RO + 12), 1.0, -1.0)
-    for f, (pn, c0) in enumerate((("pD0", 0), ("pD0", NB), ("pD1", 0))):
-        mms([(P(pn, c0 + i, c0 + NB, 16, 8), P("CLT", 128 * i, 128 * i + 128, 16), P("stO", 12 * f, 12 * f + 12), True, True, 12) for i in range(16)])
-    lin(P("oj"), P("o1", NB * RO, NB * RO + NB), 1.0, -1.0)
-    dma("y", T.yo[:, :], T.oj[:, :], "st0", [P("oj")])
-    cp(P("nw"), P("uI"))
-    dma("y", T.yu[:, :], T.nw[0:128:16, :], "st1", [P("nw")])
-    cp(P("o8", 0, 2 * NB, 1, 8), P("pD0", 0, 2 * NB, 1, 8), "va")
-    cp(P("o8", 2 * NB, 3 * NB, 1, 8), P("pD1", 0, NB, 1, 8), "va")
-    dma("y", T.yt[:, :], T.o8[0:8, 0:NB], "st2", [P("o8", 0, NB)])
-    dma("y", T.yp[:, :], T.o8[0:8, NB:2 * NB], "st3", [P("o8", NB, 2 * NB)])
-    dma("y", T.yf[:, :], T.o8[0:8, 2 * NB:3 * NB], "st4", [P("o8", 2 * NB, 3 * NB)])
+            send("P", t + 1, at(rank + away(t + 1)), P("ar", a0 + AM + 48, a0 + 2 * AM), P("st", ST * t + ST + 24, ST * t + ST + 48))
+    dma("y", T.yo[:, :], T.o[:, :], "st0", [P("o")])
+    turn = lambda pn, c0, c1, lst: mms([(P(pn, c0 + i, c1, 16, 8), P("CLT", 128 * i, 128 * i + 128, 16), lst) for i in range(16)])
+    turn("p0", 0, NB, WW(RO))
+    turn("p1", 0, 2 * NB, P("st", ST * RO + 1, ST * RO + 48, 2))
+    turn("p2", 0, NB, TA(RO))
+    for j, (out, pn, c0) in enumerate(((T.yu, "p0", 0), (T.yf, "p1", 0), (T.yp, "p1", NB), (T.yt, "p2", 0))):
+        cp(P("o8", NB * j, NB * j + NB), P(pn, c0, c0 + NB, 1, 8), "va")
+        dma("ya"[j % 2], out[:, :], T.o8[0:8, NB * j:NB * j + NB], "st%d" % (1 + j), [P("o8", NB * j, NB * j + NB)])
 
     count, known, clocks, hist = {}, {q: {} for q in queues}, {}, {}
     left = 0
@@ -551,9 +517,8 @@ def rank_program(g, core, T, topo):
         for lst, wr in ((reads, False), (writes, True)):
             for r in lst:
                 ps = r[1] in PS
-                for (a0, a1, w, oq, point) in hist.get(r[1], ()):
-                    over = a0 < r[3] and r[2] < a1
-                    if (over and (wr or w) and not (ps and q == "p" and oq == "p")) or (ps and oq != q):
+                for (z, w, oq, point) in hist.get(r[1], ()):
+                    if (meet(r, z) and (wr or w) and not (ps and q == "p" and oq == "p")) or (ps and oq != q):
                         want[point[0]] = max(want.get(point[0], 0), point[1])
         kn = known[q]
         for s in sorted(want, key=lambda z: -want[z]):
@@ -569,14 +534,16 @@ def rank_program(g, core, T, topo):
             for r in lst:
                 h = hist.setdefault(r[1], [])
                 if r[1] in PS:
-                    h[:] = [z for z in h if not (z[3] == q and z[2] == wr and r[2] <= z[0] and z[1] <= r[3])]
+                    h[:] = [z for z in h if not (z[2] == q and z[1] == wr and cover(r, z[0]))]
                 elif wr:
-                    h[:] = [z for z in h if not (r[2] <= z[0] and z[1] <= r[3])]
-                h.append((r[2], r[3], wr, q, point))
+                    h[:] = [z for z in h if not cover(r, z[0])]
+                h.append((r, wr, q, point))
 
-    for _, i, q in order(ops):
+    if not PLAN:
+        PLAN.extend(order(ops))
+    for _, i, q in PLAN:
         o = ops[i]
-        rd, wr = o["reads"], o["writes"]
+        rd, wr = [[r for r in lst if r[1] in SCRATCH] for lst in (o["reads"], o["writes"])]
         if o["kind"] == "recv":
             msg, t, src, buf = o["args"]
             note("r", rd, wr, ("m%s%d" % (msg, t), len(topo.engines(src, core)[:8])), {})
@@ -598,7 +565,7 @@ def rank_program(g, core, T, topo):
             note(q, rd, wr, (q, count[q]), dict(known[q]))
     for i in range(5):
         g.sync.wait_ge(T.sem["st%d" % i], 16)
-    for i in range(9):
+    for i in range(10):
         if known["v"].get("ld%d" % i, 0) < 16:
             g.vector.wait_ge(T.sem["ld%d" % i], 16)
     for s in ("v", "a", "p", "k"):

@@ -1,3 +1,5 @@
+import math
+import numpy as np
 from concourse.mybir import AluOpType as A, ActivationFunctionType as F
 
 NB, W, RO, N = 192, 4096, 5, 4
@@ -19,12 +21,13 @@ SCRATCH = {
     "idb": ("sbuf", [128, 128], "bfloat16"), "idh": ("sbuf", [128, 128], "float16"), "blk": ("sbuf", [128, 128], "bfloat16"),
     "blkH": ("sbuf", [128, 128], "float16"), "g8h": ("sbuf", [128, 8], "float16"), "g8s": ("sbuf", [128, 8], "float16"),
     "g32": ("sbuf", [128, 8], "bfloat16"), "g01": ("sbuf", [128, 16], "bfloat16"), "TRI": ("sbuf", [128, 128], "bfloat16"),
-    "CLT": ("sbuf", [128, 2048], "float16"), "CLP": ("sbuf", [128, 2048], "float16"), "RL": ("sbuf", [128, 2048], "float16"),
-    "KL": ("sbuf", [128, 2048], "bfloat16"), "WL": ("sbuf", [128, 2048], "bfloat16"), "SEL": ("sbuf", [8, 2048], "bfloat16"),
-    "SE0": ("sbuf", [8, 2048], "float16"),
-    "cbE": ("sbuf", [128, NB], "bfloat16"), "cst": ("sbuf", [128, 5 * NB], "bfloat16"), "kH": ("sbuf", [128, NB], "bfloat16"),
+    "CLT": ("sbuf", [128, 2048], "float16"), "CLP": ("sbuf", [128, 2048], "float16"), "KL": ("sbuf", [128, 2048], "bfloat16"),
+    "g8w": ("sbuf", [128, 8], "bfloat16"), "idF": ("sbuf", [12, 12], "float32"),
+    "xr": ("sbuf", [12, 128], "float16"), "xs": ("sbuf", [12, 128], "float16"), "xn": ("sbuf", [12, 128], "float16"),
+    "xm": ("sbuf", [12, 128], "float16"), "xw": ("sbuf", [12, 128], "float32"),
+    "cbE": ("sbuf", [128, NB], "bfloat16"), "cst": ("sbuf", [128, 2 * 256], "bfloat16"), "kH": ("sbuf", [128, NB], "bfloat16"),
     "kA": ("sbuf", [128, NB], "bfloat16"), "mH": ("sbuf", [128, NB], "float32"), "mA": ("sbuf", [128, NB], "float32"),
-    "m16": ("sbuf", [128, S3 // 4], "bfloat16"), "Ej": ("sbuf", [128, 16], "bfloat16"), "Eg": ("sbuf", [128, 32], "bfloat16"),
+    "m16": ("sbuf", [128, 1024], "bfloat16"), "Ej": ("sbuf", [128, 16], "bfloat16"), "Eg": ("sbuf", [128, 32], "bfloat16"),
     "cL": ("sbuf", [128, 12], "float32"), "half": ("sbuf", [8, 128], "float32"),
     "dm": ("sbuf", [128, 6 * DM], "float16"), "st": ("sbuf", [128, 6 * ST], "float16"),
     "am": ("sbuf", [128, 6 * AM], "float16"), "ar": ("sbuf", [128, 5 * AM], "float16"),
@@ -55,20 +58,25 @@ SCRATCH = {
 }
 PS = ("p0", "p1", "p2", "p3", "p4", "p5", "p6", "p7")
 TWO = ("bfloat16", "uint16", "float16")
-MSG = ("A", "P", "B", "b", "C", "D", "d", "E", "F")
-SEMAPHORES = ["v", "a", "p", "k", "left"] + ["ld%d" % i for i in range(10)] + ["st%d" % i for i in range(5)] \
+MSG = ("A", "P", "B", "b", "C", "D", "d", "e", "E", "F")
+SEMAPHORES = ["v", "a", "p", "k", "left"] + ["ld%d" % i for i in range(9)] + ["st%d" % i for i in range(5)] \
     + ["m%s%d" % (m, t) for m in MSG for t in range(RO)]
-PAR = {"CYC": 0.001, "PE": 0.0006, "LATE": 0.08, "FLY": 2.2, "VF": 0.01, "HUE": 7.0, "BIAS": 1.0, "PASSES": 6, "NG": 4, "BH": 2,
-       "DH": 2, "K2": "p2"}
+PAR = {"CYC": 0.00084, "PE": 0.00053, "LATE": 0.18, "FLY": 1.6, "VF": 0.012, "AF": 0.04, "HUE": 6.4, "FIRST": 3.2, "BIAS": 2.0,
+       "STEPS": 12000, "SEED": 1, "PULL": 0.5, "HEAT": 0.15, "ROUND": 15.0, "CASES": ((0.22, -0.6, 0.85), (0.12, 0.3, 1.1)), "NG": 6,
+       "DP": ((0, 96), (96, 192)), "AP": ((0, 192),), "e": ((0, 96), (96, 192)), "z": ((0, 96), (96, 192)), "NS": 4}
+WHEN = {"start": (-72.1, 0), "tables": (27.4, 0), "names": (13.8, 1.9), "x": (30.7, 2.9), "s": (42.3, 13.7), "U": (-5.6, 35.6),
+        "targets": (12.4, 0), "lists": (50.2, 0), "y": (-1.6, 2.8), "rows": (20.3, 0), "loot": (55.7, 0), "e": (13.6, 9.9),
+        "j": (2.3, 0), "first": (10.3, 0), "taste": (17.6, 0), "victims": (14.3, 0), "z": (36.4, 22.8), "g": (4.1, 5.7),
+        "nb": (6.9, 0), "swap": (34.6, 0)}
 PLAN = []
 
 
-def place(ops, before, rank, back):
+def place(ops, before, rank):
     n = len(ops)
     start, end, queue, busy, late = [0.0] * n, [0.0] * n, [None] * n, {}, PAR["LATE"]
     for i in sorted(range(n), key=lambda i: rank[i]):
         o, best = ops[i], None
-        r = max([end[j] + ops[i if back else j]["late"] for j in before[i]] + [ops[i]["late"] if back else 0.0])
+        r = max([end[j] + ops[j]["late"] for j in before[i]] + [0.0])
         for q, c in o["alt"]:
             held = [z[:2] for z in busy.get(q, ()) if z[1] > r]
             for b in o["banks"]:
@@ -95,19 +103,101 @@ def order(ops):
     for i in range(n):
         for d in pred[i]:
             succ[d].append(i)
-    tail = [0.0] * n
+    due = [0.0] * n
     for i in range(n - 1, -1, -1):
-        tail[i] = min(c for _, c in ops[i]["alt"]) + ops[i]["late"] + max([tail[j] for j in succ[i]] + [0.0])
-    rank, best = [(-tail[i], i) for i in range(n)], None
-    for _ in range(PAR["PASSES"]):
-        start, end, queue = place(ops, pred, rank, False)
-        span = max(end[i] + ops[i]["late"] for i in range(n))
-        if best is None or span < best[0]:
-            best = (span, start, queue)
-        _, end, _ = place(ops, succ, [(-end[i], -i) for i in range(n)], True)
-        rank = [(-end[i], i) for i in range(n)]
-    PAR["SPAN"] = best[0]
-    return sorted((best[1][i], i, best[2][i]) for i in range(n))
+        t, step, j = ops[i]["when"]
+        way = min(c for _, c in ops[i]["alt"]) + ops[i]["late"]
+        due[i] = min([PAR["ROUND"] * t + WHEN[step][0] + WHEN[step][1] * j] + [due[d] - way for d in succ[i]])
+    start, end, queue = place(ops, pred, [(due[i], i) for i in range(n)])
+    PAR["SPAN"] = max(end[i] + ops[i]["late"] for i in range(n))
+    return shorten(ops, pred, succ, sorted(range(n), key=lambda i: (start[i], i)), queue)
+
+
+def shorten(ops, pred, succ, seq, queue):
+    n = len(ops)
+    lag = [o["late"] for o in ops]
+    cost = [dict(o["alt"]) for o in ops]
+    alike, seen = {}, {}
+    for i, o in enumerate(ops):
+        k = o["when"][1:] + ((o["writes"] or o["reads"])[0][1],)
+        seen[(o["when"][0], k)] = seen.get((o["when"][0], k), 0) + 1
+        alike.setdefault(k + (seen[(o["when"][0], k)],), []).append(i)
+    alike = {i: {ops[j]["when"][0] - ops[i]["when"][0]: j for j in v} for v in alike.values() for i in v}
+    sends = [i for i in range(n) if ops[i]["kind"] == "send"]
+
+    cases = [(late, [late if o["kind"] == "op" else o["late"] + fly * (o["kind"] == "send") for o in ops],
+              [{q: c * (pe if q == "p" else 1.0) for q, c in o["alt"]} for o in ops]) for late, fly, pe in PAR["CASES"]]
+
+    def run(seq, queue, pick=0):
+        both = [one(seq, queue, *case) for case in cases]
+        return (sum(z[0] for z in both) / len(both),) + both[pick][1:]
+
+    def one(seq, queue, late, lag, cost):
+        end, by, on = [0.0] * n, [None] * n, {}
+        for i in seq:
+            r, b, q = 0.0, None, queue[i]
+            for d in pred[i]:
+                if end[d] + lag[d] > r:
+                    r, b = end[d] + lag[d], (d, False)
+            d = on.get(q)
+            if d is not None and end[d] > r:
+                r, b = end[d], (d, True)
+            on[q] = i
+            for bank in ops[i]["banks"]:
+                last = on.setdefault(bank, {})
+                for q2, d in last.items():
+                    if q2 != q and end[d] + late > r:
+                        r, b = end[d] + late, (d, True)
+                last[q] = i
+            end[i], by[i] = r + cost[i][q], b
+        tip = max(range(n), key=lambda i: end[i] + lag[i])
+        return end[tip] + lag[tip] + PAR["PULL"] * sum(end[i] for i in sends) / len(sends), end, by, tip, seq, queue
+
+    def swap(seq, a, b, forward):
+        pa, pb = seq.index(a), seq.index(b)
+        if pa > pb:
+            return seq
+        part = seq[pa:pb + 1]
+        near, go = (pred, {a}) if forward else (succ, {b})
+        for i in (part if forward else part[::-1]):
+            if any(d in go for d in near[i]):
+                go.add(i)
+        if a in go and b in go:
+            return seq
+        return seq[:pa] + [i for i in part if (i in go) != forward] + [i for i in part if (i in go) == forward] + seq[pb + 1:]
+
+    rng = np.random.default_rng(PAR["SEED"])
+    cur = best = run(seq, queue)
+    for step in range(PAR["STEPS"]):
+        u = rng.random(6)
+        i = cur[3] if u[0] < 0.5 else sends[int(u[1] * len(sends))]
+        lo, way = (cur[1][i] - 12.0 if u[0] >= 0.5 else -1.0), []
+        while cur[2][i] is not None and cur[1][i] > lo:
+            way.append(i)
+            i = cur[2][i][0]
+        seq, queue = cur[4], cur[5]
+        if u[2] < 0.15:
+            way = [i for i in way if len(cost[i]) > 1]
+            if way:
+                i, queue = way[int(u[3] * len(way))], list(queue)
+                other = [q for q in cost[i] if q != queue[i]][0]
+                for j in (alike[i].values() if u[4] < 0.7 else [i]):
+                    queue[j] = other
+        else:
+            way = [i for i in way if cur[2][i][1]]
+            if way:
+                b = way[int(u[3] * len(way))]
+                a = cur[2][b][0]
+                for d in (alike[a] if u[4] < 0.7 else [0]):
+                    if d in alike[b]:
+                        seq = swap(seq, alike[a][d], alike[b][d], u[2] < 0.55)
+        new = run(seq, queue, step % len(cases))
+        if new[0] - cur[0] <= -math.log(u[5]) * PAR["HEAT"] * (1.0 - step / PAR["STEPS"]):
+            cur = new
+            if cur[0] < best[0]:
+                best = cur
+    PAR["SHORT"] = best[1][best[3]] + lag[best[3]]
+    return [(0.0, i, best[5][i]) for i in best[4]]
 
 
 def rank_program(g, core, T, topo):
@@ -115,7 +205,7 @@ def rank_program(g, core, T, topo):
     if rank is None:
         return
     queues = {"v": g.vector, "a": g.scalar, "p": g.tensor, "k": g, "y": g.sync}
-    ops, last, sent, group = [], {}, {}, {}
+    ops, bundle, last, sent, group, now = [], [], {}, {}, {}, [(0, "start", 0)]
     CYC, VF = PAR["CYC"], PAR["VF"]
 
     def P(name, c0=0, c1=None, step=1, p=128):
@@ -140,6 +230,9 @@ def rank_program(g, core, T, topo):
     cover = lambda a, b: a[2] <= b[2] and b[3] <= a[3] and (a[5] == 1 or (a[5] == b[5] and (a[2] - b[2]) % a[5] == 0))
 
     def put(kind, alt, reads, writes, late=None, loose=(), **more):
+        if bundle:
+            bundle.append((alt[0], reads, writes))
+            return None
         reads, writes = flat(reads), flat(writes)
         i, deps = len(ops), set()
         for lst, wr in ((reads, False), (writes, True)):
@@ -156,16 +249,24 @@ def rank_program(g, core, T, topo):
         deps.discard(i)
         banks = sorted(set(r[1] for r in reads + writes if r[1] in PS))
         o = {"kind": kind, "alt": [(q, c) for q, c, _ in alt], "fns": {q: f for q, _, f in alt}, "reads": reads, "writes": writes,
-             "deps": deps, "banks": banks, "late": PAR["LATE"] if late is None else late}
+             "deps": deps, "banks": banks, "late": PAR["LATE"] if late is None else late, "when": now[0]}
         o.update(more)
         ops.append(o)
         return i
+
+    def together(call, js):
+        bundle.append(None)
+        for j in js:
+            call(j)
+        all_ = bundle[1:]
+        del bundle[:]
+        put("op", [("v", sum(z[0][1] for z in all_), [f for z in all_ for f in z[0][2]])], [r for z in all_ for r in z[1]], [r for z in all_ for r in z[2]])
 
     V, Sc, Te = g.vector, g.scalar, g.tensor
     dts = lambda x: SCRATCH[(x[1] if len(x) == 3 else x)[1]][2]
     two = lambda xs: all(dts(x) in TWO for x in xs)
     vc = lambda n, cyc=1.0: (0.05 if cyc in (1.5, 3.5) else VF) + max(64, n * cyc) * CYC
-    ac = lambda n, cyc=1.0: (0.065 if cyc == 1.5 else VF) + max(64, n * cyc) * CYC
+    ac = lambda n, cyc=1.0: (0.065 if cyc == 1.5 else PAR["AF"]) + max(64, n * cyc) * CYC
     size = lambda x: 16 * (x[2][3] - x[2][2]) if len(x) == 3 else x[4]
     col = lambda s: s[0] if isinstance(s, tuple) else s
 
@@ -180,8 +281,9 @@ def rank_program(g, core, T, topo):
         put("op", alt, [in_], [out])
 
     def lin(out, in_, m, b, qs="va"):
-        alt = [("v", vc(size(out), 0.5 if two([out, in_]) else 1.0), [lambda: V.tensor_scalar(out[0], in_[0], col(m), b, A.mult, A.add)]),
-               ("a", ac(size(out)), [lambda: Sc.activation(out[0], in_[0], F.Identity, bias=b, scale=col(m))])]
+        gat = len(in_) == 3
+        alt = [("v", vc(size(out), 1.5 if gat else 0.5 if two([out, in_]) else 1.0), [lambda: V.tensor_scalar(out[0], in_[0], col(m), b, A.mult, A.add)]),
+               ("a", ac(size(out), 1.5 if gat else 1.0), [lambda: Sc.activation(out[0], in_[0], F.Identity, bias=b, scale=col(m))])]
         put("op", [z for z in alt if z[0] in qs], [in_] + ([m] if isinstance(m, tuple) else []), [out])
 
     def tt(out, a, b, o):
@@ -199,6 +301,11 @@ def rank_program(g, core, T, topo):
     def ms(out, c):
         put("op", [("v", vc(size(out), 0.5 if two([out]) else 1.0), [lambda: V.memset(out[0], c)])], [], [out])
 
+    def fill(out, c):
+        src = P("CLT", 0, out[4], 1, T[out[1]].shape[0])
+        put("op", [("v", vc(size(out), 0.5 if two([out]) else 1.0), [lambda: V.memset(out[0], c)]),
+                   ("a", ac(size(out)), [lambda: Sc.activation(out[0], src[0], F.Identity, bias=c, scale=0.0)])], [src], [out])
+
     def scan(out, d0, d1, init, o0, o1):
         put("op", [("v", vc(size(out), 0.5 if two([out, d0, d1]) else 1.0),
                     [lambda: V.tensor_tensor_scan(out[0], d0[0], d1[0], init, o0, o1)])], [d0, d1], [out])
@@ -208,7 +315,7 @@ def rank_program(g, core, T, topo):
         return n[0] == 0
 
     def mms(lst, first=True, left=None):
-        c = sum((0.005 + max(min(64, z[1][4]), z[2][4]) * PAR["PE"]) * (4 if dts(z[2]) == "float32" else 1) for z in lst)
+        c = sum((max(64, z[2][4]) * PAR["PE"]) * (4 if dts(z[2]) == "float32" else 1) for z in lst)
         fns = []
         for j, z in enumerate(lst):
             if left is None:
@@ -243,7 +350,7 @@ def rank_program(g, core, T, topo):
         put("dma", [(q, 0.1, [lambda: queues[q].dma_start(out, in_)])], list(reads), list(writes), late, sem=sem)
 
     def send(msg, t, dst, out, in_):
-        sent[(msg, t)] = put("send", [("k", 0.6, None)], [in_], [], PAR["FLY"] + 0.0015 * in_[4] * (2 if dts(in_) in TWO else 4),
+        sent[(msg, t)] = put("send", [("k", 0.6, None)], [in_], [], PAR["FLY"] + 0.00133 * in_[4] * 2 + (0 if sent else PAR["FIRST"]),
                              args=(msg, t, dst, out, in_))
 
     def recv(msg, t, src, buf):
@@ -251,10 +358,15 @@ def rank_program(g, core, T, topo):
         ops[i]["deps"].add(sent[(msg, t)])
 
     blk_ = lambda m, i, p=128: P(m, 128 * i, 128 * i + 128, 1, p)
-    to_list = lambda out, m, src, c0, p=128: [(out, blk_(m, i, p), P(src, c0 + i, c0 + NB, 16, p)) for i in range(16)]
+
+    def to_list(out, src, c0, sel, pn, pc, x, m, b):
+        mms([(P(pn, pc + i, pc + 128, 16, 12), P(src, c0 + i, c0 + NB, 16), sel) for i in range(16)])
+        lin(P(x), P(pn, pc, pc + 128, 1, 12), m, b)
+        return (out, P(x), P({"float16": "idh", "bfloat16": "idb", "float32": "idF"}[SCRATCH[x][2]], 0, 12, 1, 12))
+
     to_rows = lambda pn, c0, c1, m, lst: [(P(pn, c0 + i, c1, 16), blk_(m, i), lst) for i in range(16)]
-    const = lambda out, j: (out, P("blk"), P("cst", NB * j, NB * j + out[4]))
-    CONST = (3840.0, 64.0, 240.0, -4.0, 15.0 / 512)
+    const = lambda out, j: (out, P("blk"), P("cst", 256 * j, 256 * j + out[4]))
+    CONST = ((3840.0, NB), (64.0, NB))
     away = lambda t: 1 + t % (N - 1)
     at = lambda r: T.cores[r % N]
 
@@ -298,30 +410,29 @@ def rank_program(g, core, T, topo):
     cp(TA(0), P("p6", 128, 140), "va")
     cp(PR(0), P("p6", 140, 152), "va")
     cp(FO(0), P("p6", 152, 164), "va")
-    for i in range(16):
-        ts(blk_("CLT", i), P("blkH"), P("g16", i, i + 1), A.mult)
+    for i0 in range(0, 16, 4):
+        together(lambda i: ts(blk_("CLT", i), P("blkH"), P("g16", i, i + 1), A.mult), range(i0, i0 + 4))
     cp(P("blk"), P("blkH"))
     cp(P("idb"), P("idh"))
-    for j, c in enumerate(CONST):
-        ms(P("cst", NB * j, NB * j + NB), c)
+    for j, (c, n) in enumerate(CONST):
+        ms(P("cst", 256 * j, 256 * j + n), c)
     cp(P("o"), P("ownI"))
     lin(P("dm", 2, 3 * NB, 3), P("ownI"), 1.0, -2048.0, "v")
     ms(P("m16"), 1.0)
-    ms(P("m16", 0, S3 // 4, 16), 0.0)
+    ms(P("m16", 0, 1024, 16), 0.0)
+    now[0] = (0, "tables", 0)
     ts(P("g8h"), P("i32", 0, 8), PF(1), A.is_equal)
     ts(P("g8s"), P("i32", 0, 8), PF(1), A.is_equal, 1.0 / 16, A.mult)
     ts(P("g32"), P("i32", 0, 8), PF(1), A.is_equal, 32.0, A.mult)
     for f in range(2):
         ts(P("g01", 8 * f, 8 * f + 8), P("i32", 0, 8), PF(1), A.is_equal, P("g16", f, f + 1), A.mult)
-    ms(P("RL"), 0.0)
-    for i in range(16):
-        cp(P("RL", 129 * i, 128 * i + 128, 16), P("g8s"))
-    lin(P("KL"), P("RL"), 16.0 * 16384, 0.0)
-    lin(PF(3), P("wtI"), 16.0, 0.0, "v")
-    lin(P("WL"), P("RL"), PF(3), 0.0)
-    dma("y", T.SE0[0:8, :], T.RL[0:128:16, :], "ld9", [P("RL")], [P("SE0")])
-    lin(P("SEL"), P("SE0"), 4096.0, 0.0)
-    ms(P("CLP"), 0.0)
+    for j in range(4):
+        mms([(P("p%d" % (j % 2), 128 * i, 128 * i + 128), blk_("CLT", 4 * j + i), P("idh")) for i in range(4)])
+        lin(P("KL", 512 * j, 512 * j + 512), P("p%d" % (j % 2)), 16384.0, 0.0)
+    cp(PF(3), P("wtI"))
+    ts(P("g8w"), P("i32", 0, 8), PF(1), A.is_equal, PF(3), A.mult)
+    ts(P("idF"), P("dif", 0, 12, 1, 12), 0.0, A.is_equal)
+    fill(P("CLP"), 0.0)
     cp(P("CLP", 1, 2048, 16), P("CLT", 1, 2048, 16))
     ts(P("ia"), P("ia"), PF(1), A.is_equal, 32.0, A.mult)
     ts(P("ib"), P("ib"), PF(2), A.is_gt)
@@ -329,23 +440,23 @@ def rank_program(g, core, T, topo):
     ts(P("cbE"), P("lane"), P("g16", 0, 1), A.mult)
     ts(P("cL"), P("cL"), PF(2), A.add)
     lin(P("nbb"), P("nbI"), 16.0, 0.0, "v")
-    ms(P("mA"), 1.0)
-    ms(P("mA", 0, NB, 16), 0.0)
-    ms(P("mH"), 0.0)
-    ms(P("mH", 0, NB, 16), 1e9)
+    fill(P("mA"), 1.0)
+    fill(P("mA", 0, NB, 16), 0.0)
+    fill(P("mH"), 0.0)
+    fill(P("mH", 0, NB, 16), 1e9)
+
     lin(P("Ej"), P("g16"), 8192.0, NONE, "v")
     lin(PF(4), PF(2), -2.0, 31.0, "v")
     ts(P("Eg"), P("i32"), PF(4), A.is_equal, 8192.0, A.mult)
     ts(P("Eg"), P("Eg"), NONE, A.add)
-    ms(P("half"), 0.5)
-    ms(P("Cw", NB, 6 * NB), NONE)
-    ms(P("XS"), NONE)
-    ms(P("d0", 0, 3 * NB, 3), NONE)
+    fill(P("half"), 0.5)
+    for t in range(RO):
+        fill(P("Cw", NB * t + NB, NB * t + 2 * NB), NONE)
+    fill(P("XS"), NONE)
+    fill(P("d0", 0, 3 * NB, 3), NONE)
 
-    HALVES = ((0, H), (H, NB))
-    NG = PAR["NG"]
-    Uo, Nc, Ur, FBp = P("p0", 0, NB), P("p0", NB, 2 * NB), P("p1", 0, NB), P("p1", NB, 2 * NB)
-    kH, kA, So = P("p2", 0, NB), P("p3", 0, NB), P("p3", NB, 2 * NB)
+    NG, DP = PAR["NG"], PAR["DP"]
+    Nc, FBp, kH = P("p3", NB, 2 * NB), P("p5", NB, 2 * NB), P("p2", 0, NB)
     res, Tp, nj = P("p4", 384, 396), P("p5", 0, NB, 1, 8), P("p5", NB, 2 * NB)
     Pl, taste, cnt = P("p6", 0, 12), P("p6", 12, 24), P("p6", 24, 25)
     dl = lambda a, b, s=1: P("p6", 32 + a, 32 + b, s)
@@ -353,48 +464,60 @@ def rank_program(g, core, T, topo):
     oVc, nbp = P("p7", 0, NB), P("p7", NB, 2 * NB)
     id12 = P("idb", 0, 12, 1, 12)
 
-    def offsets(t, names, pw, c0, q, sh, off):
-        for a, b in HALVES:
-            tt(P(q, a, b), P(names, a, b), P(pw, c0 + a, c0 + b), A.mult)
-            ts(P(sh, a, b), P(q, a, b), 5, A.logical_shift_right, W - 1, A.bitwise_and)
-            ts(P(off, a, b), P(sh, a, b), 77.0 * t, A.add)
+    def when(t, step, j=0):
+        now[0] = (t, step, j)
+
+    def offsets(t, names, pw, q, sh, off, a, b):
+        tt(P(q, a, b), P(names, a, b), P(pw, NB + a, NB + b), A.mult)
+        ts(P(sh, a, b), P(q, a, b), 5, A.logical_shift_right, W - 1, A.bitwise_and)
+        ts(P(off, a, b), P(sh, a, b), 77.0 * t, A.add)
 
     def looks(t, out, off):
         n = NB // NG
         for h in range(NG):
+            when(t, out, h)
             cp(P(out, 16 * n * h, 16 * n * h + 16 * n), IND(P("hx", 0, WX if t else W), P(off, n * h, n * h + n)), "va")
 
     def own_taste(t):
-        acc([const(P("p2", NB, 2 * NB), 1)] + to_rows("p2", NB, 2 * NB, "CLT", WW(t)))
+        acc([const(P("p1", NB, 2 * NB), 1)] + to_rows("p1", NB, 2 * NB, "CLT", WW(t)))
 
-    def keys(pk, row, src, dat, U, op):
-        for h in (0, 1):
-            for k in range(16):
-                tt(P3(dat, 6 * h, 6 * h + 6, k, 256, 16), P(src, 1536 * h + k, 1536 * h + 1536, 16), P(U[1], H * h, H * h + H), op)
-            out = P(pk[h], H * h, H * h + H)
-            acc([(out, P("blk"), P(row, 0, H))] + [(out, blk_("KL", i), P3(dat, 6 * h, 6 * h + 6, 16 * i, 16 * i + 16)) for i in range(16)])
+    def keys(t, pk, row, src, dat, rows, pu, op):
+        for p, (a, b) in enumerate(PAR[dat]):
+            when(t, dat, p)
+            out, U, c, d = P(pk, a, b), P(pu, a, b), a // 16, b // 16
+            mms([(U, P("idb"), P(rows, NB * t + a, NB * t + b))])
+            for k0 in range(0, 16, 2):
+                together(lambda k: tt(P3(dat, c, d, k, 256, 16), P(src, 16 * a + k, 16 * b, 16), U, op), (k0, k0 + 1))
+            acc([(out, P("blk"), P(row, a, b))] + [(out, blk_("KL", i), P3(dat, c, d, 16 * i, 16 * i + 16)) for i in range(16)])
 
+    when(0, "names")
     own_taste(0)
-    offsets(0, "o", "p2", NB, "q", "sh", "offH")
+    for a, b in DP:
+        offsets(0, "o", "p1", "q", "sh", "offH", a, b)
+    looks(0, "x", "offH")
+    when(0, "tables")
+    mms([(Nc, P("idh"), P("dm", 2, 2 + 3 * NB, 3))])
     for t in range(RO):
         host, guest = at(rank + away(t)), at(rank - away(t))
         b0, b1, a0 = NB * t, NB * t + NB, AM * t
         R = lambda n, a=0, b=NB: P(n, b0 + a, b0 + b)
         fin = t == RO - 1
         slot = lambda j, a=0, b=NB: P("dm", DM * t + 2 + j + 3 * a, DM * t + 2 + 3 * b, 3)
-        looks(t, "x", "offH")
-        for h in range(4):
-            scan(P("s", 768 * h, 768 * h + 768), P("m16"), P("x", 768 * h, 768 * h + 768), 0.0, A.mult, A.max)
-        BH = HALVES if PAR["BH"] == 2 else ((0, NB),)
-        for m, (a, b) in zip("Bb", BH):
+        n = S3 // PAR["NS"]
+        for h in range(PAR["NS"]):
+            when(t, "s", h)
+            scan(P("s", n * h, n * h + n), P("m16", 0, n), P("x", n * h, n * h + n), 0.0, A.mult, A.max)
+        for h, (m, (a, b)) in enumerate(zip("Bb", DP)):
+            when(t, "U", h)
             cp(R("Ub", a, b), P("s", 16 * a + 15, 16 * b, 16), "va")
             send(m, t, host, R("Ur", a, b), R("Ub", a, b))
+        when(t, "targets")
         gt = P("gt", 2, 36, 3)
         if t:
             recv("A", t, guest, P("ar", a0, a0 + 48))
             recv("F", t - 1, at(rank - away(t) + away(t - 1)), P("nbtn", b0 - NB, b0))
             mms([(dg(0, 36), P("idh"), P("ar", a0, a0 + 36))])
-            acc([const(dg(1, 36, 3), 2)] + to_list(dg(1, 36, 3), "RL", "nbtn", b0 - NB))
+            mms([to_list(dg(1, 36, 3), "nbtn", b0 - NB, P("g8s"), "p2", 256, "xn", 1.0, 3840.0)])
             lin(P("g0"), dg(0, 36), -2.0, 0.0)
             scan(P("gt"), P("g0"), dg(0, 36), 0.0, A.min, A.max)
             recv("P", t, guest, P("ar", a0 + 48, a0 + AM))
@@ -405,41 +528,41 @@ def rank_program(g, core, T, topo):
         cp(P("gth"), gt, "va")
         cp(P("oV"), IND(P("o"), P("tl")), "va")
         acc([const(P("p4", NB, 2 * NB), 1)] + to_rows("p4", NB, 2 * NB, "CLT", P("ar", a0 + 36, a0 + 48)))
-        offsets(t, "oV", "p4", NB, "q2", "sh2", "offA")
+        for a, b in PAR["AP"]:
+            offsets(t, "oV", "p4", "q2", "sh2", "offA", a, b)
         looks(t, "y", "offA")
-        mms(to_rows("p4", 0, NB, "CLT", P("gth")))
-        cp(P("tR"), P("p4", 0, NB), "va")
-        acc([(FBp, P("idb"), P("cbE"))] + to_rows("p1", NB, 2 * NB, "CLP", P("ar", a0 + 49, a0 + AM, 2)))
-        cp(P("FB"), FBp, "va")
+        when(t, "rows")
+        cp(P("tR"), IND(P("lane"), P("tl")), "va")
+        when(t, "loot")
         lin(oVc, P("oV"), 1.0, -2048.0)
         cp(P("nbV"), IND(P("nbb"), P("tl")), "va")
         mms([(nbp, P("idb"), P("nbV"))])
-        for a, b in BH:
-            mms([(P("p0", a, b), P("idb"), R("Ub", a, b))])
-        keys(("p2", "p2"), "kH", "x", "e", Uo, A.is_equal)
+        keys(t, "p2", "kH", "x", "e", "Ub", "p0", A.is_equal)
+        when(t, "j")
         scan(P("sc"), P("mH"), kH, 0.0, A.add, A.min)
         cp(P("jI", 0, 12), P("sc", 15, NB, 16))
         ts(P("jI", 12, 24), P("jI", 0, 12), 10, A.logical_shift_right, 15, A.bitwise_and)
         cp(P("jl"), P("jI", 12, 24))
         cp(P("OJ"), IND(P("Ej"), P("jl")), "va")
-        mms([(Nc, P("idh"), slot(0))])
         tt(R("JO"), P("OJ"), Nc, A.min)
         send("C", t, host, R("JOr"), R("JO"))
-        for m, (a, b) in zip("Bb", BH):
+        when(t, "first")
+        for m, (a, b) in zip("Bb", DP):
             recv(m, t, guest, R("Ur", a, b))
         tt(P("cmp"), IND(R("Ub"), P("tl")), R("Ur"), A.is_gt)
-        acc([const(res, 4)] + to_list(res, "RL", "cmp", 0))
+        mms([to_list(res, "cmp", 0, P("g8s"), "p5", 384, "xr", 1.0, 15.0 / 32)])
         left = [28]
         mms([(Tp, P("g8h"), P("cmp"))], True, left)
-        for c in range(12):
-            ts(P("G", 208 * c, NB * c + NB), P("tR", 16 * c, NB), P("gt", 2 + 3 * c, 3 + 3 * c), A.is_equal, P("p4", 384 + c, 385 + c), A.is_gt)
-            if c < 11:
-                mms([(P("p5", 16 * c + 16, NB, 1, 8), P("g32"), P("G", 208 * c + 16, NB * c + NB))], False, left)
-        mms([(P("p5", i, NB, 16, 8), P("TRI", 8 * i, 8 * i + 8), P("G", i, 12 * NB, 208)) for i in range(16)], False, left)
+        for cs in (range(0, 3), range(3, 7), range(7, 12)):
+            together(lambda c: ts(P("G", 208 * c, NB * c + NB), P("tR", 16 * c, NB), P("gt", 2 + 3 * c, 3 + 3 * c), A.is_equal,
+                                  P("p4", 384 + c, 385 + c), A.is_gt), cs)
+            mms([(P("p5", 16 * c + 16, NB, 1, 8), P("g32"), P("G", 208 * c + 16, NB * c + NB)) for c in cs if c < 11]
+                + [(P("p5", i, NB, 16, 8), P("TRI", 8 * i, 8 * i + 8), P("G", i, 12 * NB, 208)) for i in range(16) if 11 in cs], False, left)
         put("op", [("a", ac(NB) + 0.02, [lambda: Sc.activation(T.sg[:, :], Tp[0], F.Sign, bias=8.5, scale=-1.0, accum_out=T.acc[:, :])])],
             [Tp], [P("sg"), P("acc")])
-        acc([const(Pl, 3), (Pl, P("idh"), P("gth"))] + to_list(Pl, "SEL", "sg", 0, 8))
-        acc(to_list(taste, "WL", "Ub", b0))
+        acc([to_list(Pl, "sg", 0, P("idb", 0, 8, 1, 8), "p5", 384, "xs", 256.0, -64.0), (Pl, P("idh"), P("gth"))])
+        when(t, "taste")
+        mms([to_list(taste, "Ub", b0, P("g8w"), "p4", 0, "xw", 1.0, 0.0)])
         mms([(cnt, P("half"), P("acc"))])
         ts(P("uI", 0, 12), taste, cnt, A.add, 768.0, A.add)
         ts(P("uI", 12, 24), P("uI", 0, 12), 1023, A.bitwise_and)
@@ -448,6 +571,9 @@ def rank_program(g, core, T, topo):
         else:
             lin(WW(t + 1), P("uI", 12, 24), 2.0, -991.0, "v")
             own_taste(t + 1)
+        when(t, "victims")
+        acc([(FBp, P("idb"), P("cbE"))] + to_rows("p5", NB, 2 * NB, "CLP", P("ar", a0 + 49, a0 + AM, 2)))
+        cp(P("FB"), FBp, "va")
         tt(P("ovf"), Pl, P("cL"), A.max)
         cp(P("offV"), P("ovf"))
         cp(IND(P("Cw", b0, b1 + NB), P("offV")), P("FB"))
@@ -459,41 +585,46 @@ def rank_program(g, core, T, topo):
         if not fin:
             cp(P("am", a0 + AM, a0 + AM + 36), dl(48, 84), "va")
             send("A", t + 1, at(rank + away(t + 1)), P("ar", a0 + AM, a0 + AM + 48), P("am", a0 + AM, a0 + AM + 48))
-        for a, b in BH:
-            mms([(P("p1", a, b), P("idb"), R("Ur", a, b))])
-        keys(("p3", PAR["K2"]), "kA", "y", "z", Ur, A.max)
-        DH = HALVES if PAR["DH"] == 2 else ((0, NB),)
-        for m, (a, b) in zip("Dd", DH):
+        keys(t, "p3", "kA", "y", "z", "Ur", "p1", A.max)
+        for j, (m, (a, b)) in enumerate(zip("Dde", DP)):
+            when(t, "g", j)
             c, d = a // 16, b // 16
-            scan(P("sc2", a, b), P("mA", a, b), P("p3" if a == 0 else PAR["K2"], a, b), 0.0, A.mult, A.max)
+            scan(P("sc2", a, b), P("mA", a, b), P("p3", a, b), 0.0, A.mult, A.max)
             tt(P("gI", c, d), P("sc2", a + 15, b, 16), P("p6", c, d), A.add)
             ts(P("gI", 12 + c, 12 + d), P("gI", c, d), 9, A.logical_shift_right, 31, A.bitwise_and)
             cp(P("gl", c, d), P("gI", 12 + c, 12 + d))
             cp(P("OG", a, b), IND(P("Eg"), P("gl", c, d)), "va")
             tt(R("got", a, b), P("OG", a, b), P("p7", a, b), A.min)
             send(m, t, guest, R("gotr", a, b), R("got", a, b))
+        when(t, "nb")
         tt(R("nbt"), P("OG"), nbp, A.min)
         if not fin:
             send("F", t, at(rank - away(t) + away(t + 1)), R("nbtn"), R("nbt"))
         send("E", t, guest, R("nbtr"), R("nbt"))
+        when(t, "swap")
         recv("C", t, guest, R("JOr"))
         acc([const(nj, 0), (nj, P("blkH"), R("JOr"))])
         tt(P("XS", 1, NB + 1), P("OG"), nj, A.min)
         cp(slot(2), IND(P("XS"), P("thl")), "va")
         lin(P("d0", 2, 3 * NB, 3), slot(2), -2.0, -6144.0)
-        for m, (a, b) in zip("Dd", DH):
+        for j, (m, (a, b)) in enumerate(zip("Dde", DP)):
+            when(t + 1, "names", j)
             recv(m, t, host, R("gotr", a, b))
             acc([const(P("p3", NB + a, NB + b), 0), (P("p3", NB + a, NB + b), P("blkH"), R("gotr", a, b))])
-        for a, b in HALVES:
             tt(slot(1, a, b), P("OJ", a, b), P("p3", NB + a, NB + b), A.min)
             lin(P("d0", 1 + 3 * a, 3 * b, 3), slot(1, a, b), -2.0, -6144.0, "v")
             scan(P("dm", DM * (t + 1) + 3 * a, DM * (t + 1) + 3 * b), P("d0", 3 * a, 3 * b), P("dm", DM * t + 2 + 3 * a, DM * t + 2 + 3 * b),
                  0.0, A.min, A.max)
             lin(P("o", a, b), P("dm", DM * (t + 1) + 2 + 3 * a, DM * (t + 1) + 3 * b, 3), 1.0, 2048.0)
+            if not fin:
+                offsets(t + 1, "o", "p1", "q", "sh", "offH", a, b)
         if not fin:
-            offsets(t + 1, "o", "p2", NB, "q", "sh", "offH")
+            looks(t + 1, "x", "offH")
+            when(t + 1, "j")
+            mms([(Nc, P("idh"), P("dm", DM * (t + 1) + 2, DM * (t + 1) + 2 + 3 * NB, 3))])
+        when(t + 1, "lists")
         recv("E", t, host, R("nbtr"))
-        acc([const(dl(49, 84, 3), 2)] + to_list(dl(49, 84, 3), "RL", "nbtr", b0))
+        mms([to_list(dl(49, 84, 3), "nbtr", b0, P("g8s"), "p2", 384, "xm", 1.0, 3840.0)])
         lin(P("nm"), dl(49, 84, 3), 4.0, 192.0)
         tt(dl(25, 48, 2), P("nm"), TA(t), A.min)
         lin(P("l0"), dl(0, 84), -2.0, 0.0)
@@ -502,10 +633,10 @@ def rank_program(g, core, T, topo):
             send("P", t + 1, at(rank + away(t + 1)), P("ar", a0 + AM + 48, a0 + 2 * AM), P("st", ST * t + ST + 24, ST * t + ST + 48))
     dma("y", T.yo[:, :], T.o[:, :], "st0", [P("o")])
     turn = lambda pn, c0, c1, lst: mms([(P(pn, c0 + i, c1, 16, 8), P("CLT", 128 * i, 128 * i + 128, 16), lst) for i in range(16)])
-    turn("p0", 0, NB, WW(RO))
-    turn("p1", 0, 2 * NB, P("st", ST * RO + 1, ST * RO + 48, 2))
+    turn("p4", 0, NB, WW(RO))
+    turn("p7", 0, 2 * NB, P("st", ST * RO + 1, ST * RO + 48, 2))
     turn("p2", 0, NB, TA(RO))
-    for j, (out, pn, c0) in enumerate(((T.yu, "p0", 0), (T.yf, "p1", 0), (T.yp, "p1", NB), (T.yt, "p2", 0))):
+    for j, (out, pn, c0) in enumerate(((T.yu, "p4", 0), (T.yf, "p7", 0), (T.yp, "p7", NB), (T.yt, "p2", 0))):
         cp(P("o8", NB * j, NB * j + NB), P(pn, c0, c0 + NB, 1, 8), "va")
         dma("ya"[j % 2], out[:, :], T.o8[0:8, NB * j:NB * j + NB], "st%d" % (1 + j), [P("o8", NB * j, NB * j + NB)])
 
@@ -565,7 +696,7 @@ def rank_program(g, core, T, topo):
             note(q, rd, wr, (q, count[q]), dict(known[q]))
     for i in range(5):
         g.sync.wait_ge(T.sem["st%d" % i], 16)
-    for i in range(10):
+    for i in range(9):
         if known["v"].get("ld%d" % i, 0) < 16:
             g.vector.wait_ge(T.sem["ld%d" % i], 16)
     for s in ("v", "a", "p", "k"):

import math
import numpy as np
from concourse.mybir import AluOpType as A, ActivationFunctionType as F

NB, W, RO, N = 192, 4096, 5, 4
WX = 4416
S3 = 16 * NB
H = NB // 2
DM = 592
ST = 88
AM = 72
NONE = -4096.0

SCRATCH = {
    "hx": ("sbuf", [128, WX], "bfloat16"), "ownI": ("sbuf", [128, NB], "int32"), "nbI": ("sbuf", [128, NB], "int32"),
    "in4": ("sbuf", [8, 4 * NB], "int32"), "wtI": ("sbuf", [128, 1], "int32"), "in4h": ("sbuf", [8, 4 * NB], "float16"),
    "x48": ("sbuf", [48, 128], "float16"), "nbb": ("sbuf", [128, NB], "bfloat16"),
    "pI": ("sbuf", [128, 4], "int32"), "pF": ("sbuf", [128, 8], "float32"), "cg": ("sbuf", [128, 128], "float32"),
    "dif": ("sbuf", [128, 128], "float32"), "ia": ("sbuf", [128, 128], "float32"), "ib": ("sbuf", [128, 128], "float32"),
    "i32": ("sbuf", [128, 32], "float32"), "g16": ("sbuf", [128, 16], "float32"), "lane": ("sbuf", [128, NB], "float32"),
    "idb": ("sbuf", [128, 128], "bfloat16"), "idh": ("sbuf", [128, 128], "float16"), "blk": ("sbuf", [128, 128], "bfloat16"),
    "blkH": ("sbuf", [128, 128], "float16"), "g8h": ("sbuf", [128, 8], "float16"), "g8s": ("sbuf", [128, 8], "float16"),
    "g32": ("sbuf", [128, 8], "bfloat16"), "g01": ("sbuf", [128, 16], "bfloat16"), "TRI": ("sbuf", [128, 128], "bfloat16"),
    "CLT": ("sbuf", [128, 2048], "float16"), "CLP": ("sbuf", [128, 2048], "float16"), "KL": ("sbuf", [128, 2048], "bfloat16"),
    "g8w": ("sbuf", [128, 8], "bfloat16"), "idF": ("sbuf", [12, 12], "float32"),
    "xr": ("sbuf", [12, 128], "float16"), "xs": ("sbuf", [12, 128], "float16"), "xn": ("sbuf", [12, 128], "float16"),
    "xm": ("sbuf", [12, 128], "float16"), "xw": ("sbuf", [12, 128], "float32"),
    "cbE": ("sbuf", [128, NB], "bfloat16"), "cst": ("sbuf", [128, 2 * 256], "bfloat16"), "kH": ("sbuf", [128, NB], "bfloat16"),
    "kA": ("sbuf", [128, NB], "bfloat16"), "mH": ("sbuf", [128, NB], "float32"), "mA": ("sbuf", [128, NB], "float32"),
    "m16": ("sbuf", [128, 1024], "bfloat16"), "Ej": ("sbuf", [128, 16], "bfloat16"), "Eg": ("sbuf", [128, 32], "bfloat16"),
    "cL": ("sbuf", [128, 12], "float32"), "half": ("sbuf", [8, 128], "float32"),
    "dm": ("sbuf", [128, 6 * DM], "float16"), "st": ("sbuf", [128, 6 * ST], "float16"),
    "am": ("sbuf", [128, 6 * AM], "float16"), "ar": ("sbuf", [128, 5 * AM], "float16"),
    "Ub": ("sbuf", [128, 5 * NB], "bfloat16"), "Ur": ("sbuf", [128, 5 * NB], "bfloat16"),
    "JO": ("sbuf", [128, 5 * NB], "float16"), "JOr": ("sbuf", [128, 5 * NB], "float16"),
    "got": ("sbuf", [128, 5 * NB], "float16"), "gotr": ("sbuf", [128, 5 * NB], "float16"),
    "nbt": ("sbuf", [128, 5 * NB], "float16"), "nbtr": ("sbuf", [128, 5 * NB], "float16"), "nbtn": ("sbuf", [128, 5 * NB], "float16"),
    "Cw": ("sbuf", [128, 6 * NB], "bfloat16"),
    "o": ("sbuf", [128, NB], "float32"), "d0": ("sbuf", [128, 3 * NB], "bfloat16"),
    "q": ("sbuf", [128, NB], "int32"), "sh": ("sbuf", [128, NB], "int32"), "offH": ("sbuf", [128, NB], "uint16"),
    "q2": ("sbuf", [128, NB], "int32"), "sh2": ("sbuf", [128, NB], "int32"), "offA": ("sbuf", [128, NB], "uint16"),
    "x": ("sbuf", [128, S3], "bfloat16"), "s": ("sbuf", [128, S3], "bfloat16"), "y": ("sbuf", [128, S3], "bfloat16"),
    "e": ("sbuf", [128, 12, 256], "bfloat16"), "z": ("sbuf", [128, 12, 256], "bfloat16"),
    "sc": ("sbuf", [128, NB], "float32"), "sc2": ("sbuf", [128, NB], "float32"),
    "jI": ("sbuf", [128, 24], "int32"), "gI": ("sbuf", [128, 24], "int32"), "uI": ("sbuf", [128, 24], "int32"),
    "jl": ("sbuf", [128, 12], "uint16"), "gl": ("sbuf", [128, 12], "uint16"), "tl": ("sbuf", [128, 12], "uint16"),
    "offV": ("sbuf", [128, 12], "uint16"), "thl": ("sbuf", [128, 12], "uint16"), "ovf": ("sbuf", [128, 12], "float32"),
    "OJ": ("sbuf", [128, NB], "bfloat16"), "OG": ("sbuf", [128, NB], "bfloat16"),
    "oV": ("sbuf", [128, NB], "float32"), "nbV": ("sbuf", [128, NB], "bfloat16"),
    "tR": ("sbuf", [128, NB], "bfloat16"), "FB": ("sbuf", [128, NB], "bfloat16"), "G": ("sbuf", [128, 12 * NB], "bfloat16"),
    "cmp": ("sbuf", [128, NB], "float16"), "sg": ("sbuf", [8, NB], "bfloat16"), "acc": ("sbuf", [8, 1], "float32"),
    "xb": ("sbuf", [12, 256], "bfloat16"), "XS": ("sbuf", [128, 200], "float32"), "nm": ("sbuf", [128, 12], "float32"),
    "l0": ("sbuf", [128, 84], "float32"), "g0": ("sbuf", [128, 36], "float32"), "gt": ("sbuf", [128, 36], "float32"),
    "gth": ("sbuf", [128, 12], "float16"), "o8": ("sbuf", [8, 4 * NB], "float32"),
    "p0": ("psum", [128, 512], "float32"), "p1": ("psum", [128, 512], "float32"), "p2": ("psum", [128, 512], "float32"),
    "p3": ("psum", [128, 512], "float32"), "p4": ("psum", [128, 512], "float32"), "p5": ("psum", [128, 512], "float32"),
    "p6": ("psum", [128, 512], "float32"), "p7": ("psum", [128, 512], "float32"),
}
PS = ("p0", "p1", "p2", "p3", "p4", "p5", "p6", "p7")
TWO = ("bfloat16", "uint16", "float16")
MSG = ("A", "P", "B", "b", "C", "D", "d", "e", "E", "F")
SEMAPHORES = ["v", "a", "p", "k", "left"] + ["ld%d" % i for i in range(9)] + ["st%d" % i for i in range(5)] \
    + ["m%s%d" % (m, t) for m in MSG for t in range(RO)]
PAR = {"CYC": 0.00084, "PE": 0.00053, "LATE": 0.18, "FLY": 1.6, "VF": 0.012, "AF": 0.04, "HUE": 6.4, "FIRST": 3.2, "BIAS": 2.0,
       "STEPS": 12000, "SEED": 1, "PULL": 0.5, "HEAT": 0.15, "ROUND": 15.0, "CASES": ((0.22, -0.6, 0.85), (0.12, 0.3, 1.1)), "NG": 6,
       "DP": ((0, 96), (96, 192)), "AP": ((0, 192),), "e": ((0, 96), (96, 192)), "z": ((0, 96), (96, 192)), "NS": 4}
WHEN = {"start": (-72.1, 0), "tables": (27.4, 0), "names": (13.8, 1.9), "x": (30.7, 2.9), "s": (42.3, 13.7), "U": (-5.6, 35.6),
        "targets": (12.4, 0), "lists": (50.2, 0), "y": (-1.6, 2.8), "rows": (20.3, 0), "loot": (55.7, 0), "e": (13.6, 9.9),
        "j": (2.3, 0), "first": (10.3, 0), "taste": (17.6, 0), "victims": (14.3, 0), "z": (36.4, 22.8), "g": (4.1, 5.7),
        "nb": (6.9, 0), "swap": (34.6, 0)}
PLAN = []


def place(ops, before, rank):
    n = len(ops)
    start, end, queue, busy, late = [0.0] * n, [0.0] * n, [None] * n, {}, PAR["LATE"]
    for i in sorted(range(n), key=lambda i: rank[i]):
        o, best = ops[i], None
        r = max([end[j] + ops[j]["late"] for j in before[i]] + [0.0])
        for q, c in o["alt"]:
            held = [z[:2] for z in busy.get(q, ()) if z[1] > r]
            for b in o["banks"]:
                held += [(a - late, e + late) for a, e, q2 in busy.get(b, ()) if q2 != q and e + late > r]
            t0 = r
            for a, e in sorted(held):
                if a >= t0 + c:
                    break
                t0 = max(t0, e)
            z = t0 + c + (PAR["BIAS"] * c if q == "v" else 0.0)
            if best is None or z < best[0]:
                best = (z, t0, c, q)
        _, start[i], c, queue[i] = best
        end[i] = start[i] + c
        for b in [queue[i]] + o["banks"]:
            busy.setdefault(b, []).append((start[i], end[i], queue[i]))
    return start, end, queue


def order(ops):
    n = len(ops)
    pred = [sorted(o["deps"]) for o in ops]
    succ = [[] for _ in ops]
    for i in range(n):
        for d in pred[i]:
            succ[d].append(i)
    due = [0.0] * n
    for i in range(n - 1, -1, -1):
        t, step, j = ops[i]["when"]
        way = min(c for _, c in ops[i]["alt"]) + ops[i]["late"]
        due[i] = min([PAR["ROUND"] * t + WHEN[step][0] + WHEN[step][1] * j] + [due[d] - way for d in succ[i]])
    start, end, queue = place(ops, pred, [(due[i], i) for i in range(n)])
    PAR["SPAN"] = max(end[i] + ops[i]["late"] for i in range(n))
    return shorten(ops, pred, succ, sorted(range(n), key=lambda i: (start[i], i)), queue)


def shorten(ops, pred, succ, seq, queue):
    n = len(ops)
    lag = [o["late"] for o in ops]
    cost = [dict(o["alt"]) for o in ops]
    alike, seen = {}, {}
    for i, o in enumerate(ops):
        k = o["when"][1:] + ((o["writes"] or o["reads"])[0][1],)
        seen[(o["when"][0], k)] = seen.get((o["when"][0], k), 0) + 1
        alike.setdefault(k + (seen[(o["when"][0], k)],), []).append(i)
    alike = {i: {ops[j]["when"][0] - ops[i]["when"][0]: j for j in v} for v in alike.values() for i in v}
    sends = [i for i in range(n) if ops[i]["kind"] == "send"]

    cases = [(late, [late if o["kind"] == "op" else o["late"] + fly * (o["kind"] == "send") for o in ops],
              [{q: c * (pe if q == "p" else 1.0) for q, c in o["alt"]} for o in ops]) for late, fly, pe in PAR["CASES"]]

    def run(seq, queue, pick=0):
        both = [one(seq, queue, *case) for case in cases]
        return (sum(z[0] for z in both) / len(both),) + both[pick][1:]

    def one(seq, queue, late, lag, cost):
        end, by, on = [0.0] * n, [None] * n, {}
        for i in seq:
            r, b, q = 0.0, None, queue[i]
            for d in pred[i]:
                if end[d] + lag[d] > r:
                    r, b = end[d] + lag[d], (d, False)
            d = on.get(q)
            if d is not None and end[d] > r:
                r, b = end[d], (d, True)
            on[q] = i
            for bank in ops[i]["banks"]:
                last = on.setdefault(bank, {})
                for q2, d in last.items():
                    if q2 != q and end[d] + late > r:
                        r, b = end[d] + late, (d, True)
                last[q] = i
            end[i], by[i] = r + cost[i][q], b
        tip = max(range(n), key=lambda i: end[i] + lag[i])
        return end[tip] + lag[tip] + PAR["PULL"] * sum(end[i] for i in sends) / len(sends), end, by, tip, seq, queue

    def swap(seq, a, b, forward):
        pa, pb = seq.index(a), seq.index(b)
        if pa > pb:
            return seq
        part = seq[pa:pb + 1]
        near, go = (pred, {a}) if forward else (succ, {b})
        for i in (part if forward else part[::-1]):
            if any(d in go for d in near[i]):
                go.add(i)
        if a in go and b in go:
            return seq
        return seq[:pa] + [i for i in part if (i in go) != forward] + [i for i in part if (i in go) == forward] + seq[pb + 1:]

    rng = np.random.default_rng(PAR["SEED"])
    cur = best = run(seq, queue)
    for step in range(PAR["STEPS"]):
        u = rng.random(6)
        i = cur[3] if u[0] < 0.5 else sends[int(u[1] * len(sends))]
        lo, way = (cur[1][i] - 12.0 if u[0] >= 0.5 else -1.0), []
        while cur[2][i] is not None and cur[1][i] > lo:
            way.append(i)
            i = cur[2][i][0]
        seq, queue = cur[4], cur[5]
        if u[2] < 0.15:
            way = [i for i in way if len(cost[i]) > 1]
            if way:
                i, queue = way[int(u[3] * len(way))], list(queue)
                other = [q for q in cost[i] if q != queue[i]][0]
                for j in (alike[i].values() if u[4] < 0.7 else [i]):
                    queue[j] = other
        else:
            way = [i for i in way if cur[2][i][1]]
            if way:
                b = way[int(u[3] * len(way))]
                a = cur[2][b][0]
                for d in (alike[a] if u[4] < 0.7 else [0]):
                    if d in alike[b]:
                        seq = swap(seq, alike[a][d], alike[b][d], u[2] < 0.55)
        new = run(seq, queue, step % len(cases))
        if new[0] - cur[0] <= -math.log(u[5]) * PAR["HEAT"] * (1.0 - step / PAR["STEPS"]):
            cur = new
            if cur[0] < best[0]:
                best = cur
    PAR["SHORT"] = best[1][best[3]] + lag[best[3]]
    return [(0.0, i, best[5][i]) for i in best[4]]


def rank_program(g, core, T, topo):
    rank = T.rank_of(core)
    if rank is None:
        return
    queues = {"v": g.vector, "a": g.scalar, "p": g.tensor, "k": g, "y": g.sync}
    ops, bundle, last, sent, group, now = [], [], {}, {}, {}, [(0, "start", 0)]
    CYC, VF = PAR["CYC"], PAR["VF"]

    def P(name, c0=0, c1=None, step=1, p=128):
        b = T[name]
        c1 = b.shape[1] if c1 is None else c1
        p = min(p, b.shape[0])
        return (b[0:p, c0:c1:step] if step > 1 else b[0:p, c0:c1], name, c0, c1, (c1 - c0 + step - 1) // step, step)

    def P3(name, c0, c1, a, b, step=1):
        return (T[name][:, c0:c1, a:b:step], name, 256 * c0 + a, 256 * c1, (c1 - c0) * ((b - a + step - 1) // step), step)

    def IND(win, off):
        return (win[0].indirect(off[0]), win, off)

    def flat(xs):
        out = []
        for x in xs:
            out += [x[1], x[2]] if len(x) == 3 else [x]
        return out

    meet = lambda a, b: a[2] < b[3] and b[2] < a[3] and (a[5] != b[5] or (a[2] - b[2]) % a[5] == 0)
    cover = lambda a, b: a[2] <= b[2] and b[3] <= a[3] and (a[5] == 1 or (a[5] == b[5] and (a[2] - b[2]) % a[5] == 0))

    def put(kind, alt, reads, writes, late=None, loose=(), **more):
        if bundle:
            bundle.append((alt[0], reads, writes))
            return None
        reads, writes = flat(reads), flat(writes)
        i, deps = len(ops), set()
        for lst, wr in ((reads, False), (writes, True)):
            for r in lst:
                for (z, w, j) in last.get(r[1], ()):
                    if (wr or w) and meet(r, z) and j not in loose:
                        deps.add(j)
        for lst, wr in ((reads, False), (writes, True)):
            for r in lst:
                h = last.setdefault(r[1], [])
                if wr and not loose:
                    h[:] = [z for z in h if not cover(r, z[0])]
                h.append((r, wr, i))
        deps.discard(i)
        banks = sorted(set(r[1] for r in reads + writes if r[1] in PS))
        o = {"kind": kind, "alt": [(q, c) for q, c, _ in alt], "fns": {q: f for q, _, f in alt}, "reads": reads, "writes": writes,
             "deps": deps, "banks": banks, "late": PAR["LATE"] if late is None else late, "when": now[0]}
        o.update(more)
        ops.append(o)
        return i

    def together(call, js):
        bundle.append(None)
        for j in js:
            call(j)
        all_ = bundle[1:]
        del bundle[:]
        put("op", [("v", sum(z[0][1] for z in all_), [f for z in all_ for f in z[0][2]])], [r for z in all_ for r in z[1]], [r for z in all_ for r in z[2]])

    V, Sc, Te = g.vector, g.scalar, g.tensor
    dts = lambda x: SCRATCH[(x[1] if len(x) == 3 else x)[1]][2]
    two = lambda xs: all(dts(x) in TWO for x in xs)
    vc = lambda n, cyc=1.0: (0.05 if cyc in (1.5, 3.5) else VF) + max(64, n * cyc) * CYC
    ac = lambda n, cyc=1.0: (0.065 if cyc == 1.5 else PAR["AF"]) + max(64, n * cyc) * CYC
    size = lambda x: 16 * (x[2][3] - x[2][2]) if len(x) == 3 else x[4]
    col = lambda s: s[0] if isinstance(s, tuple) else s

    def cp(out, in_, qs="v"):
        alt = []
        gat, sca = len(in_) == 3, len(out) == 3
        n = size(in_)
        if "v" in qs:
            alt.append(("v", vc(n, 1.5 if gat else 3.5 if sca else 0.5 if two([out, in_]) else 1.0), [lambda: V.tensor_copy(out[0], in_[0])]))
        if "a" in qs:
            alt.append(("a", ac(n, 1.5 if gat else 1.0), [lambda: Sc.activation(out[0], in_[0], F.Copy)]))
        put("op", alt, [in_], [out])

    def lin(out, in_, m, b, qs="va"):
        gat = len(in_) == 3
        alt = [("v", vc(size(out), 1.5 if gat else 0.5 if two([out, in_]) else 1.0), [lambda: V.tensor_scalar(out[0], in_[0], col(m), b, A.mult, A.add)]),
               ("a", ac(size(out), 1.5 if gat else 1.0), [lambda: Sc.activation(out[0], in_[0], F.Identity, bias=b, scale=col(m))])]
        put("op", [z for z in alt if z[0] in qs], [in_] + ([m] if isinstance(m, tuple) else []), [out])

    def tt(out, a, b, o):
        c = 1.5 if len(a) == 3 else 1.0 if a[1] in PS or b[1] in PS else 2.0
        put("op", [("v", vc(size(out), c), [lambda: V.tensor_tensor(out[0], a[0], b[0], o)])], [a, b], [out])

    def ts(out, a, s1, o1, s2=None, o2=None):
        rs = [a] + [s for s in (s1, s2) if isinstance(s, tuple)]
        if o2 is None:
            f = lambda: V.tensor_scalar(out[0], a[0], col(s1), None, o1)
        else:
            f = lambda: V.tensor_scalar(out[0], a[0], col(s1), col(s2), o1, o2)
        put("op", [("v", vc(size(out), 0.5 if two([out, a]) else 1.0), [f])], rs, [out])

    def ms(out, c):
        put("op", [("v", vc(size(out), 0.5 if two([out]) else 1.0), [lambda: V.memset(out[0], c)])], [], [out])

    def fill(out, c):
        src = P("CLT", 0, out[4], 1, T[out[1]].shape[0])
        put("op", [("v", vc(size(out), 0.5 if two([out]) else 1.0), [lambda: V.memset(out[0], c)]),
                   ("a", ac(size(out)), [lambda: Sc.activation(out[0], src[0], F.Identity, bias=c, scale=0.0)])], [src], [out])

    def scan(out, d0, d1, init, o0, o1):
        put("op", [("v", vc(size(out), 0.5 if two([out, d0, d1]) else 1.0),
                    [lambda: V.tensor_tensor_scan(out[0], d0[0], d1[0], init, o0, o1)])], [d0, d1], [out])

    def closes(n):
        n[0] -= 1
        return n[0] == 0

    def mms(lst, first=True, left=None):
        c = sum((max(64, z[2][4]) * PAR["PE"]) * (4 if dts(z[2]) == "float32" else 1) for z in lst)
        fns = []
        for j, z in enumerate(lst):
            if left is None:
                fns.append(lambda z=z: Te.matmul(z[0][0], z[1][0], z[2][0], *(z[3:] or (True, True))))
            else:
                fns.append(lambda z=z, j=j: Te.matmul(z[0][0], z[1][0], z[2][0], first and j == 0, closes(left)))
        rd, wr = {}, {}
        for z in lst:
            for x, d in ((z[1], rd), (z[2], rd), (z[0], wr)):
                y = d.get(x[1], x)
                d[x[1]] = x if cover(x, y) else (None, x[1], min(x[2], y[2]), max(x[3], y[3]), 0, 1)
        bank = lst[0][0][1]
        mark = [(None, "group", 0, 1, 0, 1)] if bank == "p5" else []
        if first:
            i = put("op", [("p", c, fns)], list(rd.values()), list(wr.values()) + mark)
            group[bank] = []
        else:
            i = put("op", [("p", c, fns)], list(rd.values()) + mark, list(wr.values()), loose=group[bank])
            group[bank].append(i)

    def acc(lst):
        mms([z + (j == 0, j == len(lst) - 1) for j, z in enumerate(lst)])

    def iota(out, pattern, base, cmul, flag=True):
        if flag:
            f = lambda: g.iota(out[0], pattern, base, cmul, allow_small_or_imprecise_dtypes=True)
        else:
            f = lambda: g.iota(out[0], pattern, base, cmul)
        put("op", [("k", 0.15 + 2 * size(out) * CYC, [f])], [], [out])

    def dma(q, out, in_, sem, reads=(), writes=(), late=2.2):
        put("dma", [(q, 0.1, [lambda: queues[q].dma_start(out, in_)])], list(reads), list(writes), late, sem=sem)

    def send(msg, t, dst, out, in_):
        sent[(msg, t)] = put("send", [("k", 0.6, None)], [in_], [], PAR["FLY"] + 0.00133 * in_[4] * 2 + (0 if sent else PAR["FIRST"]),
                             args=(msg, t, dst, out, in_))

    def recv(msg, t, src, buf):
        i = put("recv", [("r%s%d" % (msg, t), 0.001, None)], [], [buf], 0.0, args=(msg, t, src, buf))
        ops[i]["deps"].add(sent[(msg, t)])

    blk_ = lambda m, i, p=128: P(m, 128 * i, 128 * i + 128, 1, p)

    def to_list(out, src, c0, sel, pn, pc, x, m, b):
        mms([(P(pn, pc + i, pc + 128, 16, 12), P(src, c0 + i, c0 + NB, 16), sel) for i in range(16)])
        lin(P(x), P(pn, pc, pc + 128, 1, 12), m, b)
        return (out, P(x), P({"float16": "idh", "bfloat16": "idb", "float32": "idF"}[SCRATCH[x][2]], 0, 12, 1, 12))

    to_rows = lambda pn, c0, c1, m, lst: [(P(pn, c0 + i, c1, 16), blk_(m, i), lst) for i in range(16)]
    const = lambda out, j: (out, P("blk"), P("cst", 256 * j, 256 * j + out[4]))
    CONST = ((3840.0, NB), (64.0, NB))
    away = lambda t: 1 + t % (N - 1)
    at = lambda r: T.cores[r % N]

    for j, (q, src) in enumerate((("a", T.tau), ("a", T.prev), ("a", T.foe), ("y", T.tas))):
        dma(q, T.in4[0:8, NB * j:NB * j + NB], src[:, :], "ld%d" % j, [], [P("in4", NB * j, NB * j + NB)])
    dma("y", T.ownI[:, :], T.own[:, :], "ld4", [], [P("ownI")])
    dma("y", T.hx[:, 0:W], T.hue[:, :], "ld5", [], [P("hx", 0, W)], PAR["HUE"])
    dma("a", T.wtI[:, :], T.wt[:, :], "ld6", [], [P("wtI")])
    dma("a", T.nbI[:, :], T.nb[:, :], "ld7", [], [P("nbI")])
    dma("y", T.hx[:, W:WX], T.hue[:, 0:WX - W], "ld8", [], [P("hx", W, WX)])

    PI = lambda j: P("pI", j, j + 1)
    PF = lambda j: P("pF", j, j + 1)
    iota(PI(0), [[0, 1]], 0, 1, False)
    iota(P("dif"), [[1, 128]], 0, -1)
    iota(P("cg"), [[1, 8], [0, 16]], 0, 0)
    iota(P("i32"), [[1, 32]], 0, 0)
    iota(P("ia"), [[0, 16], [1, 8]], 0, 0)
    iota(P("ib"), [[1, 16], [0, 8]], 0, 0)
    iota(P("cL"), [[16, 12]], 0, 0)
    iota(P("lane"), [[1, NB]], 0, 0)
    iota(P("kH"), [[0, 12], [64, 16]], 0, 0)
    iota(P("kA"), [[0, 12], [-64, 16]], 980, 0)
    ts(PI(1), PI(0), 4, A.logical_shift_right)
    ts(PI(2), PI(0), 15, A.bitwise_and)
    cp(P("pF", 0, 3), P("pI", 0, 3))
    ts(P("idh"), P("dif"), 0.0, A.is_equal)
    ts(P("blkH"), P("cg"), PF(1), A.is_equal)
    ts(P("g16"), P("i32", 0, 16), PF(2), A.is_equal)
    ms(P("am", 0, AM), 0.0)
    cp(P("in4h"), P("in4"))
    mms([(P("p6", i, 128, 16, 48), P("in4h", i, 4 * NB, 16), P("idh", 0, 8, 1, 8)) for i in range(16)])
    cp(P("x48"), P("p6", 0, 128, 1, 48))
    mms([(P("p6", 128, 176), P("x48"), P("idh", 0, 48, 1, 48))])
    FO, PR, TA = [lambda t, a=a, b=b, s=s: P("st", ST * t + a, ST * t + b, s) for a, b, s in ((1, 24, 2), (25, 48, 2), (50, 84, 3))]
    WW = lambda t: P("am", AM * t + 36, AM * t + 48)
    lin(WW(0), P("p6", 164, 176), 2.0, -991.0, "v")
    cp(P("am", 2, 36, 3), P("p6", 128, 140))
    cp(P("am", 49, 72, 2), P("p6", 140, 152))
    send("A", 0, at(rank + 1), P("ar", 0, AM), P("am", 0, AM))
    cp(TA(0), P("p6", 128, 140), "va")
    cp(PR(0), P("p6", 140, 152), "va")
    cp(FO(0), P("p6", 152, 164), "va")
    for i0 in range(0, 16, 4):
        together(lambda i: ts(blk_("CLT", i), P("blkH"), P("g16", i, i + 1), A.mult), range(i0, i0 + 4))
    cp(P("blk"), P("blkH"))
    cp(P("idb"), P("idh"))
    for j, (c, n) in enumerate(CONST):
        ms(P("cst", 256 * j, 256 * j + n), c)
    cp(P("o"), P("ownI"))
    lin(P("dm", 2, 3 * NB, 3), P("ownI"), 1.0, -2048.0, "v")
    ms(P("m16"), 1.0)
    ms(P("m16", 0, 1024, 16), 0.0)
    now[0] = (0, "tables", 0)
    ts(P("g8h"), P("i32", 0, 8), PF(1), A.is_equal)
    ts(P("g8s"), P("i32", 0, 8), PF(1), A.is_equal, 1.0 / 16, A.mult)
    ts(P("g32"), P("i32", 0, 8), PF(1), A.is_equal, 32.0, A.mult)
    for f in range(2):
        ts(P("g01", 8 * f, 8 * f + 8), P("i32", 0, 8), PF(1), A.is_equal, P("g16", f, f + 1), A.mult)
    for j in range(4):
        mms([(P("p%d" % (j % 2), 128 * i, 128 * i + 128), blk_("CLT", 4 * j + i), P("idh")) for i in range(4)])
        lin(P("KL", 512 * j, 512 * j + 512), P("p%d" % (j % 2)), 16384.0, 0.0)
    cp(PF(3), P("wtI"))
    ts(P("g8w"), P("i32", 0, 8), PF(1), A.is_equal, PF(3), A.mult)
    ts(P("idF"), P("dif", 0, 12, 1, 12), 0.0, A.is_equal)
    fill(P("CLP"), 0.0)
    cp(P("CLP", 1, 2048, 16), P("CLT", 1, 2048, 16))
    ts(P("ia"), P("ia"), PF(1), A.is_equal, 32.0, A.mult)
    ts(P("ib"), P("ib"), PF(2), A.is_gt)
    tt(P("TRI"), P("ia"), P("ib"), A.mult)
    ts(P("cbE"), P("lane"), P("g16", 0, 1), A.mult)
    ts(P("cL"), P("cL"), PF(2), A.add)
    lin(P("nbb"), P("nbI"), 16.0, 0.0, "v")
    fill(P("mA"), 1.0)
    fill(P("mA", 0, NB, 16), 0.0)
    fill(P("mH"), 0.0)
    fill(P("mH", 0, NB, 16), 1e9)

    lin(P("Ej"), P("g16"), 8192.0, NONE, "v")
    lin(PF(4), PF(2), -2.0, 31.0, "v")
    ts(P("Eg"), P("i32"), PF(4), A.is_equal, 8192.0, A.mult)
    ts(P("Eg"), P("Eg"), NONE, A.add)
    fill(P("half"), 0.5)
    for t in range(RO):
        fill(P("Cw", NB * t + NB, NB * t + 2 * NB), NONE)
    fill(P("XS"), NONE)
    fill(P("d0", 0, 3 * NB, 3), NONE)

    NG, DP = PAR["NG"], PAR["DP"]
    Nc, FBp, kH = P("p3", NB, 2 * NB), P("p5", NB, 2 * NB), P("p2", 0, NB)
    res, Tp, nj = P("p4", 384, 396), P("p5", 0, NB, 1, 8), P("p5", NB, 2 * NB)
    Pl, taste, cnt = P("p6", 0, 12), P("p6", 12, 24), P("p6", 24, 25)
    dl = lambda a, b, s=1: P("p6", 32 + a, 32 + b, s)
    dg = lambda a, b, s=1: P("p4", 400 + a, 400 + b, s)
    oVc, nbp = P("p7", 0, NB), P("p7", NB, 2 * NB)
    id12 = P("idb", 0, 12, 1, 12)

    def when(t, step, j=0):
        now[0] = (t, step, j)

    def offsets(t, names, pw, q, sh, off, a, b):
        tt(P(q, a, b), P(names, a, b), P(pw, NB + a, NB + b), A.mult)
        ts(P(sh, a, b), P(q, a, b), 5, A.logical_shift_right, W - 1, A.bitwise_and)
        ts(P(off, a, b), P(sh, a, b), 77.0 * t, A.add)

    def looks(t, out, off):
        n = NB // NG
        for h in range(NG):
            when(t, out, h)
            cp(P(out, 16 * n * h, 16 * n * h + 16 * n), IND(P("hx", 0, WX if t else W), P(off, n * h, n * h + n)), "va")

    def own_taste(t):
        acc([const(P("p1", NB, 2 * NB), 1)] + to_rows("p1", NB, 2 * NB, "CLT", WW(t)))

    def keys(t, pk, row, src, dat, rows, pu, op):
        for p, (a, b) in enumerate(PAR[dat]):
            when(t, dat, p)
            out, U, c, d = P(pk, a, b), P(pu, a, b), a // 16, b // 16
            mms([(U, P("idb"), P(rows, NB * t + a, NB * t + b))])
            for k0 in range(0, 16, 2):
                together(lambda k: tt(P3(dat, c, d, k, 256, 16), P(src, 16 * a + k, 16 * b, 16), U, op), (k0, k0 + 1))
            acc([(out, P("blk"), P(row, a, b))] + [(out, blk_("KL", i), P3(dat, c, d, 16 * i, 16 * i + 16)) for i in range(16)])

    when(0, "names")
    own_taste(0)
    for a, b in DP:
        offsets(0, "o", "p1", "q", "sh", "offH", a, b)
    looks(0, "x", "offH")
    when(0, "tables")
    mms([(Nc, P("idh"), P("dm", 2, 2 + 3 * NB, 3))])
    for t in range(RO):
        host, guest = at(rank + away(t)), at(rank - away(t))
        b0, b1, a0 = NB * t, NB * t + NB, AM * t
        R = lambda n, a=0, b=NB: P(n, b0 + a, b0 + b)
        fin = t == RO - 1
        slot = lambda j, a=0, b=NB: P("dm", DM * t + 2 + j + 3 * a, DM * t + 2 + 3 * b, 3)
        n = S3 // PAR["NS"]
        for h in range(PAR["NS"]):
            when(t, "s", h)
            scan(P("s", n * h, n * h + n), P("m16", 0, n), P("x", n * h, n * h + n), 0.0, A.mult, A.max)
        for h, (m, (a, b)) in enumerate(zip("Bb", DP)):
            when(t, "U", h)
            cp(R("Ub", a, b), P("s", 16 * a + 15, 16 * b, 16), "va")
            send(m, t, host, R("Ur", a, b), R("Ub", a, b))
        when(t, "targets")
        gt = P("gt", 2, 36, 3)
        if t:
            recv("A", t, guest, P("ar", a0, a0 + 48))
            recv("F", t - 1, at(rank - away(t) + away(t - 1)), P("nbtn", b0 - NB, b0))
            mms([(dg(0, 36), P("idh"), P("ar", a0, a0 + 36))])
            mms([to_list(dg(1, 36, 3), "nbtn", b0 - NB, P("g8s"), "p2", 256, "xn", 1.0, 3840.0)])
            lin(P("g0"), dg(0, 36), -2.0, 0.0)
            scan(P("gt"), P("g0"), dg(0, 36), 0.0, A.min, A.max)
            recv("P", t, guest, P("ar", a0 + 48, a0 + AM))
        else:
            recv("A", t, guest, P("ar", 0, AM))
            cp(gt, P("ar", 2, 36, 3))
        cp(P("tl"), gt)
        cp(P("gth"), gt, "va")
        cp(P("oV"), IND(P("o"), P("tl")), "va")
        acc([const(P("p4", NB, 2 * NB), 1)] + to_rows("p4", NB, 2 * NB, "CLT", P("ar", a0 + 36, a0 + 48)))
        for a, b in PAR["AP"]:
            offsets(t, "oV", "p4", "q2", "sh2", "offA", a, b)
        looks(t, "y", "offA")
        when(t, "rows")
        cp(P("tR"), IND(P("lane"), P("tl")), "va")
        when(t, "loot")
        lin(oVc, P("oV"), 1.0, -2048.0)
        cp(P("nbV"), IND(P("nbb"), P("tl")), "va")
        mms([(nbp, P("idb"), P("nbV"))])
        keys(t, "p2", "kH", "x", "e", "Ub", "p0", A.is_equal)
        when(t, "j")
        scan(P("sc"), P("mH"), kH, 0.0, A.add, A.min)
        cp(P("jI", 0, 12), P("sc", 15, NB, 16))
        ts(P("jI", 12, 24), P("jI", 0, 12), 10, A.logical_shift_right, 15, A.bitwise_and)
        cp(P("jl"), P("jI", 12, 24))
        cp(P("OJ"), IND(P("Ej"), P("jl")), "va")
        tt(R("JO"), P("OJ"), Nc, A.min)
        send("C", t, host, R("JOr"), R("JO"))
        when(t, "first")
        for m, (a, b) in zip("Bb", DP):
            recv(m, t, guest, R("Ur", a, b))
        tt(P("cmp"), IND(R("Ub"), P("tl")), R("Ur"), A.is_gt)
        mms([to_list(res, "cmp", 0, P("g8s"), "p5", 384, "xr", 1.0, 15.0 / 32)])
        left = [28]
        mms([(Tp, P("g8h"), P("cmp"))], True, left)
        for cs in (range(0, 3), range(3, 7), range(7, 12)):
            together(lambda c: ts(P("G", 208 * c, NB * c + NB), P("tR", 16 * c, NB), P("gt", 2 + 3 * c, 3 + 3 * c), A.is_equal,
                                  P("p4", 384 + c, 385 + c), A.is_gt), cs)
            mms([(P("p5", 16 * c + 16, NB, 1, 8), P("g32"), P("G", 208 * c + 16, NB * c + NB)) for c in cs if c < 11]
                + [(P("p5", i, NB, 16, 8), P("TRI", 8 * i, 8 * i + 8), P("G", i, 12 * NB, 208)) for i in range(16) if 11 in cs], False, left)
        put("op", [("a", ac(NB) + 0.02, [lambda: Sc.activation(T.sg[:, :], Tp[0], F.Sign, bias=8.5, scale=-1.0, accum_out=T.acc[:, :])])],
            [Tp], [P("sg"), P("acc")])
        acc([to_list(Pl, "sg", 0, P("idb", 0, 8, 1, 8), "p5", 384, "xs", 256.0, -64.0), (Pl, P("idh"), P("gth"))])
        when(t, "taste")
        mms([to_list(taste, "Ub", b0, P("g8w"), "p4", 0, "xw", 1.0, 0.0)])
        mms([(cnt, P("half"), P("acc"))])
        ts(P("uI", 0, 12), taste, cnt, A.add, 768.0, A.add)
        ts(P("uI", 12, 24), P("uI", 0, 12), 1023, A.bitwise_and)
        if fin:
            cp(WW(t + 1), P("uI", 12, 24))
        else:
            lin(WW(t + 1), P("uI", 12, 24), 2.0, -991.0, "v")
            own_taste(t + 1)
        when(t, "victims")
        acc([(FBp, P("idb"), P("cbE"))] + to_rows("p5", NB, 2 * NB, "CLP", P("ar", a0 + 49, a0 + AM, 2)))
        cp(P("FB"), FBp, "va")
        tt(P("ovf"), Pl, P("cL"), A.max)
        cp(P("offV"), P("ovf"))
        cp(IND(P("Cw", b0, b1 + NB), P("offV")), P("FB"))
        mms([(P("p6", 128 + i, 384, 16, 12), P("Cw", b1 + i, b1 + NB, 16), P("g01")) for i in range(16)])
        cp(P("xb"), P("p6", 128, 384, 1, 12), "va")
        mms([(dl(1, 24, 2), P("xb", 0, 128), id12), (dl(50, 84, 3), P("xb", 128, 256), id12), (dl(0, 24, 2), P("idh"), FO(t)),
             (dl(24, 48, 2), P("idh"), PR(t)), (dl(48, 84, 3), P("idh"), FO(t)), (dl(49, 84, 3), P("idh"), FO(t))])
        ts(P("thl"), dl(1, 24, 2), 1.0, A.add)
        if not fin:
            cp(P("am", a0 + AM, a0 + AM + 36), dl(48, 84), "va")
            send("A", t + 1, at(rank + away(t + 1)), P("ar", a0 + AM, a0 + AM + 48), P("am", a0 + AM, a0 + AM + 48))
        keys(t, "p3", "kA", "y", "z", "Ur", "p1", A.max)
        for j, (m, (a, b)) in enumerate(zip("Dde", DP)):
            when(t, "g", j)
            c, d = a // 16, b // 16
            scan(P("sc2", a, b), P("mA", a, b), P("p3", a, b), 0.0, A.mult, A.max)
            tt(P("gI", c, d), P("sc2", a + 15, b, 16), P("p6", c, d), A.add)
            ts(P("gI", 12 + c, 12 + d), P("gI", c, d), 9, A.logical_shift_right, 31, A.bitwise_and)
            cp(P("gl", c, d), P("gI", 12 + c, 12 + d))
            cp(P("OG", a, b), IND(P("Eg"), P("gl", c, d)), "va")
            tt(R("got", a, b), P("OG", a, b), P("p7", a, b), A.min)
            send(m, t, guest, R("gotr", a, b), R("got", a, b))
        when(t, "nb")
        tt(R("nbt"), P("OG"), nbp, A.min)
        if not fin:
            send("F", t, at(rank - away(t) + away(t + 1)), R("nbtn"), R("nbt"))
        send("E", t, guest, R("nbtr"), R("nbt"))
        when(t, "swap")
        recv("C", t, guest, R("JOr"))
        acc([const(nj, 0), (nj, P("blkH"), R("JOr"))])
        tt(P("XS", 1, NB + 1), P("OG"), nj, A.min)
        cp(slot(2), IND(P("XS"), P("thl")), "va")
        lin(P("d0", 2, 3 * NB, 3), slot(2), -2.0, -6144.0)
        for j, (m, (a, b)) in enumerate(zip("Dde", DP)):
            when(t + 1, "names", j)
            recv(m, t, host, R("gotr", a, b))
            acc([const(P("p3", NB + a, NB + b), 0), (P("p3", NB + a, NB + b), P("blkH"), R("gotr", a, b))])
            tt(slot(1, a, b), P("OJ", a, b), P("p3", NB + a, NB + b), A.min)
            lin(P("d0", 1 + 3 * a, 3 * b, 3), slot(1, a, b), -2.0, -6144.0, "v")
            scan(P("dm", DM * (t + 1) + 3 * a, DM * (t + 1) + 3 * b), P("d0", 3 * a, 3 * b), P("dm", DM * t + 2 + 3 * a, DM * t + 2 + 3 * b),
                 0.0, A.min, A.max)
            lin(P("o", a, b), P("dm", DM * (t + 1) + 2 + 3 * a, DM * (t + 1) + 3 * b, 3), 1.0, 2048.0)
            if not fin:
                offsets(t + 1, "o", "p1", "q", "sh", "offH", a, b)
        if not fin:
            looks(t + 1, "x", "offH")
            when(t + 1, "j")
            mms([(Nc, P("idh"), P("dm", DM * (t + 1) + 2, DM * (t + 1) + 2 + 3 * NB, 3))])
        when(t + 1, "lists")
        recv("E", t, host, R("nbtr"))
        mms([to_list(dl(49, 84, 3), "nbtr", b0, P("g8s"), "p2", 384, "xm", 1.0, 3840.0)])
        lin(P("nm"), dl(49, 84, 3), 4.0, 192.0)
        tt(dl(25, 48, 2), P("nm"), TA(t), A.min)
        lin(P("l0"), dl(0, 84), -2.0, 0.0)
        scan(P("st", ST * t + ST, ST * t + ST + 84), P("l0"), dl(0, 84), 0.0, A.min, A.max)
        if not fin:
            send("P", t + 1, at(rank + away(t + 1)), P("ar", a0 + AM + 48, a0 + 2 * AM), P("st", ST * t + ST + 24, ST * t + ST + 48))
    dma("y", T.yo[:, :], T.o[:, :], "st0", [P("o")])
    turn = lambda pn, c0, c1, lst: mms([(P(pn, c0 + i, c1, 16, 8), P("CLT", 128 * i, 128 * i + 128, 16), lst) for i in range(16)])
    turn("p4", 0, NB, WW(RO))
    turn("p7", 0, 2 * NB, P("st", ST * RO + 1, ST * RO + 48, 2))
    turn("p2", 0, NB, TA(RO))
    for j, (out, pn, c0) in enumerate(((T.yu, "p4", 0), (T.yf, "p7", 0), (T.yp, "p7", NB), (T.yt, "p2", 0))):
        cp(P("o8", NB * j, NB * j + NB), P(pn, c0, c0 + NB, 1, 8), "va")
        dma("ya"[j % 2], out[:, :], T.o8[0:8, NB * j:NB * j + NB], "st%d" % (1 + j), [P("o8", NB * j, NB * j + NB)])

    count, known, clocks, hist = {}, {q: {} for q in queues}, {}, {}
    left = 0

    def need(q, reads, writes):
        want = {}
        for lst, wr in ((reads, False), (writes, True)):
            for r in lst:
                ps = r[1] in PS
                for (z, w, oq, point) in hist.get(r[1], ()):
                    if (meet(r, z) and (wr or w) and not (ps and q == "p" and oq == "p")) or (ps and oq != q):
                        want[point[0]] = max(want.get(point[0], 0), point[1])
        kn = known[q]
        for s in sorted(want, key=lambda z: -want[z]):
            if kn.get(s, 0) < want[s]:
                queues[q].wait_ge(T.sem[s], want[s])
                for s2, n2 in clocks.get((s, want[s]), {}).items():
                    kn[s2] = max(kn.get(s2, 0), n2)
                kn[s] = want[s]

    def note(q, reads, writes, point, clock):
        clocks[point] = clock
        for lst, wr in ((reads, False), (writes, True)):
            for r in lst:
                h = hist.setdefault(r[1], [])
                if r[1] in PS:
                    h[:] = [z for z in h if not (z[2] == q and z[1] == wr and cover(r, z[0]))]
                elif wr:
                    h[:] = [z for z in h if not cover(r, z[0])]
                h.append((r, wr, q, point))

    if not PLAN:
        PLAN.extend(order(ops))
    for _, i, q in PLAN:
        o = ops[i]
        rd, wr = [[r for r in lst if r[1] in SCRATCH] for lst in (o["reads"], o["writes"])]
        if o["kind"] == "recv":
            msg, t, src, buf = o["args"]
            note("r", rd, wr, ("m%s%d" % (msg, t), len(topo.engines(src, core)[:8])), {})
            continue
        need(q, rd, wr)
        if o["kind"] == "send":
            msg, t, dst, out, in_ = o["args"]
            rid, pid = topo.addr(dst, core)
            eng = topo.engines(core, dst)[:8]
            g.remote_dma(out[0], in_[0], T.sem["m%s%d" % (msg, t)], T.sem.left, pid, rid, sum(1 << e for e in eng))
            left += len(eng)
        elif o["kind"] == "dma":
            o["fns"][q][0]().then_inc(T.sem[o["sem"]], 16)
            note(q, rd, wr, (o["sem"], 16), dict(known[q]))
        else:
            for f in o["fns"][q]:
                f().then_inc(T.sem[q], 1)
            count[q] = count.get(q, 0) + len(o["fns"][q])
            note(q, rd, wr, (q, count[q]), dict(known[q]))
    for i in range(5):
        g.sync.wait_ge(T.sem["st%d" % i], 16)
    for i in range(9):
        if known["v"].get("ld%d" % i, 0) < 16:
            g.vector.wait_ge(T.sem["ld%d" % i], 16)
    for s in ("v", "a", "p", "k"):
        g.wait_ge(T.sem[s], count[s])
    g.wait_ge(T.sem.left, left)
